import numpy as np
import ml_dtypes


def mxq(x, axis, fmt="e4m3"):
    dtype, down = {"e4m3": (ml_dtypes.float8_e4m3fn, 7), "e5m2": (ml_dtypes.float8_e5m2, 14)}[fmt]
    v = np.moveaxis(np.asarray(x, np.float32).astype(ml_dtypes.bfloat16).astype(np.float64), axis, -1)
    blocks = v.reshape(v.shape[:-1] + (-1, 32))
    amax = np.abs(blocks).max(-1, keepdims=True)
    byte = np.maximum(np.where(amax > 0, np.frexp(amax)[1] - 1 + 127, 0) - down, 1)
    scale = np.exp2(byte - 127.0)
    codes = (blocks / scale).astype(np.float32).astype(dtype).astype(np.float64)
    return np.moveaxis((codes * scale).reshape(v.shape), -1, axis)


WIDE = False


def mx_kscale(k):
    if not WIDE:
        return np.ones(k)
    levels = np.array([10, -10, 5, -5, 0])
    if k % 512:
        return np.exp2(np.random.permutation(np.resize(levels, k // 32))).repeat(32)
    a = np.empty((k // 512, 16))
    for p in range(k // 512):
        a[p, :8] = np.random.permutation(np.resize(levels, 8))
        for g in range(8):
            far = levels[np.abs(levels - a[p, g]) >= 10]
            a[p, g + 8] = far[np.random.randint(len(far))]
    return np.exp2(a.ravel()).repeat(32)


def f64(x):
    return np.asarray(x).astype(np.float64)


def striped(idx):
    return np.tile(idx.reshape(-1, 16).T, (8, 1)).astype(np.uint16)


def unstriped(offs):
    return offs[:16].T.reshape(-1).astype(np.int64)


E2M1 = np.array([0.0, 0.5, 1.0, 1.5, 2.0, 3.0, 4.0, 6.0, -0.0, -0.5, -1.0, -1.5, -2.0, -3.0, -4.0, -6.0])


def pack_weight(w, fmt):
    k, n = w.shape
    w = f64(np.asarray(w, np.float32).astype(ml_dtypes.bfloat16)).reshape(k // 32, 32, n)
    amax = np.abs(w).max(1)
    if fmt == "e4m3":
        byte = np.frexp(amax)[1] - 1 + 127 - 7
    else:
        mant, ex = np.frexp(amax / 6.0)
        byte = np.where(mant > 0.5, ex, ex - 1) + 127
    byte = np.clip(np.where(amax > 0, byte, 1), 1, 254)
    scaled = (w * np.exp2(127.0 - byte)[:, None, :]).reshape(k, n).astype(np.float32)
    by_word = np.ascontiguousarray(scaled.reshape(k // 512, 128, 4, n).transpose(0, 1, 3, 2))
    if fmt == "e4m3":
        words = by_word.astype(ml_dtypes.float8_e4m3fn).view(np.uint8)
    else:
        c = by_word.astype(ml_dtypes.float4_e2m1fn).view(np.uint8) & 0xF
        words = (c[..., 0::2] | (c[..., 1::2] << 4)).reshape(k // 512, 128, 2 * n)
    return np.ascontiguousarray(words), np.ascontiguousarray(byte.astype(np.uint8).reshape(k // 512, 16, n))


def unpack_weight(words, scales, fmt):
    g, _, n = scales.shape
    words = np.ascontiguousarray(words).reshape(g, 128, n, -1)
    if fmt == "e4m3":
        vals = words.view(ml_dtypes.float8_e4m3fn).astype(np.float64)
    else:
        nib = np.empty((g, 128, n, 4), np.uint8)
        nib[..., 0::2] = words & 0xF
        nib[..., 1::2] = words >> 4
        vals = E2M1[nib]
    vals = vals * np.repeat(np.exp2(scales.astype(np.float64) - 127.0), 8, axis=1)[..., None]
    return vals.transpose(0, 1, 3, 2).reshape(g * 512, n)


def gelu(v):
    return 0.5 * v * (1.0 + np.tanh(np.sqrt(2.0 / np.pi) * (v + 0.044715 * v**3)))


K, H, N, T, S = 1536, 1024, 384, 4096, 1024

def setup_inputs():
    n = np.random.standard_normal
    s = mx_kscale(K)[:, None]
    u = mx_kscale(H)[:, None]
    tab_words, tab_scales = pack_weight(n((K, T)) * s, "e4m3")
    offs = striped(np.random.permutation(T)[:S])
    offs2 = striped(np.random.permutation(S))
    w1 = (1.5 * n((K, H)) / np.sqrt(K) / s).astype(np.float32)
    gain = (np.exp(0.3 * n(H)) * u[:, 0]).astype(np.float32)
    w2_words, w2_scales = pack_weight(1.2 * n((H, N)) / np.sqrt(H) / u, "e2m1")
    w3 = (1.2 * n((H, N)) / np.sqrt(H) / u).astype(np.float32)
    wgo = np.exp(0.3 * n((128, S))).astype(np.float32)
    x0 = n((N, S)).astype(np.float32)
    return {"tab_words": tab_words, "tab_scales": tab_scales, "offs": offs, "offs2": offs2,
            "w1": w1, "gain": gain, "w2_words": w2_words, "w2_scales": w2_scales,
            "w3": w3, "wgo": wgo, "x0": x0}

def reference(tab_words, tab_scales, offs, offs2, w1, gain, w2_words, w2_scales, w3, wgo, x0):
    v = unpack_weight(tab_words, tab_scales, "e4m3")[:, unstriped(offs)]
    b1 = mxq(f64(w1), 0, "e4m3").T @ v
    h = b1 / (1.0 + np.exp(-b1)) * f64(gain)[:, None]
    hq = mxq(h, 0, "e4m3")
    w2 = unpack_weight(w2_words, w2_scales, "e2m1")
    d = w2.T @ hq
    e = mxq(f64(w3), 0, "e4m3").T @ hq
    y = d * e
    page = np.zeros((N, S))
    page[:, unstriped(offs2)] = np.tile(f64(wgo), (N // 128, 1)) * y
    return f64(x0) + np.tanh(page)

@@ -1,0 +1,313 @@
+from contextlib import ExitStack
+
+import concourse.mybir as mybir
+
+K, H, N, T, S = 1536, 1024, 384, 4096, 1024
+FLOPS = 2 * K * H * S + 4 * H * N * S
+
+F32 = mybir.dt.float32
+BF16 = mybir.dt.bfloat16
+I32 = mybir.dt.int32
+U32 = mybir.dt.uint32
+U16 = mybir.dt.uint16
+U8 = mybir.dt.uint8
+FP8X4 = mybir.dt.float8_e4m3fn_x4
+FP4X4 = mybir.dt.float4_e2m1fn_x4
+ACT = mybir.ActivationFunctionType
+MULT = mybir.AluOpType.mult
+ADD = mybir.AluOpType.add
+
+P = 128
+PACK = 4
+KP = P * PACK
+KA = K // KP
+HB = H // KP
+NT = N // P
+UNIT = 128
+UNITS = S // UNIT
+GROUPS = [(0, 256), (256, 512), (512, 768), (768, 1024)]
+SCALAR_GAIN = [(0, 2), (1, 2), (0, 3), (1, 3)]
+CAST_SCALAR_M = {(0, 0): 128, (0, 1): 128, (0, 2): 44, (1, 0): 0, (1, 1): 0, (1, 2): 44}
+HELD = [(1, 1), (1, 2), (1, 3)]
+EARLY = 1
+POOL_CHUNKS = []
+POOL_ADDS = []
+W3_ON_SCALAR = [1, 2]
+
+
+def tile_list_junction_desk_kernel(tc, tab_words, tab_scales, offs, offs2, w1, gain, w2_words, w2_scales, w3, wgo, x0, out):
+    nc = tc.nc
+    with ExitStack() as ctx:
+        keep = ctx.enter_context(tc.tile_pool(name="keep", bufs=1))
+        ring = ctx.enter_context(tc.tile_pool(name="ring", bufs=1))
+        psum = ctx.enter_context(tc.psum_pool(name="psum", bufs=8))
+
+        idx = keep.tile([P, S // 16], U16, name="idx")
+        idx2 = keep.tile([P, S // 16], U16, name="idx2")
+        tab = [keep.tile([P, T], I32, name=f"tab{a}", align_bytes=64) for a in range(KA)]
+        tab_sc = keep.tile([P, T], U8, name="tab_sc", align_bytes=64)
+        v_codes = [keep.tile([P, S], U32, name=f"v_codes{a}", align_bytes=64) for a in range(KA)]
+        v_sc = keep.tile([P, S], U8, name="v_sc", align_bytes=64)
+        gain_sb = keep.tile([P, HB, PACK], F32, name="gain_sb")
+        w2_codes = keep.tile([P, HB, 2 * N], U8, name="w2_codes", align_bytes=64)
+        w2_sc = keep.tile([P, HB, N], U8, name="w2_sc", align_bytes=64)
+        warm = keep.tile([P, 8], F32, name="warm")
+        warm_out = keep.tile([P, 8], F32, name="warm_out")
+
+        nc.vector.memset(tab_sc[:].bitcast(I32), 0)
+        nc.vector.memset(w2_sc[:].rearrange("p b n -> p (b n)").bitcast(I32), 0)
+        nc.vector.memset(warm[:], 0.0)
+        nc.scalar.activation(warm_out[:], warm[:], ACT.Silu)
+        for q in range(4):
+            nc.gpsimd.dma_start(
+                out=w2_sc[32 * q : 32 * q + 4, :, :].bitcast(I32),
+                in_=w2_scales[:, 4 * q : 4 * q + 4, :].rearrange("b r n -> r b n").bitcast(I32),
+            )
+
+        w1_raw = {}
+
+        def load_tab(a):
+            nc.sync.dma_start(out=tab[a][:], in_=tab_words[a].rearrange("p t i -> p (t i)").bitcast(I32))
+
+        def load_w1(b, a, pieces=1):
+            raw = ring.tile([P, PACK, KP], F32, name="w1_raw", tag="stage", bufs=6)
+            rows = w1[KP * a : KP * (a + 1), KP * b : KP * (b + 1)].rearrange("(p j) r -> p j r", j=PACK)
+            for j in range(0, PACK, PACK // pieces):
+                nc.sync.dma_start(out=raw[:, j : j + PACK // pieces, :], in_=rows[:, j : j + PACK // pieces, :])
+            w1_raw[(b, a)] = raw
+
+        w1_codes, w1_sc = {}, {}
+
+        def quantize_w1(b, a):
+            raw = w1_raw[(b, a)]
+            grouped = ring.tile([P, KP * PACK], BF16, name="w1_grouped", bufs=3, align_bytes=64)
+            dst = grouped[:].rearrange("p (t m j) -> p m j t", t=PACK, j=PACK)
+            src = raw[:].rearrange("p j (m t) -> p m j t", t=PACK)
+            ms = CAST_SCALAR_M[(b, a)]
+            if ms > 0:
+                nc.scalar.copy(dst[:, :ms], src[:, :ms])
+            if ms < P:
+                nc.vector.tensor_copy(dst[:, ms:], src[:, ms:])
+            codes = keep.tile([P, KP], U32, name=f"w1_codes{b}{a}", align_bytes=64)
+            sc = keep.tile([P, KP], U8, name=f"w1_sc{b}{a}", align_bytes=64)
+            nc.vector.quantize_mx(out=codes[:].bitcast(FP8X4), scales=sc[:], in_=grouped[:])
+            w1_codes[(b, a)], w1_sc[(b, a)] = codes, sc
+
+        def gather_words(a):
+            nc.vector.tensor_copy(v_codes[a][:], tab[a][:].bitcast(U32).indirect(idx[:]))
+
+        banks = {}
+
+        def first_product(b, a, u):
+            if a == 0:
+                banks[(b, u)] = psum.tile([P, PACK, UNIT], F32, name="bank")
+            cols = slice(UNIT * u, UNIT * (u + 1))
+            for t in range(PACK):
+                m = slice(P * t, P * (t + 1))
+                nc.tensor.matmul_mx(
+                    out=banks[(b, u)][:, t, :],
+                    lhsT=w1_codes[(b, a)][:, m].bitcast(FP8X4),
+                    lhsT_scale=w1_sc[(b, a)][:, m],
+                    rhs=v_codes[a][:, cols].bitcast(FP8X4),
+                    rhs_scale=v_sc[4 * a :, cols],
+                    start=(a == 0 and t == 0),
+                    stop=(a == KA - 1 and t == PACK - 1),
+                )
+
+        h_codes = [keep.tile([P, S], U32, name=f"h_codes{b}", align_bytes=64) for b in range(HB)]
+        h_sc = [keep.tile([P, S], U8, name=f"h_sc{b}", align_bytes=64) for b in range(HB)]
+
+        acts = {}
+
+        def silu(b, g):
+            lo, hi = GROUPS[g]
+            w = hi - lo
+            on_scalar = (b, g) in SCALAR_GAIN
+            act = ring.tile([P, PACK, w] if on_scalar else [P, w, PACK], F32, name="act", bufs=5, align_bytes=64)
+            for u in range(lo // UNIT, hi // UNIT):
+                for a in range(KA - 1 - b, KA):
+                    first_product(b, a, u)
+                cols = slice(UNIT * u - lo, UNIT * (u + 1) - lo)
+                if on_scalar:
+                    nc.scalar.activation(act[:, :, cols], banks[(b, u)][:], ACT.Silu)
+                else:
+                    nc.scalar.activation(act[:, cols, :], banks[(b, u)][:].rearrange("p t n -> p n t"), ACT.Silu)
+            acts[(b, g)] = act
+
+        def hidden(b, g):
+            lo, hi = GROUPS[g]
+            w = hi - lo
+            act = acts[(b, g)]
+            if (b, g) in HELD:
+                h_bf = ring.tile([P, w, PACK], BF16, name="h_bf", tag=f"held{g}", bufs=1, align_bytes=64)
+            else:
+                h_bf = ring.tile([P, w, PACK], BF16, name="h_bf", bufs=3, align_bytes=64)
+            if (b, g) in SCALAR_GAIN:
+                planes = ring.tile([P, PACK, w], BF16, name="planes", bufs=2, align_bytes=64)
+                for t in range(PACK):
+                    nc.scalar.activation(planes[:, t, :], act[:, t, :], ACT.Copy, scale=gain_sb[:, b, t : t + 1])
+                nc.scalar.copy(
+                    h_bf[:].rearrange("p (c i) t -> p c t i", i=4),
+                    planes[:].rearrange("p t (c i) -> p c t i", i=4),
+                )
+            else:
+                nc.vector.tensor_tensor(h_bf[:], act[:], gain_sb[:, b : b + 1, :].to_broadcast([P, w, PACK]), MULT)
+            nc.vector.quantize_mx(
+                out=h_codes[b][:, lo:hi].bitcast(FP8X4),
+                scales=h_sc[b][:, lo:hi],
+                in_=h_bf[:].rearrange("p n t -> p (n t)"),
+            )
+
+        load_tab(0)
+        for q in range(4):
+            nc.sync.dma_start(out=tab_sc[32 * q : 32 * q + 4 * KA, :].bitcast(I32), in_=tab_scales[:, 4 * q : 4 * q + 4, :].bitcast(I32))
+        nc.sync.dma_start(idx[:], offs)
+        load_w1(0, 0)
+        load_tab(1)
+        nc.sync.dma_start(idx2[:], offs2)
+        nc.sync.dma_start(out=gain_sb[:], in_=gain.rearrange("(b p t) -> p b t", b=HB, t=PACK))
+        for b in range(HB):
+            nc.sync.dma_start(out=w2_codes[:, b, :].bitcast(I32), in_=w2_words[b].bitcast(I32))
+        load_w1(0, 1)
+        load_tab(2)
+        load_w1(0, 2)
+        load_w1(1, 0)
+
+        nc.vector.tensor_copy(v_sc[:], tab_sc[:].indirect(idx[:]))
+        for a in range(KA):
+            gather_words(a)
+            quantize_w1(0, a)
+            if a < 2:
+                load_w1(1, a + 1)
+                for u in range(UNITS):
+                    first_product(0, a, u)
+
+        w3_raw = []
+        for b in range(HB):
+            raw3 = ring.tile([P, PACK, N], F32, name="w3_raw", tag="stage", bufs=6)
+            nc.sync.dma_start(out=raw3[:], in_=w3[KP * b : KP * (b + 1), :].rearrange("(p j) n -> p j n", j=PACK))
+            w3_raw.append(raw3)
+        wgo_sb = keep.tile([P, S], F32, name="wgo_sb")
+        nc.sync.dma_start(out=wgo_sb[:], in_=wgo)
+        x0_sb = []
+        for n in range(NT):
+            x0_n = ring.tile([P, S], F32, name="x0_n", tag="stage", bufs=6)
+            nc.sync.dma_start(out=x0_n[:], in_=x0[P * n : P * (n + 1), :])
+            x0_sb.append(x0_n)
+
+        for a in range(KA):
+            quantize_w1(1, a)
+        for g in range(len(GROUPS)):
+            silu(0, g)
+            if g < EARLY:
+                hidden(0, g)
+            lo, hi = GROUPS[g]
+            for u in range(lo // UNIT, hi // UNIT):
+                first_product(1, 0, u)
+
+        w3_codes, w3_sc = {}, {}
+
+        def quantize_w3(n):
+            grouped3 = keep.tile([P, HB, P, PACK], BF16, name=f"w3_grouped{n}", align_bytes=64)
+            for b in range(HB):
+                dst = grouped3[:, b].rearrange("p (c i) j -> p c j i", i=4)
+                src = w3_raw[b][:, :, P * n : P * (n + 1)].rearrange("p j (c i) -> p c j i", i=4)
+                if n in W3_ON_SCALAR:
+                    nc.scalar.copy(dst, src)
+                else:
+                    nc.vector.tensor_copy(dst, src)
+            codes = keep.tile([P, HB * P], U32, name=f"w3_codes{n}", align_bytes=64)
+            sc = keep.tile([P, HB * P], U8, name=f"w3_sc{n}", align_bytes=64)
+            nc.vector.quantize_mx(out=codes[:].bitcast(FP8X4), scales=sc[:], in_=grouped3[:].rearrange("p b c j -> p (b c j)"))
+            w3_codes[n], w3_sc[n] = codes, sc
+
+        pages = [keep.tile([P, S], F32, name=f"page{n}") for n in range(NT)]
+
+        def product_d(dst, g, n):
+            lo, hi = GROUPS[g]
+            for c in range(0, hi - lo, UNIT):
+                for b in range(HB):
+                    nc.tensor.matmul_mx(
+                        out=dst[:, c : c + UNIT],
+                        lhsT=w2_codes[:, b, 2 * P * n : 2 * P * (n + 1)].bitcast(FP4X4),
+                        lhsT_scale=w2_sc[:, b, P * n : P * (n + 1)],
+                        rhs=h_codes[b][:, lo + c : lo + c + UNIT].bitcast(FP8X4),
+                        rhs_scale=h_sc[b][:, lo + c : lo + c + UNIT],
+                        start=(b == 0),
+                        stop=(b == HB - 1),
+                    )
+
+        def product_e(dst, g, n):
+            lo, hi = GROUPS[g]
+            for b in range(HB):
+                nc.tensor.matmul_mx(
+                    out=dst,
+                    lhsT=w3_codes[n][:, P * b : P * (b + 1)].bitcast(FP8X4),
+                    lhsT_scale=w3_sc[n][:, P * b : P * (b + 1)],
+                    rhs=h_codes[b][:, lo:hi].bitcast(FP8X4),
+                    rhs_scale=h_sc[b][:, lo:hi],
+                    start=(b == 0),
+                    stop=(b == HB - 1),
+                )
+
+        def scores(g, ns):
+            lo, hi = GROUPS[g]
+            w = hi - lo
+            k = len(ns)
+            if 2 * k * w <= KP:
+                both = psum.tile([P, 2, k, w], F32, name="bank")
+                d_ps, e_ps = both[:, 0], both[:, 1]
+            else:
+                d_tile = psum.tile([P, k, w], F32, name="bank")
+                e_tile = psum.tile([P, k, w], F32, name="bank")
+                d_ps, e_ps = d_tile[:], e_tile[:]
+            for i, n in enumerate(ns):
+                product_d(d_ps[:, i, :], g, n)
+            for i, n in enumerate(ns):
+                product_e(e_ps[:, i, :], g, n)
+            if (1, g + 1) in HELD and ns[-1] == NT - 1:
+                y = ring.tile([P, k, w], F32, name="y", tag=f"held{g + 1}", bufs=1, align_bytes=64)
+            else:
+                y = ring.tile([P, k, w], F32, name="y", bufs=3, align_bytes=64)
+            places = idx2[:, lo // 16 : hi // 16]
+            if g in POOL_CHUNKS:
+                de = ring.tile([P, 2, k, w], F32, name="de", bufs=4)
+                nc.scalar.copy(de[:], both[:])
+                yy = ring.tile([P, k, w], F32, name="yy", bufs=2)
+                nc.gpsimd.tensor_tensor(yy[:], de[:, 0], de[:, 1], MULT)
+                nc.gpsimd.tensor_tensor(y[:, 0, :], yy[:, 0, :], wgo_sb[:, lo:hi], MULT)
+                nc.vector.tensor_copy(pages[ns[0]][:].indirect(places), y[:, 0, :])
+                return
+            d_sb = ring.tile([P, k, w], F32, name="d_sb", bufs=4)
+            nc.scalar.copy(d_sb[:], d_ps)
+            nc.vector.tensor_tensor(y[:], e_ps, d_sb[:], MULT)
+            for i, n in enumerate(ns):
+                nc.vector.tensor_tensor(pages[n][:].indirect(places), y[:, i, :], wgo_sb[:, lo:hi], MULT)
+
+        def finish(n):
+            for lo in range(0, S, KP):
+                th = ring.tile([P, KP], F32, name="th", bufs=4)
+                nc.scalar.activation(th[:], pages[n][:, lo : lo + KP], ACT.Tanh)
+                adder = nc.gpsimd if n in POOL_ADDS else nc.vector
+                adder.tensor_tensor(x0_sb[n][:, lo : lo + KP], x0_sb[n][:, lo : lo + KP], th[:], ADD)
+                nc.sync.dma_start(out=out[P * n : P * (n + 1), lo : lo + KP], in_=x0_sb[n][:, lo : lo + KP])
+
+        last = len(GROUPS) - 1
+        silu(1, 0)
+        hidden(1, 0)
+        quantize_w3(0)
+        scores(0, [0])
+        quantize_w3(1)
+        quantize_w3(2)
+        for g in range(1, len(GROUPS)):
+            silu(1, g)
+        for g in range(len(GROUPS)):
+            if g > 0:
+                scores(g, [0])
+            if g < last:
+                if g + 1 >= EARLY:
+                    hidden(0, g + 1)
+                hidden(1, g + 1)
+            scores(g, [1, 2])
+        for n in range(NT):
+            finish(n)

@@ -27,7 +27,7 @@ UNIT = 128
 UNITS = S // UNIT
 GROUPS = [(0, 256), (256, 512), (512, 768), (768, 1024)]
 SCALAR_GAIN = [(0, 2), (1, 2), (0, 3), (1, 3)]
-CAST_SCALAR_M = {(0, 0): 128, (0, 1): 128, (0, 2): 44, (1, 0): 0, (1, 1): 0, (1, 2): 44}
+CAST_SCALAR_M = {(0, 0): 128, (0, 1): 128, (0, 2): 44, (1, 0): 16, (1, 1): 16, (1, 2): 44}
 HELD = [(1, 1), (1, 2), (1, 3)]
 EARLY = 1
 POOL_CHUNKS = []
@@ -59,6 +59,8 @@ def tile_list_junction_desk_kernel(tc, tab_words, tab_scales, offs, offs2, w1, g
         nc.vector.memset(warm[:], 0.0)
         nc.scalar.activation(warm_out[:], warm[:], ACT.Silu)
         for q in range(4):
+            nc.gpsimd.dma_start(out=tab_sc[32 * q : 32 * q + 4 * KA, :].bitcast(I32), in_=tab_scales[:, 4 * q : 4 * q + 4, :].bitcast(I32))
+        for q in range(4):
             nc.gpsimd.dma_start(
                 out=w2_sc[32 * q : 32 * q + 4, :, :].bitcast(I32),
                 in_=w2_scales[:, 4 * q : 4 * q + 4, :].rearrange("b r n -> r b n").bitcast(I32),
@@ -69,12 +71,16 @@ def tile_list_junction_desk_kernel(tc, tab_words, tab_scales, offs, offs2, w1, g
         def load_tab(a):
             nc.sync.dma_start(out=tab[a][:], in_=tab_words[a].rearrange("p t i -> p (t i)").bitcast(I32))
 
-        def load_w1(b, a, pieces=1):
+        def load_w1_rows(a):
+            raw = ring.tile([P, PACK, H], F32, name="w1_rows", tag="wide", bufs=1)
+            nc.sync.dma_start(out=raw[:], in_=w1[KP * a : KP * (a + 1), :].rearrange("(p j) r -> p j r", j=PACK))
+            for b in range(HB):
+                w1_raw[(b, a)] = raw[:, :, KP * b : KP * (b + 1)]
+
+        def load_w1(b, a):
             raw = ring.tile([P, PACK, KP], F32, name="w1_raw", tag="stage", bufs=6)
-            rows = w1[KP * a : KP * (a + 1), KP * b : KP * (b + 1)].rearrange("(p j) r -> p j r", j=PACK)
-            for j in range(0, PACK, PACK // pieces):
-                nc.sync.dma_start(out=raw[:, j : j + PACK // pieces, :], in_=rows[:, j : j + PACK // pieces, :])
-            w1_raw[(b, a)] = raw
+            nc.sync.dma_start(out=raw[:], in_=w1[KP * a : KP * (a + 1), KP * b : KP * (b + 1)].rearrange("(p j) r -> p j r", j=PACK))
+            w1_raw[(b, a)] = raw[:]
 
         w1_codes, w1_sc = {}, {}
 
@@ -82,7 +88,7 @@ def tile_list_junction_desk_kernel(tc, tab_words, tab_scales, offs, offs2, w1, g
             raw = w1_raw[(b, a)]
             grouped = ring.tile([P, KP * PACK], BF16, name="w1_grouped", bufs=3, align_bytes=64)
             dst = grouped[:].rearrange("p (t m j) -> p m j t", t=PACK, j=PACK)
-            src = raw[:].rearrange("p j (m t) -> p m j t", t=PACK)
+            src = raw.rearrange("p j (m t) -> p m j t", t=PACK)
             ms = CAST_SCALAR_M[(b, a)]
             if ms > 0:
                 nc.scalar.copy(dst[:, :ms], src[:, :ms])
@@ -97,10 +103,12 @@ def tile_list_junction_desk_kernel(tc, tab_words, tab_scales, offs, offs2, w1, g
             nc.vector.tensor_copy(v_codes[a][:], tab[a][:].bitcast(U32).indirect(idx[:]))
 
         banks = {}
+        begun = {}
 
         def first_product(b, a, u):
             if a == 0:
                 banks[(b, u)] = psum.tile([P, PACK, UNIT], F32, name="bank")
+            begun[(b, u)] = a + 1
             cols = slice(UNIT * u, UNIT * (u + 1))
             for t in range(PACK):
                 m = slice(P * t, P * (t + 1))
@@ -125,7 +133,7 @@ def tile_list_junction_desk_kernel(tc, tab_words, tab_scales, offs, offs2, w1, g
             on_scalar = (b, g) in SCALAR_GAIN
             act = ring.tile([P, PACK, w] if on_scalar else [P, w, PACK], F32, name="act", bufs=5, align_bytes=64)
             for u in range(lo // UNIT, hi // UNIT):
-                for a in range(KA - 1 - b, KA):
+                for a in range(begun.get((b, u), 0), KA):
                     first_product(b, a, u)
                 cols = slice(UNIT * u - lo, UNIT * (u + 1) - lo)
                 if on_scalar:
@@ -159,34 +167,30 @@ def tile_list_junction_desk_kernel(tc, tab_words, tab_scales, offs, offs2, w1, g
             )
 
         load_tab(0)
-        for q in range(4):
-            nc.sync.dma_start(out=tab_sc[32 * q : 32 * q + 4 * KA, :].bitcast(I32), in_=tab_scales[:, 4 * q : 4 * q + 4, :].bitcast(I32))
         nc.sync.dma_start(idx[:], offs)
         load_w1(0, 0)
-        load_tab(1)
-        nc.sync.dma_start(idx2[:], offs2)
         nc.sync.dma_start(out=gain_sb[:], in_=gain.rearrange("(b p t) -> p b t", b=HB, t=PACK))
-        for b in range(HB):
-            nc.sync.dma_start(out=w2_codes[:, b, :].bitcast(I32), in_=w2_words[b].bitcast(I32))
+        load_tab(1)
         load_w1(0, 1)
         load_tab(2)
         load_w1(0, 2)
-        load_w1(1, 0)
+        for a in range(KA):
+            load_w1(1, a)
 
         nc.vector.tensor_copy(v_sc[:], tab_sc[:].indirect(idx[:]))
         for a in range(KA):
             gather_words(a)
             quantize_w1(0, a)
-            if a < 2:
-                load_w1(1, a + 1)
+            if a < KA - 1:
                 for u in range(UNITS):
                     first_product(0, a, u)
-
+        nc.sync.dma_start(out=w2_codes[:].bitcast(I32), in_=w2_words.rearrange("b p c -> p b c").bitcast(I32))
         w3_raw = []
         for b in range(HB):
             raw3 = ring.tile([P, PACK, N], F32, name="w3_raw", tag="stage", bufs=6)
             nc.sync.dma_start(out=raw3[:], in_=w3[KP * b : KP * (b + 1), :].rearrange("(p j) n -> p j n", j=PACK))
             w3_raw.append(raw3)
+        nc.sync.dma_start(idx2[:], offs2)
         wgo_sb = keep.tile([P, S], F32, name="wgo_sb")
         nc.sync.dma_start(out=wgo_sb[:], in_=wgo)
         x0_sb = []

@@ -28,7 +28,7 @@ UNITS = S // UNIT
 GROUPS = [(0, 256), (256, 512), (512, 768), (768, 1024)]
 SCALAR_GAIN = [(0, 2), (1, 2), (0, 3), (1, 3)]
 CAST_SCALAR_M = {(0, 0): 128, (0, 1): 128, (0, 2): 44, (1, 0): 16, (1, 1): 16, (1, 2): 44}
-HELD = [(1, 1), (1, 2), (1, 3)]
+HELD = [(1, 1), (0, 2), (0, 3)]
 EARLY = 1
 POOL_CHUNKS = []
 POOL_ADDS = []
@@ -93,7 +93,7 @@ def tile_list_junction_desk_kernel(tc, tab_words, tab_scales, offs, offs2, w1, g
             if ms > 0:
                 nc.scalar.copy(dst[:, :ms], src[:, :ms])
             if ms < P:
-                nc.vector.tensor_copy(dst[:, ms:], src[:, ms:])
+                nc.vector.tensor_copy(dst[:, ms:].rearrange("p m j t -> p m t j"), src[:, ms:].rearrange("p m j t -> p m t j"))
             codes = keep.tile([P, KP], U32, name=f"w1_codes{b}{a}", align_bytes=64)
             sc = keep.tile([P, KP], U8, name=f"w1_sc{b}{a}", align_bytes=64)
             nc.vector.quantize_mx(out=codes[:].bitcast(FP8X4), scales=sc[:], in_=grouped[:])
@@ -142,29 +142,42 @@ def tile_list_junction_desk_kernel(tc, tab_words, tab_scales, offs, offs2, w1, g
                     nc.scalar.activation(act[:, cols, :], banks[(b, u)][:].rearrange("p t n -> p n t"), ACT.Silu)
             acts[(b, g)] = act
 
-        def hidden(b, g):
+        def quantize_h(b, g, h_bf):
             lo, hi = GROUPS[g]
-            w = hi - lo
-            act = acts[(b, g)]
-            if (b, g) in HELD:
-                h_bf = ring.tile([P, w, PACK], BF16, name="h_bf", tag=f"held{g}", bufs=1, align_bytes=64)
-            else:
-                h_bf = ring.tile([P, w, PACK], BF16, name="h_bf", bufs=3, align_bytes=64)
-            if (b, g) in SCALAR_GAIN:
-                planes = ring.tile([P, PACK, w], BF16, name="planes", bufs=2, align_bytes=64)
-                for t in range(PACK):
-                    nc.scalar.activation(planes[:, t, :], act[:, t, :], ACT.Copy, scale=gain_sb[:, b, t : t + 1])
-                nc.scalar.copy(
-                    h_bf[:].rearrange("p (c i) t -> p c t i", i=4),
-                    planes[:].rearrange("p t (c i) -> p c t i", i=4),
-                )
-            else:
-                nc.vector.tensor_tensor(h_bf[:], act[:], gain_sb[:, b : b + 1, :].to_broadcast([P, w, PACK]), MULT)
             nc.vector.quantize_mx(
                 out=h_codes[b][:, lo:hi].bitcast(FP8X4),
                 scales=h_sc[b][:, lo:hi],
-                in_=h_bf[:].rearrange("p n t -> p (n t)"),
+                in_=h_bf.rearrange("p n t -> p (n t)"),
             )
+
+        def h_tile(b, g):
+            lo, hi = GROUPS[g]
+            if (b, g) in HELD:
+                return ring.tile([P, hi - lo, PACK], BF16, name="h_held", tag=f"held{g}", bufs=1, align_bytes=64)
+            return ring.tile([P, hi - lo, PACK], BF16, name="h_bf", bufs=3, align_bytes=64)
+
+        def hidden(b, g):
+            lo, hi = GROUPS[g]
+            h_bf = h_tile(b, g)
+            nc.vector.tensor_tensor(h_bf[:], acts[(b, g)][:], gain_sb[:, b : b + 1, :].to_broadcast([P, hi - lo, PACK]), MULT)
+            quantize_h(b, g, h_bf[:])
+
+        def hidden_on_scalar(g):
+            lo, hi = GROUPS[g]
+            planes = ring.tile([P, HB, PACK, hi - lo], BF16, name="planes", bufs=1, align_bytes=64)
+            for b in range(HB):
+                for t in range(PACK):
+                    nc.scalar.activation(planes[:, b, t, :], acts[(b, g)][:, t, :], ACT.Copy, scale=gain_sb[:, b, t : t + 1])
+            tiles = [h_tile(b, g) for b in range(HB)]
+            half = (hi - lo) // 2
+            for c in (0, half):
+                for b in range(HB):
+                    nc.scalar.copy(
+                        tiles[b][:, c : c + half, :].rearrange("p (c i) t -> p c t i", i=4),
+                        planes[:, b, :, c : c + half].rearrange("p t (c i) -> p c t i", i=4),
+                    )
+            for b in range(HB):
+                quantize_h(b, g, tiles[b][:])
 
         load_tab(0)
         nc.sync.dma_start(idx[:], offs)
@@ -269,7 +282,7 @@ def tile_list_junction_desk_kernel(tc, tab_words, tab_scales, offs, offs2, w1, g
                 product_d(d_ps[:, i, :], g, n)
             for i, n in enumerate(ns):
                 product_e(e_ps[:, i, :], g, n)
-            if (1, g + 1) in HELD and ns[-1] == NT - 1:
+            if ((0, g + 1) in HELD or (1, g + 1) in HELD) and ns[-1] == NT - 1:
                 y = ring.tile([P, k, w], F32, name="y", tag=f"held{g + 1}", bufs=1, align_bytes=64)
             else:
                 y = ring.tile([P, k, w], F32, name="y", bufs=3, align_bytes=64)
@@ -284,7 +297,8 @@ def tile_list_junction_desk_kernel(tc, tab_words, tab_scales, offs, offs2, w1, g
                 return
             d_sb = ring.tile([P, k, w], F32, name="d_sb", bufs=4)
             nc.scalar.copy(d_sb[:], d_ps)
-            nc.vector.tensor_tensor(y[:], e_ps, d_sb[:], MULT)
+            for i in range(k):
+                nc.vector.tensor_tensor(y[:, i, :], e_ps[:, i, :], d_sb[:, i, :], MULT)
             for i, n in enumerate(ns):
                 nc.vector.tensor_tensor(pages[n][:].indirect(places), y[:, i, :], wgo_sb[:, lo:hi], MULT)
 
@@ -309,9 +323,11 @@ def tile_list_junction_desk_kernel(tc, tab_words, tab_scales, offs, offs2, w1, g
             if g > 0:
                 scores(g, [0])
             if g < last:
-                if g + 1 >= EARLY:
+                if (0, g + 1) in SCALAR_GAIN:
+                    hidden_on_scalar(g + 1)
+                else:
                     hidden(0, g + 1)
-                hidden(1, g + 1)
+                    hidden(1, g + 1)
             scores(g, [1, 2])
         for n in range(NT):
             finish(n)

@@ -19,96 +19,85 @@ ADD = mybir.AluOpType.add
 
 P = 128
 PACK = 4
-KP = P * PACK
-KA = K // KP
-HB = H // KP
-NT = N // P
+PASS = P * PACK
+BANK = 512
+QUADS = 4
+LIST_ROWS = 16
+K_PASSES = K // PASS
+R_PASSES = H // PASS
+N_TILES = N // P
 UNIT = 128
-UNITS = S // UNIT
-GROUPS = [(0, 256), (256, 512), (512, 768), (768, 1024)]
-SCALAR_GAIN = [(0, 2), (1, 2), (0, 3), (1, 3)]
-CAST_SCALAR_M = {(0, 0): 128, (0, 1): 128, (0, 2): 44, (1, 0): 16, (1, 1): 16, (1, 2): 44}
-HELD = [(1, 1), (0, 2), (0, 3)]
-EARLY = 1
-POOL_CHUNKS = []
-POOL_ADDS = []
-W3_ON_SCALAR = [1, 2]
+CHUNK = 256
+CHUNKS = S // CHUNK
+VECTOR_GAIN_CHUNKS = 2
+SCALAR_CAST = {(0, 0): P, (0, 1): P, (0, 2): 44, (1, 0): 0, (1, 1): 16, (1, 2): 44}
+STAGE_SLOTS = 6
 
 
-def tile_list_junction_desk_kernel(tc, tab_words, tab_scales, offs, offs2, w1, gain, w2_words, w2_scales, w3, wgo, x0, out):
+def tile_list_junction_desk_kernel(
+    tc, tab_words, tab_scales, offs, offs2, w1, gain, w2_words, w2_scales, w3, wgo, x0, out
+):
     nc = tc.nc
     with ExitStack() as ctx:
         keep = ctx.enter_context(tc.tile_pool(name="keep", bufs=1))
         ring = ctx.enter_context(tc.tile_pool(name="ring", bufs=1))
         psum = ctx.enter_context(tc.psum_pool(name="psum", bufs=8))
 
-        idx = keep.tile([P, S // 16], U16, name="idx")
-        idx2 = keep.tile([P, S // 16], U16, name="idx2")
-        tab = [keep.tile([P, T], I32, name=f"tab{a}", align_bytes=64) for a in range(KA)]
+        idx = keep.tile([P, S // LIST_ROWS], U16, name="idx")
+        idx2 = keep.tile([P, S // LIST_ROWS], U16, name="idx2")
+        tab = [keep.tile([P, T], I32, name=f"tab{a}", align_bytes=64) for a in range(K_PASSES)]
         tab_sc = keep.tile([P, T], U8, name="tab_sc", align_bytes=64)
-        v_codes = [keep.tile([P, S], U32, name=f"v_codes{a}", align_bytes=64) for a in range(KA)]
+        v_codes = [keep.tile([P, S], U32, name=f"v_codes{a}", align_bytes=64) for a in range(K_PASSES)]
         v_sc = keep.tile([P, S], U8, name="v_sc", align_bytes=64)
-        gain_sb = keep.tile([P, HB, PACK], F32, name="gain_sb")
-        w2_codes = keep.tile([P, HB, 2 * N], U8, name="w2_codes", align_bytes=64)
-        w2_sc = keep.tile([P, HB, N], U8, name="w2_sc", align_bytes=64)
-        warm = keep.tile([P, 8], F32, name="warm")
-        warm_out = keep.tile([P, 8], F32, name="warm_out")
+        gain_sb = keep.tile([P, R_PASSES, PACK], F32, name="gain_sb")
+        w2_codes = keep.tile([P, R_PASSES, 2 * N], U8, name="w2_codes", align_bytes=64)
+        w2_sc = keep.tile([P, R_PASSES, N], U8, name="w2_sc", align_bytes=64)
 
         nc.vector.memset(tab_sc[:].bitcast(I32), 0)
         nc.vector.memset(w2_sc[:].rearrange("p b n -> p (b n)").bitcast(I32), 0)
-        nc.vector.memset(warm[:], 0.0)
-        nc.scalar.activation(warm_out[:], warm[:], ACT.Silu)
-        for q in range(4):
-            nc.gpsimd.dma_start(out=tab_sc[32 * q : 32 * q + 4 * KA, :].bitcast(I32), in_=tab_scales[:, 4 * q : 4 * q + 4, :].bitcast(I32))
-        for q in range(4):
+        for q in range(QUADS):
+            nc.gpsimd.dma_start(
+                out=tab_sc[32 * q : 32 * q + 4 * K_PASSES, :].bitcast(I32),
+                in_=tab_scales[:, 4 * q : 4 * q + 4, :].bitcast(I32),
+            )
+        for q in range(QUADS):
             nc.gpsimd.dma_start(
                 out=w2_sc[32 * q : 32 * q + 4, :, :].bitcast(I32),
                 in_=w2_scales[:, 4 * q : 4 * q + 4, :].rearrange("b r n -> r b n").bitcast(I32),
             )
 
-        w1_raw = {}
+        w1_raw, w1_codes, w1_sc = {}, {}, {}
 
         def load_tab(a):
             nc.sync.dma_start(out=tab[a][:], in_=tab_words[a].rearrange("p t i -> p (t i)").bitcast(I32))
 
-        def load_w1_rows(a):
-            raw = ring.tile([P, PACK, H], F32, name="w1_rows", tag="wide", bufs=1)
-            nc.sync.dma_start(out=raw[:], in_=w1[KP * a : KP * (a + 1), :].rearrange("(p j) r -> p j r", j=PACK))
-            for b in range(HB):
-                w1_raw[(b, a)] = raw[:, :, KP * b : KP * (b + 1)]
-
         def load_w1(b, a):
-            raw = ring.tile([P, PACK, KP], F32, name="w1_raw", tag="stage", bufs=6)
-            nc.sync.dma_start(out=raw[:], in_=w1[KP * a : KP * (a + 1), KP * b : KP * (b + 1)].rearrange("(p j) r -> p j r", j=PACK))
-            w1_raw[(b, a)] = raw[:]
-
-        w1_codes, w1_sc = {}, {}
+            raw = ring.tile([P, PACK, PASS], F32, name="w1_raw", tag="stage", bufs=STAGE_SLOTS)
+            rows = w1[PASS * a : PASS * (a + 1), PASS * b : PASS * (b + 1)]
+            nc.sync.dma_start(out=raw[:], in_=rows.rearrange("(p j) r -> p j r", j=PACK))
+            w1_raw[(b, a)] = raw
 
         def quantize_w1(b, a):
-            raw = w1_raw[(b, a)]
-            grouped = ring.tile([P, KP * PACK], BF16, name="w1_grouped", bufs=3, align_bytes=64)
+            grouped = ring.tile([P, PASS * PACK], BF16, name="w1_grouped", bufs=3, align_bytes=64)
             dst = grouped[:].rearrange("p (t m j) -> p m j t", t=PACK, j=PACK)
-            src = raw.rearrange("p j (m t) -> p m j t", t=PACK)
-            ms = CAST_SCALAR_M[(b, a)]
-            if ms > 0:
-                nc.scalar.copy(dst[:, :ms], src[:, :ms])
-            if ms < P:
-                nc.vector.tensor_copy(dst[:, ms:].rearrange("p m j t -> p m t j"), src[:, ms:].rearrange("p m j t -> p m t j"))
-            codes = keep.tile([P, KP], U32, name=f"w1_codes{b}{a}", align_bytes=64)
-            sc = keep.tile([P, KP], U8, name=f"w1_sc{b}{a}", align_bytes=64)
+            src = w1_raw[(b, a)][:].rearrange("p j (m t) -> p m j t", t=PACK)
+            split = SCALAR_CAST[(b, a)]
+            if split > 0:
+                nc.scalar.copy(dst[:, :split], src[:, :split])
+            if split < P:
+                nc.vector.tensor_copy(
+                    dst[:, split:].rearrange("p m j t -> p m t j"), src[:, split:].rearrange("p m j t -> p m t j")
+                )
+            codes = keep.tile([P, PASS], U32, name=f"w1_codes{b}{a}", align_bytes=64)
+            sc = keep.tile([P, PASS], U8, name=f"w1_sc{b}{a}", align_bytes=64)
             nc.vector.quantize_mx(out=codes[:].bitcast(FP8X4), scales=sc[:], in_=grouped[:])
             w1_codes[(b, a)], w1_sc[(b, a)] = codes, sc
 
-        def gather_words(a):
-            nc.vector.tensor_copy(v_codes[a][:], tab[a][:].bitcast(U32).indirect(idx[:]))
-
         banks = {}
-        begun = {}
 
         def first_product(b, a, u):
             if a == 0:
                 banks[(b, u)] = psum.tile([P, PACK, UNIT], F32, name="bank")
-            begun[(b, u)] = a + 1
             cols = slice(UNIT * u, UNIT * (u + 1))
             for t in range(PACK):
                 m = slice(P * t, P * (t + 1))
@@ -119,215 +108,202 @@ def tile_list_junction_desk_kernel(tc, tab_words, tab_scales, offs, offs2, w1, g
                     rhs=v_codes[a][:, cols].bitcast(FP8X4),
                     rhs_scale=v_sc[4 * a :, cols],
                     start=(a == 0 and t == 0),
-                    stop=(a == KA - 1 and t == PACK - 1),
+                    stop=(a == K_PASSES - 1 and t == PACK - 1),
                 )
 
-        h_codes = [keep.tile([P, S], U32, name=f"h_codes{b}", align_bytes=64) for b in range(HB)]
-        h_sc = [keep.tile([P, S], U8, name=f"h_sc{b}", align_bytes=64) for b in range(HB)]
-
+        h_codes = [keep.tile([P, S], U32, name=f"h_codes{b}", align_bytes=64) for b in range(R_PASSES)]
+        h_sc = [keep.tile([P, S], U8, name=f"h_sc{b}", align_bytes=64) for b in range(R_PASSES)]
         acts = {}
 
-        def silu(b, g):
-            lo, hi = GROUPS[g]
-            w = hi - lo
-            on_scalar = (b, g) in SCALAR_GAIN
-            act = ring.tile([P, PACK, w] if on_scalar else [P, w, PACK], F32, name="act", bufs=5, align_bytes=64)
-            for u in range(lo // UNIT, hi // UNIT):
-                for a in range(begun.get((b, u), 0), KA):
-                    first_product(b, a, u)
-                cols = slice(UNIT * u - lo, UNIT * (u + 1) - lo)
-                if on_scalar:
-                    nc.scalar.activation(act[:, :, cols], banks[(b, u)][:], ACT.Silu)
-                else:
-                    nc.scalar.activation(act[:, cols, :], banks[(b, u)][:].rearrange("p t n -> p n t"), ACT.Silu)
-            acts[(b, g)] = act
+        def units(c):
+            return range(c * CHUNK // UNIT, (c + 1) * CHUNK // UNIT)
 
-        def quantize_h(b, g, h_bf):
-            lo, hi = GROUPS[g]
+        def silu(b, c, first_pass):
+            on_vector = c < VECTOR_GAIN_CHUNKS
+            shape = [P, CHUNK, PACK] if on_vector else [P, PACK, CHUNK]
+            act = ring.tile(shape, F32, name="act", bufs=5, align_bytes=64)
+            for u in units(c):
+                for a in range(first_pass, K_PASSES):
+                    first_product(b, a, u)
+                cols = slice(UNIT * u - CHUNK * c, UNIT * (u + 1) - CHUNK * c)
+                if on_vector:
+                    nc.scalar.activation(act[:, cols, :], banks[(b, u)][:].rearrange("p t e -> p e t"), ACT.Silu)
+                else:
+                    nc.scalar.activation(act[:, :, cols], banks[(b, u)][:], ACT.Silu)
+            acts[(b, c)] = act
+
+        def h_tile(c, shared):
+            if shared:
+                return ring.tile([P, CHUNK, PACK], BF16, name="h_shared", tag=f"shared{c}", bufs=1, align_bytes=64)
+            return ring.tile([P, CHUNK, PACK], BF16, name="h_bf", bufs=3, align_bytes=64)
+
+        def quantize_h(b, c, h_bf):
+            cols = slice(CHUNK * c, CHUNK * (c + 1))
             nc.vector.quantize_mx(
-                out=h_codes[b][:, lo:hi].bitcast(FP8X4),
-                scales=h_sc[b][:, lo:hi],
-                in_=h_bf.rearrange("p n t -> p (n t)"),
+                out=h_codes[b][:, cols].bitcast(FP8X4),
+                scales=h_sc[b][:, cols],
+                in_=h_bf[:].rearrange("p e t -> p (e t)"),
             )
 
-        def h_tile(b, g):
-            lo, hi = GROUPS[g]
-            if (b, g) in HELD:
-                return ring.tile([P, hi - lo, PACK], BF16, name="h_held", tag=f"held{g}", bufs=1, align_bytes=64)
-            return ring.tile([P, hi - lo, PACK], BF16, name="h_bf", bufs=3, align_bytes=64)
+        def gain_on_vector(b, c, shared):
+            h_bf = h_tile(c, shared)
+            factors = gain_sb[:, b : b + 1, :].to_broadcast([P, CHUNK, PACK])
+            nc.vector.tensor_tensor(h_bf[:], acts[(b, c)][:], factors, MULT)
+            quantize_h(b, c, h_bf)
 
-        def hidden(b, g):
-            lo, hi = GROUPS[g]
-            h_bf = h_tile(b, g)
-            nc.vector.tensor_tensor(h_bf[:], acts[(b, g)][:], gain_sb[:, b : b + 1, :].to_broadcast([P, hi - lo, PACK]), MULT)
-            quantize_h(b, g, h_bf[:])
-
-        def hidden_on_scalar(g):
-            lo, hi = GROUPS[g]
-            planes = ring.tile([P, HB, PACK, hi - lo], BF16, name="planes", bufs=1, align_bytes=64)
-            for b in range(HB):
+        def gain_on_scalar(c):
+            runs = ring.tile([P, R_PASSES, PACK, CHUNK], BF16, name="runs", bufs=1, align_bytes=64)
+            for b in range(R_PASSES):
                 for t in range(PACK):
-                    nc.scalar.activation(planes[:, b, t, :], acts[(b, g)][:, t, :], ACT.Copy, scale=gain_sb[:, b, t : t + 1])
-            tiles = [h_tile(b, g) for b in range(HB)]
-            half = (hi - lo) // 2
-            for c in (0, half):
-                for b in range(HB):
+                    factor = gain_sb[:, b, t : t + 1]
+                    nc.scalar.activation(runs[:, b, t, :], acts[(b, c)][:, t, :], ACT.Copy, scale=factor)
+            tiles = [h_tile(c, shared=(b == 0)) for b in range(R_PASSES)]
+            half = CHUNK // 2
+            for lo in (0, half):
+                for b in range(R_PASSES):
                     nc.scalar.copy(
-                        tiles[b][:, c : c + half, :].rearrange("p (c i) t -> p c t i", i=4),
-                        planes[:, b, :, c : c + half].rearrange("p t (c i) -> p c t i", i=4),
+                        tiles[b][:, lo : lo + half, :].rearrange("p (x i) t -> p x t i", i=4),
+                        runs[:, b, :, lo : lo + half].rearrange("p t (x i) -> p x t i", i=4),
                     )
-            for b in range(HB):
-                quantize_h(b, g, tiles[b][:])
+            for b in range(R_PASSES):
+                quantize_h(b, c, tiles[b])
 
         load_tab(0)
         nc.sync.dma_start(idx[:], offs)
         load_w1(0, 0)
-        nc.sync.dma_start(out=gain_sb[:], in_=gain.rearrange("(b p t) -> p b t", b=HB, t=PACK))
-        load_tab(1)
-        load_w1(0, 1)
-        load_tab(2)
-        load_w1(0, 2)
-        for a in range(KA):
+        nc.sync.dma_start(out=gain_sb[:], in_=gain.rearrange("(b p t) -> p b t", b=R_PASSES, t=PACK))
+        for a in range(1, K_PASSES):
+            load_tab(a)
+            load_w1(0, a)
+        for a in range(K_PASSES):
             load_w1(1, a)
 
         nc.vector.tensor_copy(v_sc[:], tab_sc[:].indirect(idx[:]))
-        for a in range(KA):
-            gather_words(a)
+        for a in range(K_PASSES):
+            nc.vector.tensor_copy(v_codes[a][:], tab[a][:].bitcast(U32).indirect(idx[:]))
             quantize_w1(0, a)
-            if a < KA - 1:
-                for u in range(UNITS):
+            if a < K_PASSES - 1:
+                for u in range(S // UNIT):
                     first_product(0, a, u)
+
         nc.sync.dma_start(out=w2_codes[:].bitcast(I32), in_=w2_words.rearrange("b p c -> p b c").bitcast(I32))
         w3_raw = []
-        for b in range(HB):
-            raw3 = ring.tile([P, PACK, N], F32, name="w3_raw", tag="stage", bufs=6)
-            nc.sync.dma_start(out=raw3[:], in_=w3[KP * b : KP * (b + 1), :].rearrange("(p j) n -> p j n", j=PACK))
+        for b in range(R_PASSES):
+            raw3 = ring.tile([P, PACK, N], F32, name="w3_raw", tag="stage", bufs=STAGE_SLOTS)
+            nc.sync.dma_start(out=raw3[:], in_=w3[PASS * b : PASS * (b + 1), :].rearrange("(p j) n -> p j n", j=PACK))
             w3_raw.append(raw3)
         nc.sync.dma_start(idx2[:], offs2)
         wgo_sb = keep.tile([P, S], F32, name="wgo_sb")
         nc.sync.dma_start(out=wgo_sb[:], in_=wgo)
         x0_sb = []
-        for n in range(NT):
-            x0_n = ring.tile([P, S], F32, name="x0_n", tag="stage", bufs=6)
+        for n in range(N_TILES):
+            x0_n = ring.tile([P, S], F32, name="x0_n", tag="stage", bufs=STAGE_SLOTS)
             nc.sync.dma_start(out=x0_n[:], in_=x0[P * n : P * (n + 1), :])
             x0_sb.append(x0_n)
 
-        for a in range(KA):
+        for a in range(K_PASSES):
             quantize_w1(1, a)
-        for g in range(len(GROUPS)):
-            silu(0, g)
-            if g < EARLY:
-                hidden(0, g)
-            lo, hi = GROUPS[g]
-            for u in range(lo // UNIT, hi // UNIT):
+        for c in range(CHUNKS):
+            silu(0, c, K_PASSES - 1)
+            if c == 0:
+                gain_on_vector(0, c, shared=False)
+            for u in units(c):
                 first_product(1, 0, u)
 
         w3_codes, w3_sc = {}, {}
 
-        def quantize_w3(n):
-            grouped3 = keep.tile([P, HB, P, PACK], BF16, name=f"w3_grouped{n}", align_bytes=64)
-            for b in range(HB):
-                dst = grouped3[:, b].rearrange("p (c i) j -> p c j i", i=4)
-                src = w3_raw[b][:, :, P * n : P * (n + 1)].rearrange("p j (c i) -> p c j i", i=4)
-                if n in W3_ON_SCALAR:
-                    nc.scalar.copy(dst, src)
-                else:
-                    nc.vector.tensor_copy(dst, src)
-            codes = keep.tile([P, HB * P], U32, name=f"w3_codes{n}", align_bytes=64)
-            sc = keep.tile([P, HB * P], U8, name=f"w3_sc{n}", align_bytes=64)
-            nc.vector.quantize_mx(out=codes[:].bitcast(FP8X4), scales=sc[:], in_=grouped3[:].rearrange("p b c j -> p (b c j)"))
+        def quantize_w3(n, cast):
+            grouped3 = keep.tile([P, R_PASSES, P, PACK], BF16, name=f"w3_grouped{n}", align_bytes=64)
+            for b in range(R_PASSES):
+                cast(
+                    grouped3[:, b].rearrange("p (x i) j -> p x j i", i=4),
+                    w3_raw[b][:, :, P * n : P * (n + 1)].rearrange("p j (x i) -> p x j i", i=4),
+                )
+            codes = keep.tile([P, R_PASSES * P], U32, name=f"w3_codes{n}", align_bytes=64)
+            sc = keep.tile([P, R_PASSES * P], U8, name=f"w3_sc{n}", align_bytes=64)
+            nc.vector.quantize_mx(
+                out=codes[:].bitcast(FP8X4), scales=sc[:], in_=grouped3[:].rearrange("p b x j -> p (b x j)")
+            )
             w3_codes[n], w3_sc[n] = codes, sc
 
-        pages = [keep.tile([P, S], F32, name=f"page{n}") for n in range(NT)]
+        pages = [keep.tile([P, S], F32, name=f"page{n}") for n in range(N_TILES)]
 
-        def product_d(dst, g, n):
-            lo, hi = GROUPS[g]
-            for c in range(0, hi - lo, UNIT):
-                for b in range(HB):
+        def product_w2(dst, c, n):
+            for lo in range(0, CHUNK, UNIT):
+                cols = slice(CHUNK * c + lo, CHUNK * c + lo + UNIT)
+                for b in range(R_PASSES):
                     nc.tensor.matmul_mx(
-                        out=dst[:, c : c + UNIT],
+                        out=dst[:, lo : lo + UNIT],
                         lhsT=w2_codes[:, b, 2 * P * n : 2 * P * (n + 1)].bitcast(FP4X4),
                         lhsT_scale=w2_sc[:, b, P * n : P * (n + 1)],
-                        rhs=h_codes[b][:, lo + c : lo + c + UNIT].bitcast(FP8X4),
-                        rhs_scale=h_sc[b][:, lo + c : lo + c + UNIT],
+                        rhs=h_codes[b][:, cols].bitcast(FP8X4),
+                        rhs_scale=h_sc[b][:, cols],
                         start=(b == 0),
-                        stop=(b == HB - 1),
+                        stop=(b == R_PASSES - 1),
                     )
 
-        def product_e(dst, g, n):
-            lo, hi = GROUPS[g]
-            for b in range(HB):
+        def product_w3(dst, c, n):
+            cols = slice(CHUNK * c, CHUNK * (c + 1))
+            for b in range(R_PASSES):
                 nc.tensor.matmul_mx(
                     out=dst,
                     lhsT=w3_codes[n][:, P * b : P * (b + 1)].bitcast(FP8X4),
                     lhsT_scale=w3_sc[n][:, P * b : P * (b + 1)],
-                    rhs=h_codes[b][:, lo:hi].bitcast(FP8X4),
-                    rhs_scale=h_sc[b][:, lo:hi],
+                    rhs=h_codes[b][:, cols].bitcast(FP8X4),
+                    rhs_scale=h_sc[b][:, cols],
                     start=(b == 0),
-                    stop=(b == HB - 1),
+                    stop=(b == R_PASSES - 1),
                 )
 
-        def scores(g, ns):
-            lo, hi = GROUPS[g]
-            w = hi - lo
-            k = len(ns)
-            if 2 * k * w <= KP:
-                both = psum.tile([P, 2, k, w], F32, name="bank")
+        def scores(c, tiles_n):
+            count = len(tiles_n)
+            if 2 * count * CHUNK <= BANK:
+                both = psum.tile([P, 2, count, CHUNK], F32, name="bank")
                 d_ps, e_ps = both[:, 0], both[:, 1]
             else:
-                d_tile = psum.tile([P, k, w], F32, name="bank")
-                e_tile = psum.tile([P, k, w], F32, name="bank")
+                d_tile = psum.tile([P, count, CHUNK], F32, name="bank")
+                e_tile = psum.tile([P, count, CHUNK], F32, name="bank")
                 d_ps, e_ps = d_tile[:], e_tile[:]
-            for i, n in enumerate(ns):
-                product_d(d_ps[:, i, :], g, n)
-            for i, n in enumerate(ns):
-                product_e(e_ps[:, i, :], g, n)
-            if ((0, g + 1) in HELD or (1, g + 1) in HELD) and ns[-1] == NT - 1:
-                y = ring.tile([P, k, w], F32, name="y", tag=f"held{g + 1}", bufs=1, align_bytes=64)
+            for i, n in enumerate(tiles_n):
+                product_w2(d_ps[:, i, :], c, n)
+            for i, n in enumerate(tiles_n):
+                product_w3(e_ps[:, i, :], c, n)
+            if c + 1 < CHUNKS and tiles_n[-1] == N_TILES - 1:
+                y = ring.tile([P, count, CHUNK], F32, name="y", tag=f"shared{c + 1}", bufs=1, align_bytes=64)
             else:
-                y = ring.tile([P, k, w], F32, name="y", bufs=3, align_bytes=64)
-            places = idx2[:, lo // 16 : hi // 16]
-            if g in POOL_CHUNKS:
-                de = ring.tile([P, 2, k, w], F32, name="de", bufs=4)
-                nc.scalar.copy(de[:], both[:])
-                yy = ring.tile([P, k, w], F32, name="yy", bufs=2)
-                nc.gpsimd.tensor_tensor(yy[:], de[:, 0], de[:, 1], MULT)
-                nc.gpsimd.tensor_tensor(y[:, 0, :], yy[:, 0, :], wgo_sb[:, lo:hi], MULT)
-                nc.vector.tensor_copy(pages[ns[0]][:].indirect(places), y[:, 0, :])
-                return
-            d_sb = ring.tile([P, k, w], F32, name="d_sb", bufs=4)
+                y = ring.tile([P, count, CHUNK], F32, name="y", bufs=3, align_bytes=64)
+            d_sb = ring.tile([P, count, CHUNK], F32, name="d_sb", bufs=4)
             nc.scalar.copy(d_sb[:], d_ps)
-            for i in range(k):
+            for i in range(count):
                 nc.vector.tensor_tensor(y[:, i, :], e_ps[:, i, :], d_sb[:, i, :], MULT)
-            for i, n in enumerate(ns):
-                nc.vector.tensor_tensor(pages[n][:].indirect(places), y[:, i, :], wgo_sb[:, lo:hi], MULT)
+            places = idx2[:, CHUNK * c // LIST_ROWS : CHUNK * (c + 1) // LIST_ROWS]
+            weights = wgo_sb[:, CHUNK * c : CHUNK * (c + 1)]
+            for i, n in enumerate(tiles_n):
+                nc.vector.tensor_tensor(pages[n][:].indirect(places), y[:, i, :], weights, MULT)
 
-        def finish(n):
-            for lo in range(0, S, KP):
-                th = ring.tile([P, KP], F32, name="th", bufs=4)
-                nc.scalar.activation(th[:], pages[n][:, lo : lo + KP], ACT.Tanh)
-                adder = nc.gpsimd if n in POOL_ADDS else nc.vector
-                adder.tensor_tensor(x0_sb[n][:, lo : lo + KP], x0_sb[n][:, lo : lo + KP], th[:], ADD)
-                nc.sync.dma_start(out=out[P * n : P * (n + 1), lo : lo + KP], in_=x0_sb[n][:, lo : lo + KP])
-
-        last = len(GROUPS) - 1
-        silu(1, 0)
-        hidden(1, 0)
-        quantize_w3(0)
+        silu(1, 0, 1)
+        gain_on_vector(1, 0, shared=False)
+        quantize_w3(0, nc.vector.tensor_copy)
         scores(0, [0])
-        quantize_w3(1)
-        quantize_w3(2)
-        for g in range(1, len(GROUPS)):
-            silu(1, g)
-        for g in range(len(GROUPS)):
-            if g > 0:
-                scores(g, [0])
-            if g < last:
-                if (0, g + 1) in SCALAR_GAIN:
-                    hidden_on_scalar(g + 1)
-                else:
-                    hidden(0, g + 1)
-                    hidden(1, g + 1)
-            scores(g, [1, 2])
-        for n in range(NT):
-            finish(n)
+        for n in range(1, N_TILES):
+            quantize_w3(n, nc.scalar.copy)
+        for c in range(1, CHUNKS):
+            silu(1, c, 1)
+        for c in range(CHUNKS):
+            if c > 0:
+                scores(c, [0])
+            if c + 1 < VECTOR_GAIN_CHUNKS:
+                gain_on_vector(0, c + 1, shared=False)
+                gain_on_vector(1, c + 1, shared=True)
+            elif c + 1 < CHUNKS:
+                gain_on_scalar(c + 1)
+            scores(c, list(range(1, N_TILES)))
+
+        half_page = S // 2
+        for n in range(N_TILES):
+            for lo in range(0, S, half_page):
+                cols = slice(lo, lo + half_page)
+                bounded = ring.tile([P, half_page], F32, name="bounded", bufs=4)
+                nc.scalar.activation(bounded[:], pages[n][:, cols], ACT.Tanh)
+                nc.vector.tensor_tensor(x0_sb[n][:, cols], x0_sb[n][:, cols], bounded[:], ADD)
+                nc.sync.dma_start(out=out[P * n : P * (n + 1), cols], in_=x0_sb[n][:, cols])

@@ -27,11 +27,12 @@ K_PASSES = K // PASS
 R_PASSES = H // PASS
 N_TILES = N // P
 UNIT = 128
-CHUNK = 256
-CHUNKS = S // CHUNK
-VECTOR_GAIN_CHUNKS = 2
-SCALAR_CAST = {(0, 0): P, (0, 1): P, (0, 2): 44, (1, 0): 0, (1, 1): 16, (1, 2): 44}
+CHUNK_UNITS = [[0], [1], [2, 3], [4, 5], [6, 7]]
+CHUNKS = len(CHUNK_UNITS)
+VECTOR_GAINS = {(0, 0), (1, 0), (0, 1), (1, 1), (0, 2), (1, 2)}
+SCALAR_CAST = {(0, 0): P, (0, 1): P, (0, 2): P, (1, 0): 32, (1, 1): 32, (1, 2): 44}
 STAGE_SLOTS = 6
+SCORE_BANKS = [0, 1, 0, 1, 2, 3, 0, 4, 5, 1, 6, 7, 2]
 
 
 def tile_list_junction_desk_kernel(
@@ -41,11 +42,11 @@ def tile_list_junction_desk_kernel(
     with ExitStack() as ctx:
         keep = ctx.enter_context(tc.tile_pool(name="keep", bufs=1))
         ring = ctx.enter_context(tc.tile_pool(name="ring", bufs=1))
-        psum = ctx.enter_context(tc.psum_pool(name="psum", bufs=8))
+        psum = ctx.enter_context(tc.psum_pool(name="psum", bufs=1))
 
         idx = keep.tile([P, S // LIST_ROWS], U16, name="idx")
         idx2 = keep.tile([P, S // LIST_ROWS], U16, name="idx2")
-        tab = [keep.tile([P, T], I32, name=f"tab{a}", align_bytes=64) for a in range(K_PASSES)]
+        tab = [ring.tile([P, T], I32, name=f"tab{a}", bufs=1, align_bytes=64) for a in range(K_PASSES)]
         tab_sc = keep.tile([P, T], U8, name="tab_sc", align_bytes=64)
         v_codes = [keep.tile([P, S], U32, name=f"v_codes{a}", align_bytes=64) for a in range(K_PASSES)]
         v_sc = keep.tile([P, S], U8, name="v_sc", align_bytes=64)
@@ -78,7 +79,10 @@ def tile_list_junction_desk_kernel(
             w1_raw[(b, a)] = raw
 
         def quantize_w1(b, a):
-            grouped = ring.tile([P, PASS * PACK], BF16, name="w1_grouped", bufs=3, align_bytes=64)
+            if (b, a) == (R_PASSES - 1, K_PASSES - 1):
+                grouped = ring.tile([P, PASS * PACK], BF16, name="w1_last", tag="after_w1", bufs=1, align_bytes=64)
+            else:
+                grouped = ring.tile([P, PASS * PACK], BF16, name="w1_grouped", bufs=2, align_bytes=64)
             dst = grouped[:].rearrange("p (t m j) -> p m j t", t=PACK, j=PACK)
             src = w1_raw[(b, a)][:].rearrange("p j (m t) -> p m j t", t=PACK)
             split = SCALAR_CAST[(b, a)]
@@ -97,7 +101,7 @@ def tile_list_junction_desk_kernel(
 
         def first_product(b, a, u):
             if a == 0:
-                banks[(b, u)] = psum.tile([P, PACK, UNIT], F32, name="bank")
+                banks[(b, u)] = psum.tile([P, PACK, UNIT], F32, name=f"bank{u}")
             cols = slice(UNIT * u, UNIT * (u + 1))
             for t in range(PACK):
                 m = slice(P * t, P * (t + 1))
@@ -111,199 +115,277 @@ def tile_list_junction_desk_kernel(
                     stop=(a == K_PASSES - 1 and t == PACK - 1),
                 )
 
-        h_codes = [keep.tile([P, S], U32, name=f"h_codes{b}", align_bytes=64) for b in range(R_PASSES)]
-        h_sc = [keep.tile([P, S], U8, name=f"h_sc{b}", align_bytes=64) for b in range(R_PASSES)]
-        acts = {}
+        acts, runs, h_tiles, h_codes, h_sc = {}, {}, {}, {}, {}
 
-        def units(c):
-            return range(c * CHUNK // UNIT, (c + 1) * CHUNK // UNIT)
+        def span(c):
+            return UNIT * CHUNK_UNITS[c][0], UNIT * (CHUNK_UNITS[c][-1] + 1)
 
-        def silu(b, c, first_pass):
-            on_vector = c < VECTOR_GAIN_CHUNKS
-            shape = [P, CHUNK, PACK] if on_vector else [P, PACK, CHUNK]
-            act = ring.tile(shape, F32, name="act", bufs=5, align_bytes=64)
-            for u in units(c):
-                for a in range(first_pass, K_PASSES):
-                    first_product(b, a, u)
-                cols = slice(UNIT * u - CHUNK * c, UNIT * (u + 1) - CHUNK * c)
+        def silu(b, c, tag=None):
+            lo, hi = span(c)
+            on_vector = (b, c) in VECTOR_GAINS
+            shape = [P, hi - lo, PACK] if on_vector else [P, PACK, hi - lo]
+            if tag:
+                act = ring.tile(shape, F32, name="act", tag=tag, bufs=1, align_bytes=64)
+            elif b == 0:
+                act = keep.tile(shape, F32, name=f"act0{c}", align_bytes=64)
+            else:
+                act = ring.tile(shape, F32, name="act", bufs=2, align_bytes=64)
+            for u in CHUNK_UNITS[c]:
+                cols = slice(UNIT * u - lo, UNIT * (u + 1) - lo)
                 if on_vector:
                     nc.scalar.activation(act[:, cols, :], banks[(b, u)][:].rearrange("p t e -> p e t"), ACT.Silu)
                 else:
                     nc.scalar.activation(act[:, :, cols], banks[(b, u)][:], ACT.Silu)
             acts[(b, c)] = act
 
-        def h_tile(c, shared):
-            if shared:
-                return ring.tile([P, CHUNK, PACK], BF16, name="h_shared", tag=f"shared{c}", bufs=1, align_bytes=64)
-            return ring.tile([P, CHUNK, PACK], BF16, name="h_bf", bufs=3, align_bytes=64)
+        def h_tile(b, c, tag):
+            lo, hi = span(c)
+            h_tiles[(b, c)] = ring.tile([P, hi - lo, PACK], BF16, name="h_bf", tag=tag, bufs=1, align_bytes=64)
+            return h_tiles[(b, c)]
 
-        def quantize_h(b, c, h_bf):
-            cols = slice(CHUNK * c, CHUNK * (c + 1))
-            nc.vector.quantize_mx(
-                out=h_codes[b][:, cols].bitcast(FP8X4),
-                scales=h_sc[b][:, cols],
-                in_=h_bf[:].rearrange("p e t -> p (e t)"),
-            )
+        def gain_on_vector(b, c, tag):
+            lo, hi = span(c)
+            factors = gain_sb[:, b : b + 1, :].to_broadcast([P, hi - lo, PACK])
+            nc.vector.tensor_tensor(h_tile(b, c, tag)[:], acts[(b, c)][:], factors, MULT)
 
-        def gain_on_vector(b, c, shared):
-            h_bf = h_tile(c, shared)
-            factors = gain_sb[:, b : b + 1, :].to_broadcast([P, CHUNK, PACK])
-            nc.vector.tensor_tensor(h_bf[:], acts[(b, c)][:], factors, MULT)
-            quantize_h(b, c, h_bf)
-
-        def gain_on_scalar(c):
-            runs = ring.tile([P, R_PASSES, PACK, CHUNK], BF16, name="runs", bufs=1, align_bytes=64)
-            for b in range(R_PASSES):
+        def gain_on_scalar(passes, c, tags):
+            lo, hi = span(c)
+            rows = ring.tile([P, len(passes), PACK, hi - lo], BF16, name="runs", bufs=1, align_bytes=64)
+            for i, b in enumerate(passes):
                 for t in range(PACK):
                     factor = gain_sb[:, b, t : t + 1]
-                    nc.scalar.activation(runs[:, b, t, :], acts[(b, c)][:, t, :], ACT.Copy, scale=factor)
-            tiles = [h_tile(c, shared=(b == 0)) for b in range(R_PASSES)]
-            half = CHUNK // 2
-            for lo in (0, half):
-                for b in range(R_PASSES):
+                    nc.scalar.activation(rows[:, i, t, :], acts[(b, c)][:, t, :], ACT.Copy, scale=factor)
+            tiles = [h_tile(b, c, tag) for b, tag in zip(passes, tags)]
+            half = (hi - lo) // 2
+            for k in (0, half):
+                for i in range(len(passes)):
                     nc.scalar.copy(
-                        tiles[b][:, lo : lo + half, :].rearrange("p (x i) t -> p x t i", i=4),
-                        runs[:, b, :, lo : lo + half].rearrange("p t (x i) -> p x t i", i=4),
+                        tiles[i][:, k : k + half, :].rearrange("p (x i) t -> p x t i", i=4),
+                        rows[:, i, :, k : k + half].rearrange("p t (x i) -> p x t i", i=4),
                     )
-            for b in range(R_PASSES):
-                quantize_h(b, c, tiles[b])
+
+        def quantize_h(b, c):
+            lo, hi = span(c)
+            h_codes[(b, c)] = keep.tile([P, hi - lo], U32, name=f"h_codes{b}{c}", align_bytes=64)
+            h_sc[(b, c)] = keep.tile([P, hi - lo], U8, name=f"h_sc{b}{c}", align_bytes=64)
+            nc.vector.quantize_mx(
+                out=h_codes[(b, c)][:].bitcast(FP8X4),
+                scales=h_sc[(b, c)][:],
+                in_=h_tiles[(b, c)][:].rearrange("p e t -> p (e t)"),
+            )
 
         load_tab(0)
         nc.sync.dma_start(idx[:], offs)
         load_w1(0, 0)
+        load_tab(1)
+        load_w1(0, 1)
+        load_w1(0, 2)
+        load_tab(2)
         nc.sync.dma_start(out=gain_sb[:], in_=gain.rearrange("(b p t) -> p b t", b=R_PASSES, t=PACK))
-        for a in range(1, K_PASSES):
-            load_tab(a)
-            load_w1(0, a)
         for a in range(K_PASSES):
             load_w1(1, a)
-
         nc.vector.tensor_copy(v_sc[:], tab_sc[:].indirect(idx[:]))
         for a in range(K_PASSES):
-            nc.vector.tensor_copy(v_codes[a][:], tab[a][:].bitcast(U32).indirect(idx[:]))
             quantize_w1(0, a)
-            if a < K_PASSES - 1:
-                for u in range(S // UNIT):
-                    first_product(0, a, u)
+            width = S if a < K_PASSES - 1 else S // 2
+            for lo in range(0, S, width):
+                entries = idx[:, lo // LIST_ROWS : (lo + width) // LIST_ROWS]
+                nc.vector.tensor_copy(v_codes[a][:, lo : lo + width], tab[a][:].bitcast(U32).indirect(entries))
+            for u in range(S // UNIT):
+                first_product(0, a, u)
 
-        nc.sync.dma_start(out=w2_codes[:].bitcast(I32), in_=w2_words.rearrange("b p c -> p b c").bitcast(I32))
-        w3_raw = []
+        w3_both = ring.tile([P, R_PASSES, PACK, N], F32, name="w3_both", tag="tab0", bufs=1, align_bytes=64)
+        w3_raw = [w3_both[:, b] for b in range(R_PASSES)]
         for b in range(R_PASSES):
-            raw3 = ring.tile([P, PACK, N], F32, name="w3_raw", tag="stage", bufs=STAGE_SLOTS)
-            nc.sync.dma_start(out=raw3[:], in_=w3[PASS * b : PASS * (b + 1), :].rearrange("(p j) n -> p j n", j=PACK))
-            w3_raw.append(raw3)
+            nc.sync.dma_start(out=w3_raw[b], in_=w3[PASS * b : PASS * (b + 1), :].rearrange("(p j) n -> p j n", j=PACK))
+        nc.sync.dma_start(out=w2_codes[:].bitcast(I32), in_=w2_words.rearrange("b p c -> p b c").bitcast(I32))
         nc.sync.dma_start(idx2[:], offs2)
-        wgo_sb = keep.tile([P, S], F32, name="wgo_sb")
-        nc.sync.dma_start(out=wgo_sb[:], in_=wgo)
-        x0_sb = []
-        for n in range(N_TILES):
-            x0_n = ring.tile([P, S], F32, name="x0_n", tag="stage", bufs=STAGE_SLOTS)
-            nc.sync.dma_start(out=x0_n[:], in_=x0[P * n : P * (n + 1), :])
-            x0_sb.append(x0_n)
-
-        for a in range(K_PASSES):
-            quantize_w1(1, a)
-        for c in range(CHUNKS):
-            silu(0, c, K_PASSES - 1)
-            if c == 0:
-                gain_on_vector(0, c, shared=False)
-            for u in units(c):
-                first_product(1, 0, u)
+        wgo_sb = {}
+        for chunks in ([0, 1], list(range(2, CHUNKS))):
+            lo, hi = span(chunks[0])[0], span(chunks[-1])[1]
+            part = keep.tile([P, hi - lo], F32, name=f"wgo{chunks[0]}")
+            nc.sync.dma_start(out=part[:], in_=wgo[:, lo:hi])
+            for c in chunks:
+                wgo_sb[c] = part[:, span(c)[0] - lo : span(c)[1] - lo]
 
         w3_codes, w3_sc = {}, {}
 
-        def quantize_w3(n, cast):
-            grouped3 = keep.tile([P, R_PASSES, P, PACK], BF16, name=f"w3_grouped{n}", align_bytes=64)
-            for b in range(R_PASSES):
+        def quantize_w3(passes, tiles_n, cast, tag):
+            width = P * len(tiles_n)
+            grouped3 = ring.tile([P, len(passes), width, PACK], BF16, name="w3_grouped", tag=tag, bufs=1, align_bytes=64)
+            for i, b in enumerate(passes):
                 cast(
-                    grouped3[:, b].rearrange("p (x i) j -> p x j i", i=4),
-                    w3_raw[b][:, :, P * n : P * (n + 1)].rearrange("p j (x i) -> p x j i", i=4),
+                    grouped3[:, i].rearrange("p (x i) j -> p x j i", i=4),
+                    w3_raw[b][:, :, P * tiles_n[0] : P * tiles_n[0] + width].rearrange("p j (x i) -> p x j i", i=4),
                 )
-            codes = keep.tile([P, R_PASSES * P], U32, name=f"w3_codes{n}", align_bytes=64)
-            sc = keep.tile([P, R_PASSES * P], U8, name=f"w3_sc{n}", align_bytes=64)
+            codes = keep.tile([P, len(passes) * width], U32, name=f"w3_codes_{tag}", align_bytes=64)
+            sc = keep.tile([P, len(passes) * width], U8, name=f"w3_sc_{tag}", align_bytes=64)
             nc.vector.quantize_mx(
                 out=codes[:].bitcast(FP8X4), scales=sc[:], in_=grouped3[:].rearrange("p b x j -> p (b x j)")
             )
-            w3_codes[n], w3_sc[n] = codes, sc
+            for i, b in enumerate(passes):
+                for k, n in enumerate(tiles_n):
+                    cols = slice(width * i + P * k, width * i + P * (k + 1))
+                    w3_codes[(b, n)], w3_sc[(b, n)] = codes[:, cols], sc[:, cols]
 
         pages = [keep.tile([P, S], F32, name=f"page{n}") for n in range(N_TILES)]
 
         def product_w2(dst, c, n):
-            for lo in range(0, CHUNK, UNIT):
-                cols = slice(CHUNK * c + lo, CHUNK * c + lo + UNIT)
+            for i in range(len(CHUNK_UNITS[c])):
+                cols = slice(UNIT * i, UNIT * (i + 1))
                 for b in range(R_PASSES):
                     nc.tensor.matmul_mx(
-                        out=dst[:, lo : lo + UNIT],
+                        out=dst[:, cols],
                         lhsT=w2_codes[:, b, 2 * P * n : 2 * P * (n + 1)].bitcast(FP4X4),
                         lhsT_scale=w2_sc[:, b, P * n : P * (n + 1)],
-                        rhs=h_codes[b][:, cols].bitcast(FP8X4),
-                        rhs_scale=h_sc[b][:, cols],
+                        rhs=h_codes[(b, c)][:, cols].bitcast(FP8X4),
+                        rhs_scale=h_sc[(b, c)][:, cols],
                         start=(b == 0),
                         stop=(b == R_PASSES - 1),
                     )
 
         def product_w3(dst, c, n):
-            cols = slice(CHUNK * c, CHUNK * (c + 1))
             for b in range(R_PASSES):
                 nc.tensor.matmul_mx(
                     out=dst,
-                    lhsT=w3_codes[n][:, P * b : P * (b + 1)].bitcast(FP8X4),
-                    lhsT_scale=w3_sc[n][:, P * b : P * (b + 1)],
-                    rhs=h_codes[b][:, cols].bitcast(FP8X4),
-                    rhs_scale=h_sc[b][:, cols],
+                    lhsT=w3_codes[(b, n)].bitcast(FP8X4),
+                    lhsT_scale=w3_sc[(b, n)],
+                    rhs=h_codes[(b, c)][:].bitcast(FP8X4),
+                    rhs_scale=h_sc[(b, c)][:],
                     start=(b == 0),
                     stop=(b == R_PASSES - 1),
                 )
 
-        def scores(c, tiles_n):
+        used_banks = []
+        sums, ys = {}, {}
+
+        def score_bank(shape):
+            number = SCORE_BANKS[len(used_banks)]
+            used_banks.append(number)
+            return psum.tile(shape, F32, name=f"bank{number}")
+
+        def products(c, tiles_n):
+            lo, hi = span(c)
             count = len(tiles_n)
-            if 2 * count * CHUNK <= BANK:
-                both = psum.tile([P, 2, count, CHUNK], F32, name="bank")
+            if 2 * count * (hi - lo) <= BANK:
+                both = score_bank([P, 2, count, hi - lo])
                 d_ps, e_ps = both[:, 0], both[:, 1]
             else:
-                d_tile = psum.tile([P, count, CHUNK], F32, name="bank")
-                e_tile = psum.tile([P, count, CHUNK], F32, name="bank")
-                d_ps, e_ps = d_tile[:], e_tile[:]
+                d_ps = score_bank([P, count, hi - lo])[:]
+                e_ps = score_bank([P, count, hi - lo])[:]
             for i, n in enumerate(tiles_n):
                 product_w2(d_ps[:, i, :], c, n)
             for i, n in enumerate(tiles_n):
                 product_w3(e_ps[:, i, :], c, n)
-            if c + 1 < CHUNKS and tiles_n[-1] == N_TILES - 1:
-                y = ring.tile([P, count, CHUNK], F32, name="y", tag=f"shared{c + 1}", bufs=1, align_bytes=64)
-            else:
-                y = ring.tile([P, count, CHUNK], F32, name="y", bufs=3, align_bytes=64)
-            d_sb = ring.tile([P, count, CHUNK], F32, name="d_sb", bufs=4)
+            sums[(c, tiles_n[0])] = (d_ps, e_ps)
+
+        def copy_d(c, tiles_n):
+            lo, hi = span(c)
+            d_ps, e_ps = sums[(c, tiles_n[0])]
+            d_sb = ring.tile([P, len(tiles_n), hi - lo], F32, name="d_sb", bufs=3)
             nc.scalar.copy(d_sb[:], d_ps)
-            for i in range(count):
-                nc.vector.tensor_tensor(y[:, i, :], e_ps[:, i, :], d_sb[:, i, :], MULT)
-            places = idx2[:, CHUNK * c // LIST_ROWS : CHUNK * (c + 1) // LIST_ROWS]
-            weights = wgo_sb[:, CHUNK * c : CHUNK * (c + 1)]
+            sums[(c, tiles_n[0])] = (d_sb, e_ps)
+
+        def multiply(c, tiles_n, tag=None):
+            lo, hi = span(c)
+            shape = [P, len(tiles_n), hi - lo]
+            if tag:
+                y = ring.tile(shape, F32, name="y", tag=tag, bufs=1, align_bytes=64)
+            else:
+                y = ring.tile(shape, F32, name="y", bufs=2, align_bytes=64)
+            d_sb, e_ps = sums[(c, tiles_n[0])]
             for i, n in enumerate(tiles_n):
-                nc.vector.tensor_tensor(pages[n][:].indirect(places), y[:, i, :], weights, MULT)
+                nc.vector.tensor_tensor(y[:, i, :], e_ps[:, i, :], d_sb[:, i, :], MULT)
+                ys[(c, n)] = y[:, i, :]
 
-        silu(1, 0, 1)
-        gain_on_vector(1, 0, shared=False)
-        quantize_w3(0, nc.vector.tensor_copy)
-        scores(0, [0])
-        for n in range(1, N_TILES):
-            quantize_w3(n, nc.scalar.copy)
-        for c in range(1, CHUNKS):
-            silu(1, c, 1)
-        for c in range(CHUNKS):
-            if c > 0:
-                scores(c, [0])
-            if c + 1 < VECTOR_GAIN_CHUNKS:
-                gain_on_vector(0, c + 1, shared=False)
-                gain_on_vector(1, c + 1, shared=True)
-            elif c + 1 < CHUNKS:
-                gain_on_scalar(c + 1)
-            scores(c, list(range(1, N_TILES)))
+        def place(c, tiles_n):
+            lo, hi = span(c)
+            places = idx2[:, lo // LIST_ROWS : hi // LIST_ROWS]
+            for n in tiles_n:
+                nc.vector.tensor_tensor(pages[n][:].indirect(places), ys[(c, n)], wgo_sb[c], MULT)
 
-        half_page = S // 2
-        for n in range(N_TILES):
-            for lo in range(0, S, half_page):
-                cols = slice(lo, lo + half_page)
-                bounded = ring.tile([P, half_page], F32, name="bounded", bufs=4)
+        def second_half(a, chunks):
+            for c in chunks:
+                for u in CHUNK_UNITS[c]:
+                    first_product(1, a, u)
+
+        def finish(n, pieces):
+            width = S // pieces
+            for lo in range(0, S, width):
+                cols = slice(lo, lo + width)
+                bounded = ring.tile([P, width], F32, name="bounded", bufs=4)
                 nc.scalar.activation(bounded[:], pages[n][:, cols], ACT.Tanh)
                 nc.vector.tensor_tensor(x0_sb[n][:, cols], x0_sb[n][:, cols], bounded[:], ADD)
                 nc.sync.dma_start(out=out[P * n : P * (n + 1), cols], in_=x0_sb[n][:, cols])
+
+        def load_x0():
+            for n in range(N_TILES):
+                x0_n = ring.tile([P, S], F32, name="x0_n", tag="stage", bufs=STAGE_SLOTS)
+                nc.sync.dma_start(out=x0_n[:], in_=x0[P * n : P * (n + 1), :])
+                x0_sb.append(x0_n)
+
+        x0_sb = []
+        quantize_w1(1, 0)
+        quantize_w1(1, 1)
+        quantize_w1(1, 2)
+        load_x0()
+        silu(0, 0)
+        silu(0, 1)
+        for a in range(K_PASSES):
+            second_half(a, [0, 1])
+        gain_on_vector(0, 0, "h00")
+        quantize_h(0, 0)
+        gain_on_vector(0, 1, "h01")
+        quantize_h(0, 1)
+        silu(1, 0, "after_gain")
+        silu(1, 1)
+        gain_on_vector(1, 0, "shared1")
+        quantize_h(1, 0)
+        quantize_w3([0, 1], [0], nc.vector.tensor_copy, "w3_first")
+        products(0, [0])
+        copy_d(0, [0])
+        multiply(0, [0])
+        place(0, [0])
+        gain_on_vector(1, 1, "shared1")
+        quantize_h(1, 1)
+        products(1, [0])
+        copy_d(1, [0])
+        multiply(1, [0])
+        place(1, [0])
+        silu(0, 2)
+        gain_on_vector(0, 2, "after_w1")
+        quantize_h(0, 2)
+        quantize_w3([0], [1, 2], nc.scalar.copy, "w3_second")
+        quantize_w3([1], [1, 2], nc.scalar.copy, "after_gain")
+        silu(0, 3)
+        silu(0, 4)
+        for c in range(2, CHUNKS):
+            for a in range(K_PASSES):
+                second_half(a, [c])
+        silu(1, 2)
+        for c in (0, 1):
+            products(c, [1, 2])
+            copy_d(c, [1, 2])
+        gain_on_vector(1, 2, "shared2")
+        quantize_h(1, 2)
+        multiply(0, [1, 2])
+        place(0, [1, 2])
+        multiply(1, [1, 2], "shared2")
+        place(1, [1, 2])
+        for c in range(2, CHUNKS):
+            products(c, [0, 1])
+            products(c, [2])
+            if c + 1 < CHUNKS:
+                silu(1, c + 1)
+                gain_on_scalar([0, 1], c + 1, [f"shared{c + 1}", f"second{c + 1}"])
+            copy_d(c, [0, 1])
+            copy_d(c, [2])
+            if c + 1 < CHUNKS:
+                quantize_h(0, c + 1)
+                quantize_h(1, c + 1)
+            multiply(c, [0, 1], f"shared{c + 1}" if c + 1 < CHUNKS else None)
+            multiply(c, [2], f"second{c + 1}" if c + 1 < CHUNKS else None)
+            place(c, [0, 1, 2])
+        finish(0, 2)
+        finish(1, 2)
+        finish(2, 4)

@@ -20,19 +20,18 @@ ADD = mybir.AluOpType.add
 P = 128
 PACK = 4
 PASS = P * PACK
-BANK = 512
 QUADS = 4
 LIST_ROWS = 16
 K_PASSES = K // PASS
 R_PASSES = H // PASS
 N_TILES = N // P
 UNIT = 128
-CHUNK_UNITS = [[0], [1], [2, 3], [4, 5], [6, 7]]
-CHUNKS = len(CHUNK_UNITS)
-VECTOR_GAINS = {(0, 0), (1, 0), (0, 1), (1, 1), (0, 2), (1, 2)}
-SCALAR_CAST = {(0, 0): P, (0, 1): P, (0, 2): P, (1, 0): 32, (1, 1): 32, (1, 2): 44}
+CHUNK = 2 * UNIT
+CHUNKS = S // CHUNK
+VECTOR_GAIN_CHUNKS = 2
+SCALAR_SHARE = 44
 STAGE_SLOTS = 6
-SCORE_BANKS = [0, 1, 0, 1, 2, 3, 0, 4, 5, 1, 6, 7, 2]
+SCORE_BANKS = [0, 1, 0, 2, 3, 1, 4, 5, 0, 6, 7, 2]
 
 
 def tile_list_junction_desk_kernel(
@@ -44,9 +43,12 @@ def tile_list_junction_desk_kernel(
         ring = ctx.enter_context(tc.tile_pool(name="ring", bufs=1))
         psum = ctx.enter_context(tc.psum_pool(name="psum", bufs=1))
 
+        def slot_tile(shape, dtype, name, tag):
+            return ring.tile(shape, dtype, name=name, tag=tag, bufs=1, align_bytes=64)
+
         idx = keep.tile([P, S // LIST_ROWS], U16, name="idx")
         idx2 = keep.tile([P, S // LIST_ROWS], U16, name="idx2")
-        tab = [ring.tile([P, T], I32, name=f"tab{a}", bufs=1, align_bytes=64) for a in range(K_PASSES)]
+        tab = [slot_tile([P, T], I32, f"tab{a}", f"tab{a}") for a in range(K_PASSES)]
         tab_sc = keep.tile([P, T], U8, name="tab_sc", align_bytes=64)
         v_codes = [keep.tile([P, S], U32, name=f"v_codes{a}", align_bytes=64) for a in range(K_PASSES)]
         v_sc = keep.tile([P, S], U8, name="v_sc", align_bytes=64)
@@ -67,7 +69,7 @@ def tile_list_junction_desk_kernel(
                 in_=w2_scales[:, 4 * q : 4 * q + 4, :].rearrange("b r n -> r b n").bitcast(I32),
             )
 
-        w1_raw, w1_codes, w1_sc = {}, {}, {}
+        w1_raw, w1_grouped, w1_codes, w1_sc = {}, {}, {}, {}
 
         def load_tab(a):
             nc.sync.dma_start(out=tab[a][:], in_=tab_words[a].rearrange("p t i -> p (t i)").bitcast(I32))
@@ -78,23 +80,25 @@ def tile_list_junction_desk_kernel(
             nc.sync.dma_start(out=raw[:], in_=rows.rearrange("(p j) r -> p j r", j=PACK))
             w1_raw[(b, a)] = raw
 
-        def quantize_w1(b, a):
+        def cast_w1(b, a):
             if (b, a) == (R_PASSES - 1, K_PASSES - 1):
-                grouped = ring.tile([P, PASS * PACK], BF16, name="w1_last", tag="after_w1", bufs=1, align_bytes=64)
+                grouped = slot_tile([P, PASS * PACK], BF16, "w1_last", "after_w1")
             else:
                 grouped = ring.tile([P, PASS * PACK], BF16, name="w1_grouped", bufs=2, align_bytes=64)
             dst = grouped[:].rearrange("p (t m j) -> p m j t", t=PACK, j=PACK)
             src = w1_raw[(b, a)][:].rearrange("p j (m t) -> p m j t", t=PACK)
-            split = SCALAR_CAST[(b, a)]
-            if split > 0:
-                nc.scalar.copy(dst[:, :split], src[:, :split])
+            split = P if b == 0 else SCALAR_SHARE
+            nc.scalar.copy(dst[:, :split], src[:, :split])
             if split < P:
                 nc.vector.tensor_copy(
                     dst[:, split:].rearrange("p m j t -> p m t j"), src[:, split:].rearrange("p m j t -> p m t j")
                 )
+            w1_grouped[(b, a)] = grouped
+
+        def quantize_w1(b, a):
             codes = keep.tile([P, PASS], U32, name=f"w1_codes{b}{a}", align_bytes=64)
             sc = keep.tile([P, PASS], U8, name=f"w1_sc{b}{a}", align_bytes=64)
-            nc.vector.quantize_mx(out=codes[:].bitcast(FP8X4), scales=sc[:], in_=grouped[:])
+            nc.vector.quantize_mx(out=codes[:].bitcast(FP8X4), scales=sc[:], in_=w1_grouped[(b, a)][:])
             w1_codes[(b, a)], w1_sc[(b, a)] = codes, sc
 
         banks = {}
@@ -115,59 +119,52 @@ def tile_list_junction_desk_kernel(
                     stop=(a == K_PASSES - 1 and t == PACK - 1),
                 )
 
-        acts, runs, h_tiles, h_codes, h_sc = {}, {}, {}, {}, {}
+        def second_half(c):
+            for a in range(K_PASSES):
+                for u in (2 * c, 2 * c + 1):
+                    first_product(1, a, u)
 
-        def span(c):
-            return UNIT * CHUNK_UNITS[c][0], UNIT * (CHUNK_UNITS[c][-1] + 1)
+        acts, h_tiles, h_codes, h_sc = {}, {}, {}, {}
 
-        def silu(b, c, tag=None):
-            lo, hi = span(c)
-            on_vector = (b, c) in VECTOR_GAINS
-            shape = [P, hi - lo, PACK] if on_vector else [P, PACK, hi - lo]
-            if tag:
-                act = ring.tile(shape, F32, name="act", tag=tag, bufs=1, align_bytes=64)
-            elif b == 0:
+        def silu(b, c, tag="act"):
+            on_vector = c < VECTOR_GAIN_CHUNKS
+            shape = [P, CHUNK, PACK] if on_vector else [P, PACK, CHUNK]
+            if b == 0:
                 act = keep.tile(shape, F32, name=f"act0{c}", align_bytes=64)
             else:
-                act = ring.tile(shape, F32, name="act", bufs=2, align_bytes=64)
-            for u in CHUNK_UNITS[c]:
-                cols = slice(UNIT * u - lo, UNIT * (u + 1) - lo)
+                act = slot_tile(shape, F32, "act", tag)
+            for i in range(CHUNK // UNIT):
+                bank = banks[(b, 2 * c + i)]
+                cols = slice(UNIT * i, UNIT * (i + 1))
                 if on_vector:
-                    nc.scalar.activation(act[:, cols, :], banks[(b, u)][:].rearrange("p t e -> p e t"), ACT.Silu)
+                    nc.scalar.activation(act[:, cols, :], bank[:].rearrange("p t e -> p e t"), ACT.Silu)
                 else:
-                    nc.scalar.activation(act[:, :, cols], banks[(b, u)][:], ACT.Silu)
+                    nc.scalar.activation(act[:, :, cols], bank[:], ACT.Silu)
             acts[(b, c)] = act
 
-        def h_tile(b, c, tag):
-            lo, hi = span(c)
-            h_tiles[(b, c)] = ring.tile([P, hi - lo, PACK], BF16, name="h_bf", tag=tag, bufs=1, align_bytes=64)
-            return h_tiles[(b, c)]
-
         def gain_on_vector(b, c, tag):
-            lo, hi = span(c)
-            factors = gain_sb[:, b : b + 1, :].to_broadcast([P, hi - lo, PACK])
-            nc.vector.tensor_tensor(h_tile(b, c, tag)[:], acts[(b, c)][:], factors, MULT)
+            h_tiles[(b, c)] = slot_tile([P, CHUNK, PACK], BF16, "h_bf", tag)
+            factors = gain_sb[:, b : b + 1, :].to_broadcast([P, CHUNK, PACK])
+            nc.vector.tensor_tensor(h_tiles[(b, c)][:], acts[(b, c)][:], factors, MULT)
 
-        def gain_on_scalar(passes, c, tags):
-            lo, hi = span(c)
-            rows = ring.tile([P, len(passes), PACK, hi - lo], BF16, name="runs", bufs=1, align_bytes=64)
-            for i, b in enumerate(passes):
+        def gain_on_scalar(c):
+            runs = slot_tile([P, R_PASSES, PACK, CHUNK], BF16, "runs", "runs")
+            for b in range(R_PASSES):
                 for t in range(PACK):
                     factor = gain_sb[:, b, t : t + 1]
-                    nc.scalar.activation(rows[:, i, t, :], acts[(b, c)][:, t, :], ACT.Copy, scale=factor)
-            tiles = [h_tile(b, c, tag) for b, tag in zip(passes, tags)]
-            half = (hi - lo) // 2
-            for k in (0, half):
-                for i in range(len(passes)):
+                    nc.scalar.activation(runs[:, b, t, :], acts[(b, c)][:, t, :], ACT.Copy, scale=factor)
+            for b, tag in enumerate((f"shared{c}", f"second{c}")):
+                h_tiles[(b, c)] = slot_tile([P, CHUNK, PACK], BF16, "h_bf", tag)
+            for lo in range(0, CHUNK, UNIT):
+                for b in range(R_PASSES):
                     nc.scalar.copy(
-                        tiles[i][:, k : k + half, :].rearrange("p (x i) t -> p x t i", i=4),
-                        rows[:, i, :, k : k + half].rearrange("p t (x i) -> p x t i", i=4),
+                        h_tiles[(b, c)][:, lo : lo + UNIT, :].rearrange("p (x i) t -> p x t i", i=4),
+                        runs[:, b, :, lo : lo + UNIT].rearrange("p t (x i) -> p x t i", i=4),
                     )
 
         def quantize_h(b, c):
-            lo, hi = span(c)
-            h_codes[(b, c)] = keep.tile([P, hi - lo], U32, name=f"h_codes{b}{c}", align_bytes=64)
-            h_sc[(b, c)] = keep.tile([P, hi - lo], U8, name=f"h_sc{b}{c}", align_bytes=64)
+            h_codes[(b, c)] = keep.tile([P, CHUNK], U32, name=f"h_codes{b}{c}", align_bytes=64)
+            h_sc[(b, c)] = keep.tile([P, CHUNK], U8, name=f"h_sc{b}{c}", align_bytes=64)
             nc.vector.quantize_mx(
                 out=h_codes[(b, c)][:].bitcast(FP8X4),
                 scales=h_sc[(b, c)][:],
@@ -181,11 +178,14 @@ def tile_list_junction_desk_kernel(
         load_w1(0, 1)
         load_w1(0, 2)
         load_tab(2)
+        load_w1(1, 0)
         nc.sync.dma_start(out=gain_sb[:], in_=gain.rearrange("(b p t) -> p b t", b=R_PASSES, t=PACK))
-        for a in range(K_PASSES):
+        for a in range(1, K_PASSES):
             load_w1(1, a)
+
         nc.vector.tensor_copy(v_sc[:], tab_sc[:].indirect(idx[:]))
         for a in range(K_PASSES):
+            cast_w1(0, a)
             quantize_w1(0, a)
             width = S if a < K_PASSES - 1 else S // 2
             for lo in range(0, S, width):
@@ -194,30 +194,29 @@ def tile_list_junction_desk_kernel(
             for u in range(S // UNIT):
                 first_product(0, a, u)
 
-        w3_both = ring.tile([P, R_PASSES, PACK, N], F32, name="w3_both", tag="tab0", bufs=1, align_bytes=64)
-        w3_raw = [w3_both[:, b] for b in range(R_PASSES)]
+        w3_raw = slot_tile([P, R_PASSES, PACK, N], F32, "w3_both", "tab0")
         for b in range(R_PASSES):
-            nc.sync.dma_start(out=w3_raw[b], in_=w3[PASS * b : PASS * (b + 1), :].rearrange("(p j) n -> p j n", j=PACK))
+            rows3 = w3[PASS * b : PASS * (b + 1), :]
+            nc.sync.dma_start(out=w3_raw[:, b], in_=rows3.rearrange("(p j) n -> p j n", j=PACK))
         nc.sync.dma_start(out=w2_codes[:].bitcast(I32), in_=w2_words.rearrange("b p c -> p b c").bitcast(I32))
         nc.sync.dma_start(idx2[:], offs2)
-        wgo_sb = {}
-        for chunks in ([0, 1], list(range(2, CHUNKS))):
-            lo, hi = span(chunks[0])[0], span(chunks[-1])[1]
-            part = keep.tile([P, hi - lo], F32, name=f"wgo{chunks[0]}")
-            nc.sync.dma_start(out=part[:], in_=wgo[:, lo:hi])
-            for c in chunks:
-                wgo_sb[c] = part[:, span(c)[0] - lo : span(c)[1] - lo]
+        wgo_first = keep.tile([P, CHUNK], F32, name="wgo0")
+        nc.sync.dma_start(out=wgo_first[:], in_=wgo[:, :CHUNK])
+        wgo_rest = keep.tile([P, S - CHUNK], F32, name="wgo1")
+        nc.sync.dma_start(out=wgo_rest[:], in_=wgo[:, CHUNK:])
+        wgo_sb = [wgo_first[:, :]] + [wgo_rest[:, CHUNK * c : CHUNK * (c + 1)] for c in range(CHUNKS - 1)]
 
         w3_codes, w3_sc = {}, {}
 
         def quantize_w3(passes, tiles_n, cast, tag):
             width = P * len(tiles_n)
-            grouped3 = ring.tile([P, len(passes), width, PACK], BF16, name="w3_grouped", tag=tag, bufs=1, align_bytes=64)
+            grouped3 = slot_tile([P, len(passes), width, PACK], BF16, "w3_grouped", tag)
             for i, b in enumerate(passes):
-                cast(
-                    grouped3[:, i].rearrange("p (x i) j -> p x j i", i=4),
-                    w3_raw[b][:, :, P * tiles_n[0] : P * tiles_n[0] + width].rearrange("p j (x i) -> p x j i", i=4),
-                )
+                for k, n in enumerate(tiles_n):
+                    cast(
+                        grouped3[:, i, P * k : P * (k + 1)].rearrange("p (x i) j -> p x j i", i=4),
+                        w3_raw[:, b, :, P * n : P * (n + 1)].rearrange("p j (x i) -> p x j i", i=4),
+                    )
             codes = keep.tile([P, len(passes) * width], U32, name=f"w3_codes_{tag}", align_bytes=64)
             sc = keep.tile([P, len(passes) * width], U8, name=f"w3_sc_{tag}", align_bytes=64)
             nc.vector.quantize_mx(
@@ -231,8 +230,8 @@ def tile_list_junction_desk_kernel(
         pages = [keep.tile([P, S], F32, name=f"page{n}") for n in range(N_TILES)]
 
         def product_w2(dst, c, n):
-            for i in range(len(CHUNK_UNITS[c])):
-                cols = slice(UNIT * i, UNIT * (i + 1))
+            for lo in range(0, CHUNK, UNIT):
+                cols = slice(lo, lo + UNIT)
                 for b in range(R_PASSES):
                     nc.tensor.matmul_mx(
                         out=dst[:, cols],
@@ -257,7 +256,7 @@ def tile_list_junction_desk_kernel(
                 )
 
         used_banks = []
-        sums, ys = {}, {}
+        d_ps, e_ps, d_sb, ys = {}, {}, {}, {}
 
         def score_bank(shape):
             number = SCORE_BANKS[len(used_banks)]
@@ -265,127 +264,110 @@ def tile_list_junction_desk_kernel(
             return psum.tile(shape, F32, name=f"bank{number}")
 
         def products(c, tiles_n):
-            lo, hi = span(c)
-            count = len(tiles_n)
-            if 2 * count * (hi - lo) <= BANK:
-                both = score_bank([P, 2, count, hi - lo])
-                d_ps, e_ps = both[:, 0], both[:, 1]
+            key = (c, tiles_n[0])
+            if len(tiles_n) == 1:
+                both = score_bank([P, 2, 1, CHUNK])
+                d_ps[key], e_ps[key] = both[:, 0], both[:, 1]
             else:
-                d_ps = score_bank([P, count, hi - lo])[:]
-                e_ps = score_bank([P, count, hi - lo])[:]
+                d_ps[key] = score_bank([P, len(tiles_n), CHUNK])[:]
+                e_ps[key] = score_bank([P, len(tiles_n), CHUNK])[:]
             for i, n in enumerate(tiles_n):
-                product_w2(d_ps[:, i, :], c, n)
+                product_w2(d_ps[key][:, i, :], c, n)
             for i, n in enumerate(tiles_n):
-                product_w3(e_ps[:, i, :], c, n)
-            sums[(c, tiles_n[0])] = (d_ps, e_ps)
+                product_w3(e_ps[key][:, i, :], c, n)
 
-        def copy_d(c, tiles_n):
-            lo, hi = span(c)
-            d_ps, e_ps = sums[(c, tiles_n[0])]
-            d_sb = ring.tile([P, len(tiles_n), hi - lo], F32, name="d_sb", bufs=3)
-            nc.scalar.copy(d_sb[:], d_ps)
-            sums[(c, tiles_n[0])] = (d_sb, e_ps)
-
-        def multiply(c, tiles_n, tag=None):
-            lo, hi = span(c)
-            shape = [P, len(tiles_n), hi - lo]
+        def copy_d(c, tiles_n, tag=None):
+            key = (c, tiles_n[0])
             if tag:
-                y = ring.tile(shape, F32, name="y", tag=tag, bufs=1, align_bytes=64)
+                d_sb[key] = slot_tile([P, len(tiles_n), CHUNK], F32, "d_sb", tag)
             else:
-                y = ring.tile(shape, F32, name="y", bufs=2, align_bytes=64)
-            d_sb, e_ps = sums[(c, tiles_n[0])]
+                d_sb[key] = ring.tile([P, len(tiles_n), CHUNK], F32, name="d_sb", bufs=3)
+            nc.scalar.copy(d_sb[key][:], d_ps[key])
+
+        def multiply(c, tiles_n, tag=None, apart=False):
+            key = (c, tiles_n[0])
+            if tag:
+                y = slot_tile([P, len(tiles_n), CHUNK], F32, "y", tag)
+            else:
+                y = ring.tile([P, len(tiles_n), CHUNK], F32, name="y", bufs=2, align_bytes=64)
+            if apart:
+                for i in range(len(tiles_n)):
+                    nc.vector.tensor_tensor(y[:, i, :], e_ps[key][:, i, :], d_sb[key][:, i, :], MULT)
+            else:
+                nc.vector.tensor_tensor(y[:], e_ps[key], d_sb[key][:], MULT)
             for i, n in enumerate(tiles_n):
-                nc.vector.tensor_tensor(y[:, i, :], e_ps[:, i, :], d_sb[:, i, :], MULT)
                 ys[(c, n)] = y[:, i, :]
 
         def place(c, tiles_n):
-            lo, hi = span(c)
-            places = idx2[:, lo // LIST_ROWS : hi // LIST_ROWS]
+            places = idx2[:, CHUNK * c // LIST_ROWS : CHUNK * (c + 1) // LIST_ROWS]
             for n in tiles_n:
                 nc.vector.tensor_tensor(pages[n][:].indirect(places), ys[(c, n)], wgo_sb[c], MULT)
 
-        def second_half(a, chunks):
-            for c in chunks:
-                for u in CHUNK_UNITS[c]:
-                    first_product(1, a, u)
+        cast_w1(1, 0)
+        silu(0, 0)
+        quantize_w1(1, 0)
+        gain_on_vector(0, 0, "second3")
+        cast_w1(1, 1)
+        quantize_h(0, 0)
+        quantize_w1(1, 1)
+        cast_w1(1, 2)
+        quantize_w1(1, 2)
 
-        def finish(n, pieces):
-            width = S // pieces
+        x0_sb = []
+        for n in range(N_TILES):
+            x0_n = ring.tile([P, S], F32, name="x0_n", tag="stage", bufs=STAGE_SLOTS)
+            nc.sync.dma_start(out=x0_n[:], in_=x0[P * n : P * (n + 1), :])
+            x0_sb.append(x0_n)
+
+        second_half(0)
+        silu(1, 0, "after_gain")
+        gain_on_vector(1, 0, "shared1")
+        quantize_h(1, 0)
+        quantize_w3([0, 1], [0], nc.vector.tensor_copy, "w3_first")
+        products(0, [0])
+        copy_d(0, [0], "runs")
+        multiply(0, [0])
+        place(0, [0])
+
+        silu(0, 1)
+        gain_on_vector(0, 1, "after_w1")
+        quantize_h(0, 1)
+        quantize_w3([0], [1, 2], nc.scalar.copy, "w3_second")
+        quantize_w3([1], [1, 2], nc.scalar.copy, "after_gain")
+        for c in range(VECTOR_GAIN_CHUNKS, CHUNKS):
+            silu(0, c)
+        for c in range(1, CHUNKS):
+            second_half(c)
+
+        silu(1, 1, "act_second")
+        products(0, [1, 2])
+        copy_d(0, [1, 2])
+        gain_on_vector(1, 1, "shared1")
+        quantize_h(1, 1)
+        multiply(0, [1, 2], "shared1", apart=True)
+        place(0, [1, 2])
+
+        for c in range(1, CHUNKS):
+            has_next = c + 1 < CHUNKS
+            products(c, [0, 1])
+            products(c, [2])
+            if has_next:
+                silu(1, c + 1)
+                gain_on_scalar(c + 1)
+            copy_d(c, [0, 1])
+            copy_d(c, [2])
+            if has_next:
+                quantize_h(0, c + 1)
+                quantize_h(1, c + 1)
+            multiply(c, [0, 1], f"shared{c + 1}" if has_next else None)
+            multiply(c, [2], f"second{c + 1}" if has_next else None)
+            place(c, [0, 1, 2])
+
+        for n in range(N_TILES):
+            width = S // 2 if n < N_TILES - 1 else S // 4
             for lo in range(0, S, width):
                 cols = slice(lo, lo + width)
                 bounded = ring.tile([P, width], F32, name="bounded", bufs=4)
                 nc.scalar.activation(bounded[:], pages[n][:, cols], ACT.Tanh)
                 nc.vector.tensor_tensor(x0_sb[n][:, cols], x0_sb[n][:, cols], bounded[:], ADD)
                 nc.sync.dma_start(out=out[P * n : P * (n + 1), cols], in_=x0_sb[n][:, cols])
-
-        def load_x0():
-            for n in range(N_TILES):
-                x0_n = ring.tile([P, S], F32, name="x0_n", tag="stage", bufs=STAGE_SLOTS)
-                nc.sync.dma_start(out=x0_n[:], in_=x0[P * n : P * (n + 1), :])
-                x0_sb.append(x0_n)
-
-        x0_sb = []
-        quantize_w1(1, 0)
-        quantize_w1(1, 1)
-        quantize_w1(1, 2)
-        load_x0()
-        silu(0, 0)
-        silu(0, 1)
-        for a in range(K_PASSES):
-            second_half(a, [0, 1])
-        gain_on_vector(0, 0, "h00")
-        quantize_h(0, 0)
-        gain_on_vector(0, 1, "h01")
-        quantize_h(0, 1)
-        silu(1, 0, "after_gain")
-        silu(1, 1)
-        gain_on_vector(1, 0, "shared1")
-        quantize_h(1, 0)
-        quantize_w3([0, 1], [0], nc.vector.tensor_copy, "w3_first")
-        products(0, [0])
-        copy_d(0, [0])
-        multiply(0, [0])
-        place(0, [0])
-        gain_on_vector(1, 1, "shared1")
-        quantize_h(1, 1)
-        products(1, [0])
-        copy_d(1, [0])
-        multiply(1, [0])
-        place(1, [0])
-        silu(0, 2)
-        gain_on_vector(0, 2, "after_w1")
-        quantize_h(0, 2)
-        quantize_w3([0], [1, 2], nc.scalar.copy, "w3_second")
-        quantize_w3([1], [1, 2], nc.scalar.copy, "after_gain")
-        silu(0, 3)
-        silu(0, 4)
-        for c in range(2, CHUNKS):
-            for a in range(K_PASSES):
-                second_half(a, [c])
-        silu(1, 2)
-        for c in (0, 1):
-            products(c, [1, 2])
-            copy_d(c, [1, 2])
-        gain_on_vector(1, 2, "shared2")
-        quantize_h(1, 2)
-        multiply(0, [1, 2])
-        place(0, [1, 2])
-        multiply(1, [1, 2], "shared2")
-        place(1, [1, 2])
-        for c in range(2, CHUNKS):
-            products(c, [0, 1])
-            products(c, [2])
-            if c + 1 < CHUNKS:
-                silu(1, c + 1)
-                gain_on_scalar([0, 1], c + 1, [f"shared{c + 1}", f"second{c + 1}"])
-            copy_d(c, [0, 1])
-            copy_d(c, [2])
-            if c + 1 < CHUNKS:
-                quantize_h(0, c + 1)
-                quantize_h(1, c + 1)
-            multiply(c, [0, 1], f"shared{c + 1}" if c + 1 < CHUNKS else None)
-            multiply(c, [2], f"second{c + 1}" if c + 1 < CHUNKS else None)
-            place(c, [0, 1, 2])
-        finish(0, 2)
-        finish(1, 2)
-        finish(2, 4)

@@ -283,6 +283,9 @@ def tile_list_junction_desk_kernel(
             else:
                 d_sb[key] = ring.tile([P, len(tiles_n), CHUNK], F32, name="d_sb", bufs=3)
             nc.scalar.copy(d_sb[key][:], d_ps[key])
+            if c > 0:
+                for i in range(len(tiles_n)):
+                    nc.gpsimd.tensor_tensor(d_sb[key][:, i, :], d_sb[key][:, i, :], wgo_sb[c], MULT)
 
         def multiply(c, tiles_n, tag=None, apart=False):
             key = (c, tiles_n[0])
@@ -301,7 +304,10 @@ def tile_list_junction_desk_kernel(
         def place(c, tiles_n):
             places = idx2[:, CHUNK * c // LIST_ROWS : CHUNK * (c + 1) // LIST_ROWS]
             for n in tiles_n:
-                nc.vector.tensor_tensor(pages[n][:].indirect(places), ys[(c, n)], wgo_sb[c], MULT)
+                if c > 0:
+                    nc.vector.tensor_copy(pages[n][:].indirect(places), ys[(c, n)])
+                else:
+                    nc.vector.tensor_tensor(pages[n][:].indirect(places), ys[(c, n)], wgo_sb[c], MULT)
 
         cast_w1(1, 0)
         silu(0, 0)
@@ -351,11 +357,11 @@ def tile_list_junction_desk_kernel(
             has_next = c + 1 < CHUNKS
             products(c, [0, 1])
             products(c, [2])
+            copy_d(c, [0, 1])
+            copy_d(c, [2])
             if has_next:
                 silu(1, c + 1)
                 gain_on_scalar(c + 1)
-            copy_d(c, [0, 1])
-            copy_d(c, [2])
             if has_next:
                 quantize_h(0, c + 1)
                 quantize_h(1, c + 1)

@@ -28,10 +28,8 @@ N_TILES = N // P
 UNIT = 128
 CHUNK = 2 * UNIT
 CHUNKS = S // CHUNK
-VECTOR_GAIN_CHUNKS = 2
 SCALAR_SHARE = 44
-STAGE_SLOTS = 6
-SCORE_BANKS = [0, 1, 0, 2, 3, 1, 4, 5, 0, 6, 7, 2]
+EARLY_SHARE = 72
 
 
 def tile_list_junction_desk_kernel(
@@ -41,10 +39,17 @@ def tile_list_junction_desk_kernel(
     with ExitStack() as ctx:
         keep = ctx.enter_context(tc.tile_pool(name="keep", bufs=1))
         ring = ctx.enter_context(tc.tile_pool(name="ring", bufs=1))
+        relay = ctx.enter_context(tc.tile_pool(name="relay", bufs=1))
         psum = ctx.enter_context(tc.psum_pool(name="psum", bufs=1))
 
         def slot_tile(shape, dtype, name, tag):
             return ring.tile(shape, dtype, name=name, tag=tag, bufs=1, align_bytes=64)
+
+        def relay_tile(shape, dtype, name, kib):
+            return relay.tile(shape, dtype, name=name, align_bytes=64, offset=1024 * kib)
+
+        def bank(number, shape):
+            return psum.tile(shape, F32, name=f"bank{number}")
 
         idx = keep.tile([P, S // LIST_ROWS], U16, name="idx")
         idx2 = keep.tile([P, S // LIST_ROWS], U16, name="idx2")
@@ -74,20 +79,28 @@ def tile_list_junction_desk_kernel(
         def load_tab(a):
             nc.sync.dma_start(out=tab[a][:], in_=tab_words[a].rearrange("p t i -> p (t i)").bitcast(I32))
 
+        def load_w1_rows(a):
+            raw = slot_tile([P, PACK, H], F32, "w1_rows", "rows")
+            nc.sync.dma_start(out=raw[:], in_=w1[PASS * a : PASS * (a + 1), :].rearrange("(p j) r -> p j r", j=PACK))
+            for b in range(R_PASSES):
+                w1_raw[(b, a)] = raw[:, :, PASS * b : PASS * (b + 1)]
+
         def load_w1(b, a):
-            raw = ring.tile([P, PACK, PASS], F32, name="w1_raw", tag="stage", bufs=STAGE_SLOTS)
+            if (b, a) == (R_PASSES - 1, K_PASSES - 1):
+                raw = relay_tile([P, PACK, PASS], F32, "w1_raw_last", 10)
+            else:
+                raw = slot_tile([P, PACK, PASS], F32, "w1_raw", f"piece{b}{a}")
             rows = w1[PASS * a : PASS * (a + 1), PASS * b : PASS * (b + 1)]
             nc.sync.dma_start(out=raw[:], in_=rows.rearrange("(p j) r -> p j r", j=PACK))
-            w1_raw[(b, a)] = raw
+            w1_raw[(b, a)] = raw[:]
 
-        def cast_w1(b, a):
+        def cast_w1(b, a, split):
             if (b, a) == (R_PASSES - 1, K_PASSES - 1):
-                grouped = slot_tile([P, PASS * PACK], BF16, "w1_last", "after_w1")
+                grouped = relay_tile([P, PASS * PACK], BF16, "w1_last", 0)
             else:
                 grouped = ring.tile([P, PASS * PACK], BF16, name="w1_grouped", bufs=2, align_bytes=64)
             dst = grouped[:].rearrange("p (t m j) -> p m j t", t=PACK, j=PACK)
-            src = w1_raw[(b, a)][:].rearrange("p j (m t) -> p m j t", t=PACK)
-            split = P if b == 0 else SCALAR_SHARE
+            src = w1_raw[(b, a)].rearrange("p j (m t) -> p m j t", t=PACK)
             nc.scalar.copy(dst[:, :split], src[:, :split])
             if split < P:
                 nc.vector.tensor_copy(
@@ -105,7 +118,7 @@ def tile_list_junction_desk_kernel(
 
         def first_product(b, a, u):
             if a == 0:
-                banks[(b, u)] = psum.tile([P, PACK, UNIT], F32, name=f"bank{u}")
+                banks[(b, u)] = bank(u, [P, PACK, UNIT])
             cols = slice(UNIT * u, UNIT * (u + 1))
             for t in range(PACK):
                 m = slice(P * t, P * (t + 1))
@@ -124,77 +137,80 @@ def tile_list_junction_desk_kernel(
                 for u in (2 * c, 2 * c + 1):
                     first_product(1, a, u)
 
-        acts, h_tiles, h_codes, h_sc = {}, {}, {}, {}
+        h_codes, h_sc = {}, {}
 
-        def silu(b, c, tag="act"):
-            on_vector = c < VECTOR_GAIN_CHUNKS
-            shape = [P, CHUNK, PACK] if on_vector else [P, PACK, CHUNK]
-            if b == 0:
-                act = keep.tile(shape, F32, name=f"act0{c}", align_bytes=64)
-            else:
-                act = slot_tile(shape, F32, "act", tag)
-            for i in range(CHUNK // UNIT):
-                bank = banks[(b, 2 * c + i)]
-                cols = slice(UNIT * i, UNIT * (i + 1))
-                if on_vector:
-                    nc.scalar.activation(act[:, cols, :], bank[:].rearrange("p t e -> p e t"), ACT.Silu)
-                else:
-                    nc.scalar.activation(act[:, :, cols], bank[:], ACT.Silu)
-            acts[(b, c)] = act
+        def silu_woven(b, units, tag=None):
+            shape = [P, UNIT * len(units), PACK]
+            act = slot_tile(shape, F32, "act", tag) if tag else relay_tile(shape, F32, "act_1", 10)
+            for i, u in enumerate(units):
+                sums = banks[(b, u)][:].rearrange("p t e -> p e t")
+                nc.scalar.activation(act[:, UNIT * i : UNIT * (i + 1), :], sums, ACT.Silu)
+            return act
 
-        def gain_on_vector(b, c, tag):
-            h_tiles[(b, c)] = slot_tile([P, CHUNK, PACK], BF16, "h_bf", tag)
+        def silu_in_runs(b, units, tag):
+            act = slot_tile([P, PACK, UNIT * len(units)], F32, "act", tag)
+            for i, u in enumerate(units):
+                nc.scalar.activation(act[:, :, UNIT * i : UNIT * (i + 1)], banks[(b, u)][:], ACT.Silu)
+            return act
+
+        def gain_on_vector(b, act, h_bf):
             factors = gain_sb[:, b : b + 1, :].to_broadcast([P, CHUNK, PACK])
-            nc.vector.tensor_tensor(h_tiles[(b, c)][:], acts[(b, c)][:], factors, MULT)
+            nc.vector.tensor_tensor(h_bf, act[:], factors, MULT)
 
-        def gain_on_scalar(c):
-            runs = slot_tile([P, R_PASSES, PACK, CHUNK], BF16, "runs", "runs")
-            for b in range(R_PASSES):
-                for t in range(PACK):
-                    factor = gain_sb[:, b, t : t + 1]
-                    nc.scalar.activation(runs[:, b, t, :], acts[(b, c)][:, t, :], ACT.Copy, scale=factor)
-            for b, tag in enumerate((f"shared{c}", f"second{c}")):
-                h_tiles[(b, c)] = slot_tile([P, CHUNK, PACK], BF16, "h_bf", tag)
-            for lo in range(0, CHUNK, UNIT):
-                for b in range(R_PASSES):
-                    nc.scalar.copy(
-                        h_tiles[(b, c)][:, lo : lo + UNIT, :].rearrange("p (x i) t -> p x t i", i=4),
-                        runs[:, b, :, lo : lo + UNIT].rearrange("p t (x i) -> p x t i", i=4),
-                    )
+        def gain_on_scalar(b, act, h_bf, tag):
+            width = act.shape[2]
+            runs = slot_tile([P, PACK, width], BF16, "runs", tag)
+            for t in range(PACK):
+                nc.scalar.activation(runs[:, t, :], act[:, t, :], ACT.Copy, scale=gain_sb[:, b, t : t + 1])
+            for lo in range(0, width, UNIT):
+                nc.scalar.copy(
+                    h_bf[:, lo : lo + UNIT, :].rearrange("p (x i) t -> p x t i", i=4),
+                    runs[:, :, lo : lo + UNIT].rearrange("p t (x i) -> p x t i", i=4),
+                )
 
-        def quantize_h(b, c):
-            h_codes[(b, c)] = keep.tile([P, CHUNK], U32, name=f"h_codes{b}{c}", align_bytes=64)
-            h_sc[(b, c)] = keep.tile([P, CHUNK], U8, name=f"h_sc{b}{c}", align_bytes=64)
-            nc.vector.quantize_mx(
-                out=h_codes[(b, c)][:].bitcast(FP8X4),
-                scales=h_sc[(b, c)][:],
-                in_=h_tiles[(b, c)][:].rearrange("p e t -> p (e t)"),
-            )
+        def quantize_h(h_tile, parts, codes=None):
+            width = CHUNK * len(parts)
+            name = f"{parts[0][0]}{parts[0][1]}"
+            if codes is None:
+                codes = keep.tile([P, width], U32, name=f"h_codes{name}", align_bytes=64)
+            sc = keep.tile([P, width], U8, name=f"h_sc{name}", align_bytes=64)
+            nc.vector.quantize_mx(out=codes[:].bitcast(FP8X4), scales=sc[:], in_=flat(h_tile))
+            for i, part in enumerate(parts):
+                cols = slice(CHUNK * i, CHUNK * (i + 1))
+                h_codes[part], h_sc[part] = codes[:, cols], sc[:, cols]
+
+        def flat(h_tile):
+            return h_tile[:].rearrange("p e t -> p (e t)")
 
         load_tab(0)
         nc.sync.dma_start(idx[:], offs)
-        load_w1(0, 0)
+        nc.sync.dma_start(out=gain_sb[:], in_=gain.rearrange("(b p t) -> p b t", b=R_PASSES, t=PACK))
+        load_w1_rows(0)
         load_tab(1)
         load_w1(0, 1)
         load_w1(0, 2)
         load_tab(2)
-        load_w1(1, 0)
-        nc.sync.dma_start(out=gain_sb[:], in_=gain.rearrange("(b p t) -> p b t", b=R_PASSES, t=PACK))
-        for a in range(1, K_PASSES):
-            load_w1(1, a)
+        load_w1(1, 1)
+        load_w1(1, 2)
+
+        gain_row = keep.tile([P, CHUNK, PACK], F32, name="gain_row")
+        nc.vector.tensor_copy(gain_row[:], gain_sb[:, 0:1, :].to_broadcast([P, CHUNK, PACK]))
 
         nc.vector.tensor_copy(v_sc[:], tab_sc[:].indirect(idx[:]))
         for a in range(K_PASSES):
-            cast_w1(0, a)
+            cast_w1(0, a, P)
             quantize_w1(0, a)
-            width = S if a < K_PASSES - 1 else S // 2
-            for lo in range(0, S, width):
-                entries = idx[:, lo // LIST_ROWS : (lo + width) // LIST_ROWS]
-                nc.vector.tensor_copy(v_codes[a][:, lo : lo + width], tab[a][:].bitcast(U32).indirect(entries))
+            cuts = [0, S] if a < K_PASSES - 1 else [0, CHUNK, S]
+            for lo, hi in zip(cuts, cuts[1:]):
+                entries = idx[:, lo // LIST_ROWS : hi // LIST_ROWS]
+                nc.vector.tensor_copy(v_codes[a][:, lo:hi], tab[a][:].bitcast(U32).indirect(entries))
             for u in range(S // UNIT):
                 first_product(0, a, u)
+            if a == 0:
+                cast_w1(1, 0, P)
+                quantize_w1(1, 0)
 
-        w3_raw = slot_tile([P, R_PASSES, PACK, N], F32, "w3_both", "tab0")
+        w3_raw = keep.tile([P, R_PASSES, PACK, N], F32, name="w3_raw")
         for b in range(R_PASSES):
             rows3 = w3[PASS * b : PASS * (b + 1), :]
             nc.sync.dma_start(out=w3_raw[:, b], in_=rows3.rearrange("(p j) n -> p j n", j=PACK))
@@ -202,46 +218,45 @@ def tile_list_junction_desk_kernel(
         nc.sync.dma_start(idx2[:], offs2)
         wgo_first = keep.tile([P, CHUNK], F32, name="wgo0")
         nc.sync.dma_start(out=wgo_first[:], in_=wgo[:, :CHUNK])
-        wgo_rest = keep.tile([P, S - CHUNK], F32, name="wgo1")
+        wgo_rest = slot_tile([P, S - CHUNK], F32, "wgo1", "piece01")
         nc.sync.dma_start(out=wgo_rest[:], in_=wgo[:, CHUNK:])
         wgo_sb = [wgo_first[:, :]] + [wgo_rest[:, CHUNK * c : CHUNK * (c + 1)] for c in range(CHUNKS - 1)]
+        x0_sb = slot_tile([P, N_TILES, S], F32, "x0_sb", f"tab{K_PASSES - 1}")
+        for n in range(N_TILES):
+            nc.sync.dma_start(out=x0_sb[:, n, :], in_=x0[P * n : P * (n + 1), :])
 
         w3_codes, w3_sc = {}, {}
 
-        def quantize_w3(passes, tiles_n, cast, tag):
-            width = P * len(tiles_n)
-            grouped3 = slot_tile([P, len(passes), width, PACK], BF16, "w3_grouped", tag)
-            for i, b in enumerate(passes):
-                for k, n in enumerate(tiles_n):
-                    cast(
-                        grouped3[:, i, P * k : P * (k + 1)].rearrange("p (x i) j -> p x j i", i=4),
-                        w3_raw[:, b, :, P * n : P * (n + 1)].rearrange("p j (x i) -> p x j i", i=4),
-                    )
-            codes = keep.tile([P, len(passes) * width], U32, name=f"w3_codes_{tag}", align_bytes=64)
-            sc = keep.tile([P, len(passes) * width], U8, name=f"w3_sc_{tag}", align_bytes=64)
-            nc.vector.quantize_mx(
-                out=codes[:].bitcast(FP8X4), scales=sc[:], in_=grouped3[:].rearrange("p b x j -> p (b x j)")
+        def cast_w3(dst, b, tiles_n, cast=nc.vector.tensor_copy):
+            cols = slice(P * tiles_n[0], P * (tiles_n[-1] + 1))
+            cast(
+                dst.rearrange("p (x i) j -> p x j i", i=4),
+                w3_raw[:, b, :, cols].rearrange("p j (x i) -> p x j i", i=4),
             )
-            for i, b in enumerate(passes):
-                for k, n in enumerate(tiles_n):
-                    cols = slice(width * i + P * k, width * i + P * (k + 1))
-                    w3_codes[(b, n)], w3_sc[(b, n)] = codes[:, cols], sc[:, cols]
+
+        def quantize_w3(grouped3, parts):
+            width = P * len(parts)
+            name = f"{parts[0][0]}{parts[0][1]}"
+            codes = keep.tile([P, width], U32, name=f"w3_codes{name}", align_bytes=64)
+            sc = keep.tile([P, width], U8, name=f"w3_sc{name}", align_bytes=64)
+            nc.vector.quantize_mx(out=codes[:].bitcast(FP8X4), scales=sc[:], in_=flat(grouped3))
+            for k, part in enumerate(parts):
+                cols = slice(P * k, P * (k + 1))
+                w3_codes[part], w3_sc[part] = codes[:, cols], sc[:, cols]
 
         pages = [keep.tile([P, S], F32, name=f"page{n}") for n in range(N_TILES)]
 
         def product_w2(dst, c, n):
-            for lo in range(0, CHUNK, UNIT):
-                cols = slice(lo, lo + UNIT)
-                for b in range(R_PASSES):
-                    nc.tensor.matmul_mx(
-                        out=dst[:, cols],
-                        lhsT=w2_codes[:, b, 2 * P * n : 2 * P * (n + 1)].bitcast(FP4X4),
-                        lhsT_scale=w2_sc[:, b, P * n : P * (n + 1)],
-                        rhs=h_codes[(b, c)][:, cols].bitcast(FP8X4),
-                        rhs_scale=h_sc[(b, c)][:, cols],
-                        start=(b == 0),
-                        stop=(b == R_PASSES - 1),
-                    )
+            for b in range(R_PASSES):
+                nc.tensor.matmul_mx(
+                    out=dst,
+                    lhsT=w2_codes[:, b, 2 * P * n : 2 * P * (n + 1)].bitcast(FP4X4),
+                    lhsT_scale=w2_sc[:, b, P * n : P * (n + 1)],
+                    rhs=h_codes[(b, c)].bitcast(FP8X4),
+                    rhs_scale=h_sc[(b, c)],
+                    start=(b == 0),
+                    stop=(b == R_PASSES - 1),
+                )
 
         def product_w3(dst, c, n):
             for b in range(R_PASSES):
@@ -249,131 +264,157 @@ def tile_list_junction_desk_kernel(
                     out=dst,
                     lhsT=w3_codes[(b, n)].bitcast(FP8X4),
                     lhsT_scale=w3_sc[(b, n)],
-                    rhs=h_codes[(b, c)][:].bitcast(FP8X4),
-                    rhs_scale=h_sc[(b, c)][:],
+                    rhs=h_codes[(b, c)].bitcast(FP8X4),
+                    rhs_scale=h_sc[(b, c)],
                     start=(b == 0),
                     stop=(b == R_PASSES - 1),
                 )
 
-        used_banks = []
-        d_ps, e_ps, d_sb, ys = {}, {}, {}, {}
+        def products(jobs, d_bank, e_bank):
+            d_ps = bank(d_bank, [P, len(jobs), CHUNK])
+            e_ps = bank(e_bank, [P, len(jobs), CHUNK])
+            for i, (c, n) in enumerate(jobs):
+                product_w2(d_ps[:, i, :], c, n)
+            for i, (c, n) in enumerate(jobs):
+                product_w3(e_ps[:, i, :], c, n)
+            return d_ps, e_ps
 
-        def score_bank(shape):
-            number = SCORE_BANKS[len(used_banks)]
-            used_banks.append(number)
-            return psum.tile(shape, F32, name=f"bank{number}")
+        def weigh_on_vector(d_ps, c):
+            weighted = slot_tile([P, 1, CHUNK], F32, "weighted", "single")
+            nc.vector.tensor_tensor(weighted[:, 0, :], d_ps[:, 0, :], wgo_sb[c], MULT)
+            return weighted
 
-        def products(c, tiles_n):
-            key = (c, tiles_n[0])
-            if len(tiles_n) == 1:
-                both = score_bank([P, 2, 1, CHUNK])
-                d_ps[key], e_ps[key] = both[:, 0], both[:, 1]
-            else:
-                d_ps[key] = score_bank([P, len(tiles_n), CHUNK])[:]
-                e_ps[key] = score_bank([P, len(tiles_n), CHUNK])[:]
-            for i, n in enumerate(tiles_n):
-                product_w2(d_ps[key][:, i, :], c, n)
-            for i, n in enumerate(tiles_n):
-                product_w3(e_ps[key][:, i, :], c, n)
+        def weigh(d_ps, c, d_sb, weighted):
+            count = weighted.shape[1]
+            nc.scalar.copy(d_sb, d_ps)
+            factors = wgo_sb[c].rearrange("p (o e) -> p o e", o=1).to_broadcast([P, count, CHUNK])
+            nc.gpsimd.tensor_tensor(weighted, d_sb, factors, MULT)
 
-        def copy_d(c, tiles_n, tag=None):
-            key = (c, tiles_n[0])
-            if tag:
-                d_sb[key] = slot_tile([P, len(tiles_n), CHUNK], F32, "d_sb", tag)
-            else:
-                d_sb[key] = ring.tile([P, len(tiles_n), CHUNK], F32, name="d_sb", bufs=3)
-            nc.scalar.copy(d_sb[key][:], d_ps[key])
-            if c > 0:
-                for i in range(len(tiles_n)):
-                    nc.gpsimd.tensor_tensor(d_sb[key][:, i, :], d_sb[key][:, i, :], wgo_sb[c], MULT)
+        def multiply(y, e_ps, weighted):
+            nc.vector.tensor_tensor(y, e_ps, weighted, MULT)
 
-        def multiply(c, tiles_n, tag=None, apart=False):
-            key = (c, tiles_n[0])
-            if tag:
-                y = slot_tile([P, len(tiles_n), CHUNK], F32, "y", tag)
-            else:
-                y = ring.tile([P, len(tiles_n), CHUNK], F32, name="y", bufs=2, align_bytes=64)
-            if apart:
-                for i in range(len(tiles_n)):
-                    nc.vector.tensor_tensor(y[:, i, :], e_ps[key][:, i, :], d_sb[key][:, i, :], MULT)
-            else:
-                nc.vector.tensor_tensor(y[:], e_ps[key], d_sb[key][:], MULT)
-            for i, n in enumerate(tiles_n):
-                ys[(c, n)] = y[:, i, :]
+        def place(n, lo, hi, y):
+            nc.vector.tensor_copy(pages[n][:].indirect(idx2[:, lo // LIST_ROWS : hi // LIST_ROWS]), y)
 
-        def place(c, tiles_n):
-            places = idx2[:, CHUNK * c // LIST_ROWS : CHUNK * (c + 1) // LIST_ROWS]
-            for n in tiles_n:
-                if c > 0:
-                    nc.vector.tensor_copy(pages[n][:].indirect(places), ys[(c, n)])
-                else:
-                    nc.vector.tensor_tensor(pages[n][:].indirect(places), ys[(c, n)], wgo_sb[c], MULT)
+        def bound(y):
+            bounded = slot_tile([P, y.shape[1]], F32, "bounded_y", "bounded_y")
+            nc.scalar.activation(bounded[:], y, ACT.Tanh)
+            return bounded[:]
 
-        cast_w1(1, 0)
-        silu(0, 0)
-        quantize_w1(1, 0)
-        gain_on_vector(0, 0, "second3")
-        cast_w1(1, 1)
-        quantize_h(0, 0)
+        def finish_pair(c, e_ps, weighted, y_pair):
+            for i in range(2):
+                multiply(y_pair[:, i, :], e_ps[:, i, :], weighted[:, i, :])
+            place(1, CHUNK * c, CHUNK * (c + 1), y_pair[:, 0, :])
+            place(2, CHUNK * c, CHUNK * (c + 1), bound(y_pair[:, 1, :]))
+
+        def single_products(c, number):
+            both = bank(number, [P, 2, CHUNK])
+            product_w2(both[:, 0, :], c, 0)
+            product_w3(both[:, 1, :], c, 0)
+            return both[:, 0:1, :], both[:, 1:2, :]
+
+        act = silu_woven(0, [0, 1], "act00")
+        cast_w1(1, 1, EARLY_SHARE)
         quantize_w1(1, 1)
-        cast_w1(1, 2)
+        h_early = slot_tile([P, CHUNK, PACK], BF16, "h_bf", "h_early")
+        gain_on_vector(0, act, h_early[:])
+        cast_w1(1, 2, SCALAR_SHARE)
         quantize_w1(1, 2)
 
-        x0_sb = []
-        for n in range(N_TILES):
-            x0_n = ring.tile([P, S], F32, name="x0_n", tag="stage", bufs=STAGE_SLOTS)
-            nc.sync.dma_start(out=x0_n[:], in_=x0[P * n : P * (n + 1), :])
-            x0_sb.append(x0_n)
+        act_next = silu_woven(0, [2, 3])
 
         second_half(0)
-        silu(1, 0, "after_gain")
-        gain_on_vector(1, 0, "shared1")
-        quantize_h(1, 0)
-        quantize_w3([0, 1], [0], nc.vector.tensor_copy, "w3_first")
-        products(0, [0])
-        copy_d(0, [0], "runs")
-        multiply(0, [0])
-        place(0, [0])
+        act = silu_woven(1, [0, 1], "rows")
+        h_first = slot_tile([P, CHUNK, PACK], BF16, "h_bf", "after_h0")
+        gain_on_vector(1, act, h_first[:])
+        w3_first = slot_tile([P, R_PASSES * P, PACK], BF16, "w3_grouped", "w3_first")
+        for b in range(R_PASSES):
+            cast_w3(w3_first[:, P * b : P * (b + 1)], b, [0])
+        quantize_h(h_first, [(1, 0)])
+        quantize_h(h_early, [(0, 0)], relay_tile([P, CHUNK], U32, "h_codes_early", 14))
+        quantize_w3(w3_first, [(0, 0), (1, 0)])
+        d_ps, e_ps = products([(0, 0)], 0, 1)
+        y_first = slot_tile([P, CHUNK], F32, "y", "y_single")
+        multiply(y_first[:], e_ps[:, 0, :], weigh_on_vector(d_ps, 0)[:, 0, :])
+        w3_rest = slot_tile([P, 2 * P, PACK], BF16, "w3_grouped", "w3_second")
+        for n in (1, 2):
+            cast_w3(w3_rest[:, P * (n - 1) : P * n], 0, [n], nc.scalar.copy)
+        quantize_w3(w3_rest, [(0, 1), (0, 2)])
+        w3_rest = slot_tile([P, 2 * P, PACK], BF16, "w3_grouped", "after_h0")
+        cast_w3(w3_rest[:], 1, [1, 2])
+        quantize_w3(w3_rest, [(1, 1), (1, 2)])
+        place(0, 0, CHUNK, y_first[:])
 
-        silu(0, 1)
-        gain_on_vector(0, 1, "after_w1")
-        quantize_h(0, 1)
-        quantize_w3([0], [1, 2], nc.scalar.copy, "w3_second")
-        quantize_w3([1], [1, 2], nc.scalar.copy, "after_gain")
-        for c in range(VECTOR_GAIN_CHUNKS, CHUNKS):
-            silu(0, c)
-        for c in range(1, CHUNKS):
-            second_half(c)
+        second_half(1)
+        act_runs = silu_in_runs(1, [2, 3], "tab0")
+        h_both = relay_tile([P, 2 * CHUNK, PACK], BF16, "h_1", 0)
+        gain_on_vector(0, act_next, h_both[:, :CHUNK])
+        d_ps, e_ps = products([(0, 1), (0, 2)], 2, 3)
+        weighted = slot_tile([P, 2, CHUNK], F32, "weighted", "pair")
+        weigh(d_ps[:], 0, weighted[:], weighted[:])
+        gain_on_scalar(1, act_runs, h_both[:, CHUNK:], "runs_first")
+        quantize_h(h_both, [(0, 1), (1, 1)])
+        finish_pair(0, e_ps, weighted, relay_tile([P, 2, CHUNK], F32, "y_0", 0))
 
-        silu(1, 1, "act_second")
-        products(0, [1, 2])
-        copy_d(0, [1, 2])
-        gain_on_vector(1, 1, "shared1")
-        quantize_h(1, 1)
-        multiply(0, [1, 2], "shared1", apart=True)
-        place(0, [1, 2])
+        h_both = relay_tile([P, 2 * CHUNK, PACK], BF16, "h_2", 2)
+        for i, tag in enumerate(("piece11", "h_early")):
+            act = silu_woven(0, [4 + i], tag)
+            nc.gpsimd.tensor_tensor(h_both[:, UNIT * i : UNIT * (i + 1)], act[:], gain_row[:, :UNIT], MULT)
+        d_one, e_one = single_products(1, 0)
+        d_ps, e_ps = products([(1, 1), (1, 2)], 1, 2)
+        weighted_one = slot_tile([P, 1, CHUNK], F32, "weighted", "single")
+        weigh(d_one, 1, weighted_one[:], weighted_one[:])
+        weighted = slot_tile([P, 2, CHUNK], F32, "weighted", "pair_next")
+        weigh(d_ps[:], 1, slot_tile([P, 2, CHUNK], F32, "d_sb", "codes2")[:], weighted[:])
+        second_half(2)
+        y_first = slot_tile([P, CHUNK], F32, "y", "y_single")
+        multiply(y_first[:], e_one[:, 0, :], weighted_one[:, 0, :])
+        place(0, CHUNK, 2 * CHUNK, y_first[:])
+        gain_on_scalar(1, silu_in_runs(1, [4, 5], "tab0"), h_both[:, CHUNK:], "runs1")
+        quantize_h(h_both, [(0, 2), (1, 2)], slot_tile([P, 2 * CHUNK], U32, "h_codes", "codes2"))
+        finish_pair(1, e_ps, weighted, relay_tile([P, 2, CHUNK], F32, "y_1", 2))
 
-        for c in range(1, CHUNKS):
-            has_next = c + 1 < CHUNKS
-            products(c, [0, 1])
-            products(c, [2])
-            copy_d(c, [0, 1])
-            copy_d(c, [2])
-            if has_next:
-                silu(1, c + 1)
-                gain_on_scalar(c + 1)
-            if has_next:
-                quantize_h(0, c + 1)
-                quantize_h(1, c + 1)
-            multiply(c, [0, 1], f"shared{c + 1}" if has_next else None)
-            multiply(c, [2], f"second{c + 1}" if has_next else None)
-            place(c, [0, 1, 2])
+        h_both = relay_tile([P, 2 * CHUNK, PACK], BF16, "h_3", 4)
+        nc.gpsimd.tensor_tensor(h_both[:, :CHUNK], silu_woven(0, [6, 7], "runs_first")[:], gain_row[:], MULT)
+        d_ps, e_ps = products([(2, 0), (2, 1)], 4, 5)
+        weighted = slot_tile([P, 2, CHUNK], F32, "weighted", "pair")
+        weigh(d_ps[:], 2, slot_tile([P, 2, CHUNK], F32, "d_sb", "codes3")[:], weighted[:])
+        second_half(3)
+        gain_on_scalar(1, silu_in_runs(1, [6, 7], "rows"), h_both[:, CHUNK:], "runs0")
+        quantize_h(h_both, [(0, 3), (1, 3)], slot_tile([P, 2 * CHUNK], U32, "h_codes", "codes3"))
+        y_pair = relay_tile([P, 2, CHUNK], F32, "y_2", 4)
+        for n in range(2):
+            multiply(y_pair[:, n, :], e_ps[:, n, :], weighted[:, n, :])
+        for n in range(2):
+            place(n, 2 * CHUNK, 3 * CHUNK, y_pair[:, n, :])
 
-        for n in range(N_TILES):
-            width = S // 2 if n < N_TILES - 1 else S // 4
-            for lo in range(0, S, width):
-                cols = slice(lo, lo + width)
-                bounded = ring.tile([P, width], F32, name="bounded", bufs=4)
-                nc.scalar.activation(bounded[:], pages[n][:, cols], ACT.Tanh)
-                nc.vector.tensor_tensor(x0_sb[n][:, cols], x0_sb[n][:, cols], bounded[:], ADD)
-                nc.sync.dma_start(out=out[P * n : P * (n + 1), cols], in_=x0_sb[n][:, cols])
+        d_ps, e_ps = products([(3, 0), (3, 1)], 6, 7)
+        weighted = slot_tile([P, 2, CHUNK], F32, "weighted", "pair_next")
+        weigh(d_ps[:], 3, weighted[:], weighted[:])
+        d_both, e_both = products([(2, 2), (3, 2)], 0, 3)
+        d_sb = slot_tile([P, 2 * CHUNK], F32, "d_sb", "d_last")
+        weighted_both = slot_tile([P, 2 * CHUNK], F32, "weighted", "pair")
+        nc.scalar.copy(d_sb[:], d_both[:].rearrange("p c e -> p (c e)"))
+        nc.gpsimd.tensor_tensor(weighted_both[:], d_sb[:], wgo_rest[:, CHUNK:], MULT)
+        y_first = slot_tile([P, CHUNK], F32, "y", "y_single")
+        multiply(y_first[:], e_ps[:, 0, :], weighted[:, 0, :])
+        place(0, 3 * CHUNK, S, y_first[:])
+        y_second = slot_tile([P, CHUNK], F32, "y", "d_last")
+        multiply(y_second[:], e_ps[:, 1, :], weighted[:, 1, :])
+        y_both = slot_tile([P, 2 * CHUNK], F32, "y", "y_both")
+        multiply(y_both[:], e_both[:].rearrange("p c e -> p (c e)"), weighted_both[:])
+        place(1, 3 * CHUNK, S, y_second[:])
+        place(2, 2 * CHUNK, S, bound(y_both[:]))
+
+        half = S // 2
+        for n, lo, tag in ((0, 0, "piece02"), (0, half, "piece11"), (1, 0, "tab0"), (1, half, "tab1")):
+            cols = slice(lo, lo + half)
+            bounded = slot_tile([P, half], F32, "bounded", tag)
+            nc.scalar.activation(bounded[:], pages[n][:, cols], ACT.Tanh)
+            nc.gpsimd.tensor_tensor(x0_sb[:, n, cols], x0_sb[:, n, cols], bounded[:], ADD)
+            nc.sync.dma_start(out=out[P * n : P * (n + 1), cols], in_=x0_sb[:, n, cols])
+        sums = slot_tile([P, S], F32, "sums", "tab1")
+        for lo in range(0, S, S // 4):
+            cols = slice(lo, lo + S // 4)
+            nc.vector.tensor_tensor(sums[:, cols], x0_sb[:, 2, cols], pages[2][:, cols], ADD)
+            nc.sync.dma_start(out=out[2 * P :, cols], in_=sums[:, cols])

@@ -28,8 +28,7 @@ N_TILES = N // P
 UNIT = 128
 CHUNK = 2 * UNIT
 CHUNKS = S // CHUNK
-SCALAR_SHARE = 44
-EARLY_SHARE = 72
+POOL_END = 640
 
 
 def tile_list_junction_desk_kernel(
@@ -46,7 +45,7 @@ def tile_list_junction_desk_kernel(
             return ring.tile(shape, dtype, name=name, tag=tag, bufs=1, align_bytes=64)
 
         def relay_tile(shape, dtype, name, kib):
-            return relay.tile(shape, dtype, name=name, align_bytes=64, offset=1024 * kib)
+            return relay.tile(shape, dtype, name=name, align_bytes=64, offset=int(1024 * kib))
 
         def bank(number, shape):
             return psum.tile(shape, F32, name=f"bank{number}")
@@ -80,32 +79,19 @@ def tile_list_junction_desk_kernel(
             nc.sync.dma_start(out=tab[a][:], in_=tab_words[a].rearrange("p t i -> p (t i)").bitcast(I32))
 
         def load_w1_rows(a):
-            raw = slot_tile([P, PACK, H], F32, "w1_rows", "rows")
+            raw = slot_tile([P, PACK, H], F32, "w1_rows", f"rows{a}")
             nc.sync.dma_start(out=raw[:], in_=w1[PASS * a : PASS * (a + 1), :].rearrange("(p j) r -> p j r", j=PACK))
             for b in range(R_PASSES):
                 w1_raw[(b, a)] = raw[:, :, PASS * b : PASS * (b + 1)]
 
-        def load_w1(b, a):
-            if (b, a) == (R_PASSES - 1, K_PASSES - 1):
-                raw = relay_tile([P, PACK, PASS], F32, "w1_raw_last", 10)
-            else:
-                raw = slot_tile([P, PACK, PASS], F32, "w1_raw", f"piece{b}{a}")
-            rows = w1[PASS * a : PASS * (a + 1), PASS * b : PASS * (b + 1)]
-            nc.sync.dma_start(out=raw[:], in_=rows.rearrange("(p j) r -> p j r", j=PACK))
-            w1_raw[(b, a)] = raw[:]
-
-        def cast_w1(b, a, split):
-            if (b, a) == (R_PASSES - 1, K_PASSES - 1):
-                grouped = relay_tile([P, PASS * PACK], BF16, "w1_last", 0)
-            else:
-                grouped = ring.tile([P, PASS * PACK], BF16, name="w1_grouped", bufs=2, align_bytes=64)
+        def cast_w1(b, a, on_vector):
+            grouped = ring.tile([P, PASS * PACK], BF16, name="w1_grouped", bufs=2, align_bytes=64)
             dst = grouped[:].rearrange("p (t m j) -> p m j t", t=PACK, j=PACK)
             src = w1_raw[(b, a)].rearrange("p j (m t) -> p m j t", t=PACK)
-            nc.scalar.copy(dst[:, :split], src[:, :split])
-            if split < P:
-                nc.vector.tensor_copy(
-                    dst[:, split:].rearrange("p m j t -> p m t j"), src[:, split:].rearrange("p m j t -> p m t j")
-                )
+            if on_vector:
+                nc.vector.tensor_copy(dst.rearrange("p m j t -> p m t j"), src.rearrange("p m j t -> p m t j"))
+            else:
+                nc.scalar.copy(dst, src)
             w1_grouped[(b, a)] = grouped
 
         def quantize_w1(b, a):
@@ -116,9 +102,9 @@ def tile_list_junction_desk_kernel(
 
         banks = {}
 
-        def first_product(b, a, u):
+        def first_product(b, a, u, number):
             if a == 0:
-                banks[(b, u)] = bank(u, [P, PACK, UNIT])
+                banks[(b, u)] = bank(number, [P, PACK, UNIT])
             cols = slice(UNIT * u, UNIT * (u + 1))
             for t in range(PACK):
                 m = slice(P * t, P * (t + 1))
@@ -132,47 +118,52 @@ def tile_list_junction_desk_kernel(
                     stop=(a == K_PASSES - 1 and t == PACK - 1),
                 )
 
-        def second_half(c):
-            for a in range(K_PASSES):
-                for u in (2 * c, 2 * c + 1):
-                    first_product(1, a, u)
+        def chunk_pass(c, a):
+            for b in range(R_PASSES):
+                for i in range(2):
+                    first_product(b, a, 2 * c + i, (4 if c else 0) + 2 * b + i)
+
+        def whole_chunk(c):
+            for b in range(R_PASSES):
+                for i in range(2):
+                    for a in range(K_PASSES):
+                        first_product(b, a, 2 * c + i, 4 + 2 * b + i)
 
         h_codes, h_sc = {}, {}
 
-        def silu_woven(b, units, tag=None):
-            shape = [P, UNIT * len(units), PACK]
-            act = slot_tile(shape, F32, "act", tag) if tag else relay_tile(shape, F32, "act_1", 10)
+        def silu_woven(b, units, act):
             for i, u in enumerate(units):
                 sums = banks[(b, u)][:].rearrange("p t e -> p e t")
                 nc.scalar.activation(act[:, UNIT * i : UNIT * (i + 1), :], sums, ACT.Silu)
             return act
 
-        def silu_in_runs(b, units, tag):
-            act = slot_tile([P, PACK, UNIT * len(units)], F32, "act", tag)
-            for i, u in enumerate(units):
-                nc.scalar.activation(act[:, :, UNIT * i : UNIT * (i + 1)], banks[(b, u)][:], ACT.Silu)
+        def silu_in_runs(c, act):
+            for i in range(CHUNK // UNIT):
+                nc.scalar.activation(act[:, :, UNIT * i : UNIT * (i + 1)], banks[(1, 2 * c + i)][:], ACT.Silu)
             return act
 
         def gain_on_vector(b, act, h_bf):
-            factors = gain_sb[:, b : b + 1, :].to_broadcast([P, CHUNK, PACK])
-            nc.vector.tensor_tensor(h_bf, act[:], factors, MULT)
+            factors = gain_sb[:, b : b + 1, :].to_broadcast([P, UNIT, PACK])
+            for lo in range(0, CHUNK, UNIT):
+                nc.vector.tensor_tensor(h_bf[:, lo : lo + UNIT], act[:, lo : lo + UNIT], factors, MULT)
 
-        def gain_on_scalar(b, act, h_bf, tag):
-            width = act.shape[2]
-            runs = slot_tile([P, PACK, width], BF16, "runs", tag)
+        def gain_in_runs(act, runs):
             for t in range(PACK):
-                nc.scalar.activation(runs[:, t, :], act[:, t, :], ACT.Copy, scale=gain_sb[:, b, t : t + 1])
-            for lo in range(0, width, UNIT):
+                nc.scalar.activation(runs[:, t, :], act[:, t, :], ACT.Copy, scale=gain_sb[:, 1, t : t + 1])
+            return runs
+
+        def weave(h_bf, runs, units=(0, 1)):
+            for i in units:
+                cols = slice(UNIT * i, UNIT * (i + 1))
                 nc.scalar.copy(
-                    h_bf[:, lo : lo + UNIT, :].rearrange("p (x i) t -> p x t i", i=4),
-                    runs[:, :, lo : lo + UNIT].rearrange("p t (x i) -> p x t i", i=4),
+                    h_bf[:, cols, :].rearrange("p (x i) t -> p x t i", i=4),
+                    runs[:, :, cols].rearrange("p t (x i) -> p x t i", i=4),
                 )
 
-        def quantize_h(h_tile, parts, codes=None):
+        def quantize_h(h_tile, parts):
             width = CHUNK * len(parts)
             name = f"{parts[0][0]}{parts[0][1]}"
-            if codes is None:
-                codes = keep.tile([P, width], U32, name=f"h_codes{name}", align_bytes=64)
+            codes = keep.tile([P, width], U32, name=f"h_codes{name}", align_bytes=64)
             sc = keep.tile([P, width], U8, name=f"h_sc{name}", align_bytes=64)
             nc.vector.quantize_mx(out=codes[:].bitcast(FP8X4), scales=sc[:], in_=flat(h_tile))
             for i, part in enumerate(parts):
@@ -187,28 +178,24 @@ def tile_list_junction_desk_kernel(
         nc.sync.dma_start(out=gain_sb[:], in_=gain.rearrange("(b p t) -> p b t", b=R_PASSES, t=PACK))
         load_w1_rows(0)
         load_tab(1)
-        load_w1(0, 1)
-        load_w1(0, 2)
+        load_w1_rows(1)
+        load_w1_rows(2)
         load_tab(2)
-        load_w1(1, 1)
-        load_w1(1, 2)
 
         gain_row = keep.tile([P, CHUNK, PACK], F32, name="gain_row")
         nc.vector.tensor_copy(gain_row[:], gain_sb[:, 0:1, :].to_broadcast([P, CHUNK, PACK]))
 
         nc.vector.tensor_copy(v_sc[:], tab_sc[:].indirect(idx[:]))
         for a in range(K_PASSES):
-            cast_w1(0, a, P)
-            quantize_w1(0, a)
-            cuts = [0, S] if a < K_PASSES - 1 else [0, CHUNK, S]
+            for b in range(R_PASSES):
+                cast_w1(b, a, on_vector=(b == 1))
+                quantize_w1(b, a)
+            cuts = [0, S] if a < K_PASSES - 1 else [0, CHUNK, 2 * CHUNK, S]
             for lo, hi in zip(cuts, cuts[1:]):
                 entries = idx[:, lo // LIST_ROWS : hi // LIST_ROWS]
                 nc.vector.tensor_copy(v_codes[a][:, lo:hi], tab[a][:].bitcast(U32).indirect(entries))
-            for u in range(S // UNIT):
-                first_product(0, a, u)
-            if a == 0:
-                cast_w1(1, 0, P)
-                quantize_w1(1, 0)
+            for c in range(2):
+                chunk_pass(c, a)
 
         w3_raw = keep.tile([P, R_PASSES, PACK, N], F32, name="w3_raw")
         for b in range(R_PASSES):
@@ -218,7 +205,7 @@ def tile_list_junction_desk_kernel(
         nc.sync.dma_start(idx2[:], offs2)
         wgo_first = keep.tile([P, CHUNK], F32, name="wgo0")
         nc.sync.dma_start(out=wgo_first[:], in_=wgo[:, :CHUNK])
-        wgo_rest = slot_tile([P, S - CHUNK], F32, "wgo1", "piece01")
+        wgo_rest = slot_tile([P, S - CHUNK], F32, "wgo1", "tab0")
         nc.sync.dma_start(out=wgo_rest[:], in_=wgo[:, CHUNK:])
         wgo_sb = [wgo_first[:, :]] + [wgo_rest[:, CHUNK * c : CHUNK * (c + 1)] for c in range(CHUNKS - 1)]
         x0_sb = slot_tile([P, N_TILES, S], F32, "x0_sb", f"tab{K_PASSES - 1}")
@@ -246,37 +233,31 @@ def tile_list_junction_desk_kernel(
 
         pages = [keep.tile([P, S], F32, name=f"page{n}") for n in range(N_TILES)]
 
-        def product_w2(dst, c, n):
+        def sums(dst, jobs, weights):
             for b in range(R_PASSES):
-                nc.tensor.matmul_mx(
-                    out=dst,
-                    lhsT=w2_codes[:, b, 2 * P * n : 2 * P * (n + 1)].bitcast(FP4X4),
-                    lhsT_scale=w2_sc[:, b, P * n : P * (n + 1)],
-                    rhs=h_codes[(b, c)].bitcast(FP8X4),
-                    rhs_scale=h_sc[(b, c)],
-                    start=(b == 0),
-                    stop=(b == R_PASSES - 1),
-                )
+                for i, (c, n) in enumerate(jobs):
+                    codes, scales = weights(b, n)
+                    nc.tensor.matmul_mx(
+                        out=dst[:, i, :],
+                        lhsT=codes,
+                        lhsT_scale=scales,
+                        rhs=h_codes[(b, c)].bitcast(FP8X4),
+                        rhs_scale=h_sc[(b, c)],
+                        start=(b == 0 and i == 0),
+                        stop=(b == R_PASSES - 1 and i == len(jobs) - 1),
+                    )
 
-        def product_w3(dst, c, n):
-            for b in range(R_PASSES):
-                nc.tensor.matmul_mx(
-                    out=dst,
-                    lhsT=w3_codes[(b, n)].bitcast(FP8X4),
-                    lhsT_scale=w3_sc[(b, n)],
-                    rhs=h_codes[(b, c)].bitcast(FP8X4),
-                    rhs_scale=h_sc[(b, c)],
-                    start=(b == 0),
-                    stop=(b == R_PASSES - 1),
-                )
+        def w2_of(b, n):
+            return w2_codes[:, b, 2 * P * n : 2 * P * (n + 1)].bitcast(FP4X4), w2_sc[:, b, P * n : P * (n + 1)]
+
+        def w3_of(b, n):
+            return w3_codes[(b, n)].bitcast(FP8X4), w3_sc[(b, n)]
 
         def products(jobs, d_bank, e_bank):
             d_ps = bank(d_bank, [P, len(jobs), CHUNK])
             e_ps = bank(e_bank, [P, len(jobs), CHUNK])
-            for i, (c, n) in enumerate(jobs):
-                product_w2(d_ps[:, i, :], c, n)
-            for i, (c, n) in enumerate(jobs):
-                product_w3(e_ps[:, i, :], c, n)
+            sums(d_ps, jobs, w2_of)
+            sums(e_ps, jobs, w3_of)
             return d_ps, e_ps
 
         def weigh_on_vector(d_ps, c):
@@ -296,125 +277,136 @@ def tile_list_junction_desk_kernel(
         def place(n, lo, hi, y):
             nc.vector.tensor_copy(pages[n][:].indirect(idx2[:, lo // LIST_ROWS : hi // LIST_ROWS]), y)
 
-        def bound(y):
-            bounded = slot_tile([P, y.shape[1]], F32, "bounded_y", "bounded_y")
+        def bound(y, bounded):
             nc.scalar.activation(bounded[:], y, ACT.Tanh)
             return bounded[:]
 
-        def finish_pair(c, e_ps, weighted, y_pair):
+        def finish_pair(c, e_ps, weighted, y_pair, bounded):
             for i in range(2):
                 multiply(y_pair[:, i, :], e_ps[:, i, :], weighted[:, i, :])
             place(1, CHUNK * c, CHUNK * (c + 1), y_pair[:, 0, :])
-            place(2, CHUNK * c, CHUNK * (c + 1), bound(y_pair[:, 1, :]))
+            place(2, CHUNK * c, CHUNK * (c + 1), bound(y_pair[:, 1, :], bounded))
 
         def single_products(c, number):
             both = bank(number, [P, 2, CHUNK])
-            product_w2(both[:, 0, :], c, 0)
-            product_w3(both[:, 1, :], c, 0)
+            sums(both[:, 0:1, :], [(c, 0)], w2_of)
+            sums(both[:, 1:2, :], [(c, 0)], w3_of)
             return both[:, 0:1, :], both[:, 1:2, :]
 
-        act = silu_woven(0, [0, 1], "act00")
-        cast_w1(1, 1, EARLY_SHARE)
-        quantize_w1(1, 1)
-        h_early = slot_tile([P, CHUNK, PACK], BF16, "h_bf", "h_early")
-        gain_on_vector(0, act, h_early[:])
-        cast_w1(1, 2, SCALAR_SHARE)
-        quantize_w1(1, 2)
-
-        act_next = silu_woven(0, [2, 3])
-
-        second_half(0)
-        act = silu_woven(1, [0, 1], "rows")
-        h_first = slot_tile([P, CHUNK, PACK], BF16, "h_bf", "after_h0")
-        gain_on_vector(1, act, h_first[:])
+        h_first = slot_tile([P, 2 * CHUNK, PACK], BF16, "h_bf", "h_first")
+        act_tiles = [relay_tile([P, CHUNK, PACK], F32, "act_0", 32), relay_tile([P, CHUNK, PACK], F32, "act_10", 24)]
+        for b, act in enumerate(act_tiles):
+            silu_woven(b, [0, 1], act)
+            gain_on_vector(b, act, h_first[:, CHUNK * b : CHUNK * (b + 1)])
         w3_first = slot_tile([P, R_PASSES * P, PACK], BF16, "w3_grouped", "w3_first")
         for b in range(R_PASSES):
             cast_w3(w3_first[:, P * b : P * (b + 1)], b, [0])
-        quantize_h(h_first, [(1, 0)])
-        quantize_h(h_early, [(0, 0)], relay_tile([P, CHUNK], U32, "h_codes_early", 14))
+        quantize_h(h_first, [(0, 0), (1, 0)])
         quantize_w3(w3_first, [(0, 0), (1, 0)])
+        act_next = silu_woven(0, [2, 3], relay_tile([P, CHUNK, PACK], F32, "act_1", 10))
         d_ps, e_ps = products([(0, 0)], 0, 1)
         y_first = slot_tile([P, CHUNK], F32, "y", "y_single")
-        multiply(y_first[:], e_ps[:, 0, :], weigh_on_vector(d_ps, 0)[:, 0, :])
-        w3_rest = slot_tile([P, 2 * P, PACK], BF16, "w3_grouped", "w3_second")
+        weighted_one = weigh_on_vector(d_ps, 0)
+        w3_rest = relay_tile([P, 2 * P, PACK], BF16, "w3_second", 32)
         for n in (1, 2):
             cast_w3(w3_rest[:, P * (n - 1) : P * n], 0, [n], nc.scalar.copy)
         quantize_w3(w3_rest, [(0, 1), (0, 2)])
-        w3_rest = slot_tile([P, 2 * P, PACK], BF16, "w3_grouped", "after_h0")
-        cast_w3(w3_rest[:], 1, [1, 2])
+        w3_rest = relay_tile([P, 2 * P, PACK], BF16, "w3_rest", 27)
+        for n in (1, 2):
+            cast_w3(w3_rest[:, P * (n - 1) : P * n], 1, [n])
         quantize_w3(w3_rest, [(1, 1), (1, 2)])
-        place(0, 0, CHUNK, y_first[:])
-
-        second_half(1)
-        act_runs = silu_in_runs(1, [2, 3], "tab0")
-        h_both = relay_tile([P, 2 * CHUNK, PACK], BF16, "h_1", 0)
-        gain_on_vector(0, act_next, h_both[:, :CHUNK])
+        multiply(y_first[:], e_ps[:, 0, :], weighted_one[:, 0, :])
         d_ps, e_ps = products([(0, 1), (0, 2)], 2, 3)
         weighted = slot_tile([P, 2, CHUNK], F32, "weighted", "pair")
-        weigh(d_ps[:], 0, weighted[:], weighted[:])
-        gain_on_scalar(1, act_runs, h_both[:, CHUNK:], "runs_first")
-        quantize_h(h_both, [(0, 1), (1, 1)])
-        finish_pair(0, e_ps, weighted, relay_tile([P, 2, CHUNK], F32, "y_0", 0))
+        for i in range(2):
+            nc.vector.tensor_tensor(weighted[:, i, :], d_ps[:, i, :], wgo_sb[0], MULT)
+        place(0, 0, CHUNK, y_first[:])
 
-        h_both = relay_tile([P, 2 * CHUNK, PACK], BF16, "h_2", 2)
-        for i, tag in enumerate(("piece11", "h_early")):
-            act = silu_woven(0, [4 + i], tag)
-            nc.gpsimd.tensor_tensor(h_both[:, UNIT * i : UNIT * (i + 1)], act[:], gain_row[:, :UNIT], MULT)
+        act_runs = silu_in_runs(1, slot_tile([P, PACK, CHUNK], F32, "act", "rows0"))
+        h_both = relay_tile([P, 2 * CHUNK, PACK], BF16, "h_1", 28.5)
+        nc.gpsimd.tensor_tensor(h_both[:, :CHUNK], act_next[:], gain_row[:], MULT)
+        weave(h_both[:, CHUNK:], gain_in_runs(act_runs, relay_tile([P, PACK, CHUNK], BF16, "runs_1", 1)))
+        quantize_h(h_both, [(0, 1), (1, 1)])
+
+        h_both = relay_tile([P, 2 * CHUNK, PACK], BF16, "h_2", 25)
+        whole_chunk(2)
+        act = silu_woven(0, [4, 5], relay_tile([P, CHUNK, PACK], F32, "act_2", 2))
+        nc.gpsimd.tensor_tensor(h_both[:, :CHUNK], act[:], gain_row[:], MULT)
+        act_runs = silu_in_runs(2, slot_tile([P, PACK, CHUNK], F32, "act", "rows0"))
+        runs = gain_in_runs(act_runs, relay_tile([P, PACK, CHUNK], BF16, "runs_2", 18))
+        y_pair = relay_tile([P, 2, CHUNK], F32, "y_0", 0)
+        finish_pair(0, e_ps, weighted, y_pair, slot_tile([P, CHUNK], F32, "bounded", "bounded_y"))
         d_one, e_one = single_products(1, 0)
         d_ps, e_ps = products([(1, 1), (1, 2)], 1, 2)
-        weighted_one = slot_tile([P, 1, CHUNK], F32, "weighted", "single")
-        weigh(d_one, 1, weighted_one[:], weighted_one[:])
-        weighted = slot_tile([P, 2, CHUNK], F32, "weighted", "pair_next")
-        weigh(d_ps[:], 1, slot_tile([P, 2, CHUNK], F32, "d_sb", "codes2")[:], weighted[:])
-        second_half(2)
+        weighted_one = weigh_on_vector(d_one, 1)
         y_first = slot_tile([P, CHUNK], F32, "y", "y_single")
         multiply(y_first[:], e_one[:, 0, :], weighted_one[:, 0, :])
         place(0, CHUNK, 2 * CHUNK, y_first[:])
-        gain_on_scalar(1, silu_in_runs(1, [4, 5], "tab0"), h_both[:, CHUNK:], "runs1")
-        quantize_h(h_both, [(0, 2), (1, 2)], slot_tile([P, 2 * CHUNK], U32, "h_codes", "codes2"))
-        finish_pair(1, e_ps, weighted, relay_tile([P, 2, CHUNK], F32, "y_1", 2))
+        whole_chunk(3)
+        act = silu_woven(0, [6, 7], slot_tile([P, CHUNK, PACK], F32, "act", "rows0"))
+        weighted = slot_tile([P, 2, CHUNK], F32, "weighted", "pair_next")
+        weigh(d_ps[:], 1, weighted[:], weighted[:])
+        weave(h_both[:, CHUNK:], runs)
+        quantize_h(h_both, [(0, 2), (1, 2)])
 
-        h_both = relay_tile([P, 2 * CHUNK, PACK], BF16, "h_3", 4)
-        nc.gpsimd.tensor_tensor(h_both[:, :CHUNK], silu_woven(0, [6, 7], "runs_first")[:], gain_row[:], MULT)
-        d_ps, e_ps = products([(2, 0), (2, 1)], 4, 5)
-        weighted = slot_tile([P, 2, CHUNK], F32, "weighted", "pair")
-        weigh(d_ps[:], 2, slot_tile([P, 2, CHUNK], F32, "d_sb", "codes3")[:], weighted[:])
-        second_half(3)
-        gain_on_scalar(1, silu_in_runs(1, [6, 7], "rows"), h_both[:, CHUNK:], "runs0")
-        quantize_h(h_both, [(0, 3), (1, 3)], slot_tile([P, 2 * CHUNK], U32, "h_codes", "codes3"))
-        y_pair = relay_tile([P, 2, CHUNK], F32, "y_2", 4)
-        for n in range(2):
-            multiply(y_pair[:, n, :], e_ps[:, n, :], weighted[:, n, :])
+        h_both = relay_tile([P, 2 * CHUNK, PACK], BF16, "h_3", 22)
+        nc.gpsimd.tensor_tensor(h_both[:, :CHUNK], act[:], gain_row[:], MULT)
+        act_runs = silu_in_runs(3, relay_tile([P, PACK, CHUNK], F32, "act_13", 14))
+        runs = gain_in_runs(act_runs, relay_tile([P, PACK, CHUNK], BF16, "runs_3", 20))
+        y_pair = relay_tile([P, 2, CHUNK], F32, "y_1", 18)
+        finish_pair(1, e_ps, weighted, y_pair, relay_tile([P, CHUNK], F32, "bounded_1", 16))
+
+        weave(h_both[:, CHUNK:], runs, [0])
+        d_ps, e_ps = products([(2, 0), (2, 1)], 3, 0)
+        weighted = relay_tile([P, 1, CHUNK], F32, "weighted_2", 14)
+        weigh(d_ps[:, :1], 2, weighted[:], weighted[:])
+        weighted_one = weigh_on_vector(d_ps[:, 1:], 2)
+        weave(h_both[:, CHUNK:], runs, [1])
+        quantize_h(h_both, [(0, 3), (1, 3)])
+        y_pair = relay_tile([P, 2, CHUNK], F32, "y_2", 20)
+        for n, factor in enumerate((weighted, weighted_one)):
+            multiply(y_pair[:, n, :], e_ps[:, n, :], factor[:, 0, :])
         for n in range(2):
             place(n, 2 * CHUNK, 3 * CHUNK, y_pair[:, n, :])
 
-        d_ps, e_ps = products([(3, 0), (3, 1)], 6, 7)
-        weighted = slot_tile([P, 2, CHUNK], F32, "weighted", "pair_next")
-        weigh(d_ps[:], 3, weighted[:], weighted[:])
-        d_both, e_both = products([(2, 2), (3, 2)], 0, 3)
-        d_sb = slot_tile([P, 2 * CHUNK], F32, "d_sb", "d_last")
-        weighted_both = slot_tile([P, 2 * CHUNK], F32, "weighted", "pair")
-        nc.scalar.copy(d_sb[:], d_both[:].rearrange("p c e -> p (c e)"))
-        nc.gpsimd.tensor_tensor(weighted_both[:], d_sb[:], wgo_rest[:, CHUNK:], MULT)
+        d_ps, e_ps = bank(1, [P, 2, CHUNK]), bank(2, [P, 2, CHUNK])
+        for i, job in enumerate([(2, 2), (3, 0)]):
+            sums(d_ps[:, i : i + 1, :], [job], w2_of)
+        for i, job in enumerate([(2, 2), (3, 0)]):
+            sums(e_ps[:, i : i + 1, :], [job], w3_of)
+        weighted = slot_tile([P, 2 * CHUNK], F32, "weighted", "pair_next")
+        nc.scalar.copy(weighted[:], d_ps[:].rearrange("p c e -> p (c e)"))
+        nc.gpsimd.tensor_tensor(weighted[:], weighted[:], wgo_rest[:, CHUNK:], MULT)
         y_first = slot_tile([P, CHUNK], F32, "y", "y_single")
-        multiply(y_first[:], e_ps[:, 0, :], weighted[:, 0, :])
-        place(0, 3 * CHUNK, S, y_first[:])
-        y_second = slot_tile([P, CHUNK], F32, "y", "d_last")
-        multiply(y_second[:], e_ps[:, 1, :], weighted[:, 1, :])
         y_both = slot_tile([P, 2 * CHUNK], F32, "y", "y_both")
-        multiply(y_both[:], e_both[:].rearrange("p c e -> p (c e)"), weighted_both[:])
+        multiply(y_first[:], e_ps[:, 1, :], weighted[:, CHUNK:])
+        multiply(y_both[:, :CHUNK], e_ps[:, 0, :], weighted[:, :CHUNK])
+        place(0, 3 * CHUNK, S, y_first[:])
+        d_ps, e_ps = products([(3, 1), (3, 2)], 4, 5)
+        weighted = slot_tile([P, 2, CHUNK], F32, "weighted", "pair")
+        weigh(d_ps[:], 3, weighted[:], weighted[:])
+        y_second = slot_tile([P, CHUNK], F32, "y", "y_second")
+        multiply(y_second[:], e_ps[:, 0, :], weighted[:, 0, :])
+        multiply(y_both[:, CHUNK:], e_ps[:, 1, :], weighted[:, 1, :])
         place(1, 3 * CHUNK, S, y_second[:])
-        place(2, 2 * CHUNK, S, bound(y_both[:]))
+        place(2, 2 * CHUNK, S, bound(y_both[:], slot_tile([P, 2 * CHUNK], F32, "bounded", "bounded_y")))
 
-        half = S // 2
-        for n, lo, tag in ((0, 0, "piece02"), (0, half, "piece11"), (1, 0, "tab0"), (1, half, "tab1")):
-            cols = slice(lo, lo + half)
-            bounded = slot_tile([P, half], F32, "bounded", tag)
-            nc.scalar.activation(bounded[:], pages[n][:, cols], ACT.Tanh)
-            nc.gpsimd.tensor_tensor(x0_sb[:, n, cols], x0_sb[:, n, cols], bounded[:], ADD)
-            nc.sync.dma_start(out=out[P * n : P * (n + 1), cols], in_=x0_sb[:, n, cols])
-        sums = slot_tile([P, S], F32, "sums", "tab1")
+        for n, lo, hi, tag in (
+            (0, 0, CHUNK, "rows1"),
+            (0, CHUNK, S, "rows2"),
+            (1, 0, POOL_END - CHUNK, "tab1b"),
+            (1, POOL_END - CHUNK, POOL_END, "tab1"),
+        ):
+            bounded = slot_tile([P, hi - lo], F32, "bounded", tag)
+            nc.scalar.activation(bounded[:], pages[n][:, lo:hi], ACT.Tanh)
+            nc.gpsimd.tensor_tensor(x0_sb[:, n, lo:hi], x0_sb[:, n, lo:hi], bounded[:], ADD)
+            nc.sync.dma_start(out=out[P * n : P * (n + 1), lo:hi], in_=x0_sb[:, n, lo:hi])
+        totals = slot_tile([P, 2, S], F32, "totals", "tab1")
+        bounded = slot_tile([P, S - POOL_END], F32, "bounded", "rows0")
+        nc.scalar.activation(bounded[:], pages[1][:, POOL_END:], ACT.Tanh)
+        nc.vector.tensor_tensor(totals[:, 0, POOL_END:], x0_sb[:, 1, POOL_END:], bounded[:], ADD)
+        nc.sync.dma_start(out=out[P : 2 * P, POOL_END:], in_=totals[:, 0, POOL_END:])
         for lo in range(0, S, S // 4):
             cols = slice(lo, lo + S // 4)
-            nc.vector.tensor_tensor(sums[:, cols], x0_sb[:, 2, cols], pages[2][:, cols], ADD)
-            nc.sync.dma_start(out=out[2 * P :, cols], in_=sums[:, cols])
+            nc.vector.tensor_tensor(totals[:, 1, cols], x0_sb[:, 2, cols], pages[2][:, cols], ADD)
+            nc.sync.dma_start(out=out[2 * P :, cols], in_=totals[:, 1, cols])

@@ -152,13 +152,10 @@ def tile_list_junction_desk_kernel(
                 nc.scalar.activation(runs[:, t, :], act[:, t, :], ACT.Copy, scale=gain_sb[:, 1, t : t + 1])
             return runs
 
-        def weave(h_bf, runs, units=(0, 1)):
-            for i in units:
-                cols = slice(UNIT * i, UNIT * (i + 1))
-                nc.scalar.copy(
-                    h_bf[:, cols, :].rearrange("p (x i) t -> p x t i", i=4),
-                    runs[:, :, cols].rearrange("p t (x i) -> p x t i", i=4),
-                )
+        def weave(h_bf, runs):
+            nc.scalar.copy(
+                h_bf.rearrange("p (x i) t -> p x t i", i=4), runs.rearrange("p t (x i) -> p x t i", i=4)
+            )
 
         def quantize_h(h_tile, parts):
             width = CHUNK * len(parts)
@@ -190,7 +187,7 @@ def tile_list_junction_desk_kernel(
             for b in range(R_PASSES):
                 cast_w1(b, a, on_vector=(b == 1))
                 quantize_w1(b, a)
-            cuts = [0, S] if a < K_PASSES - 1 else [0, CHUNK, 2 * CHUNK, S]
+            cuts = [0, S] if a < K_PASSES - 1 else [0, CHUNK, S]
             for lo, hi in zip(cuts, cuts[1:]):
                 entries = idx[:, lo // LIST_ROWS : hi // LIST_ROWS]
                 nc.vector.tensor_copy(v_codes[a][:, lo:hi], tab[a][:].bitcast(U32).indirect(entries))
@@ -308,24 +305,22 @@ def tile_list_junction_desk_kernel(
         y_first = slot_tile([P, CHUNK], F32, "y", "y_single")
         weighted_one = weigh_on_vector(d_ps, 0)
         w3_rest = relay_tile([P, 2 * P, PACK], BF16, "w3_second", 32)
-        for n in (1, 2):
-            cast_w3(w3_rest[:, P * (n - 1) : P * n], 0, [n], nc.scalar.copy)
+        cast_w3(w3_rest[:], 0, [1, 2], nc.scalar.copy)
         quantize_w3(w3_rest, [(0, 1), (0, 2)])
         w3_rest = relay_tile([P, 2 * P, PACK], BF16, "w3_rest", 27)
-        for n in (1, 2):
-            cast_w3(w3_rest[:, P * (n - 1) : P * n], 1, [n])
+        cast_w3(w3_rest[:], 1, [1, 2])
         quantize_w3(w3_rest, [(1, 1), (1, 2)])
         multiply(y_first[:], e_ps[:, 0, :], weighted_one[:, 0, :])
         d_ps, e_ps = products([(0, 1), (0, 2)], 2, 3)
         weighted = slot_tile([P, 2, CHUNK], F32, "weighted", "pair")
-        for i in range(2):
-            nc.vector.tensor_tensor(weighted[:, i, :], d_ps[:, i, :], wgo_sb[0], MULT)
+        factors = wgo_sb[0].rearrange("p (o e) -> p o e", o=1).to_broadcast([P, 2, CHUNK])
+        nc.vector.tensor_tensor(weighted[:], d_ps[:], factors, MULT)
         place(0, 0, CHUNK, y_first[:])
 
         act_runs = silu_in_runs(1, slot_tile([P, PACK, CHUNK], F32, "act", "rows0"))
         h_both = relay_tile([P, 2 * CHUNK, PACK], BF16, "h_1", 28.5)
         nc.gpsimd.tensor_tensor(h_both[:, :CHUNK], act_next[:], gain_row[:], MULT)
-        weave(h_both[:, CHUNK:], gain_in_runs(act_runs, relay_tile([P, PACK, CHUNK], BF16, "runs_1", 1)))
+        weave(h_both[:, CHUNK:], gain_in_runs(act_runs, relay_tile([P, PACK, CHUNK], BF16, "runs_1", 1))[:])
         quantize_h(h_both, [(0, 1), (1, 1)])
 
         h_both = relay_tile([P, 2 * CHUNK, PACK], BF16, "h_2", 25)
@@ -346,36 +341,36 @@ def tile_list_junction_desk_kernel(
         act = silu_woven(0, [6, 7], slot_tile([P, CHUNK, PACK], F32, "act", "rows0"))
         weighted = slot_tile([P, 2, CHUNK], F32, "weighted", "pair_next")
         weigh(d_ps[:], 1, weighted[:], weighted[:])
-        weave(h_both[:, CHUNK:], runs)
+        weave(h_both[:, CHUNK:], runs[:])
         quantize_h(h_both, [(0, 2), (1, 2)])
 
         h_both = relay_tile([P, 2 * CHUNK, PACK], BF16, "h_3", 22)
         nc.gpsimd.tensor_tensor(h_both[:, :CHUNK], act[:], gain_row[:], MULT)
         act_runs = silu_in_runs(3, relay_tile([P, PACK, CHUNK], F32, "act_13", 14))
-        runs = gain_in_runs(act_runs, relay_tile([P, PACK, CHUNK], BF16, "runs_3", 20))
+        runs = gain_in_runs(act_runs, relay_tile([P, PACK, CHUNK], BF16, "runs_3", 7))
         y_pair = relay_tile([P, 2, CHUNK], F32, "y_1", 18)
         finish_pair(1, e_ps, weighted, y_pair, relay_tile([P, CHUNK], F32, "bounded_1", 16))
 
-        weave(h_both[:, CHUNK:], runs, [0])
+        weave(h_both[:, CHUNK : CHUNK + UNIT], runs[:, :, :UNIT])
         d_ps, e_ps = products([(2, 0), (2, 1)], 3, 0)
         weighted = relay_tile([P, 1, CHUNK], F32, "weighted_2", 14)
         weigh(d_ps[:, :1], 2, weighted[:], weighted[:])
         weighted_one = weigh_on_vector(d_ps[:, 1:], 2)
-        weave(h_both[:, CHUNK:], runs, [1])
+        weave(h_both[:, CHUNK + UNIT :], runs[:, :, UNIT:])
         quantize_h(h_both, [(0, 3), (1, 3)])
-        y_pair = relay_tile([P, 2, CHUNK], F32, "y_2", 20)
+        y_pair = relay_tile([P, 2, CHUNK], F32, "y_2", 6)
         for n, factor in enumerate((weighted, weighted_one)):
             multiply(y_pair[:, n, :], e_ps[:, n, :], factor[:, 0, :])
         for n in range(2):
             place(n, 2 * CHUNK, 3 * CHUNK, y_pair[:, n, :])
 
         d_ps, e_ps = bank(1, [P, 2, CHUNK]), bank(2, [P, 2, CHUNK])
+        weighted = relay_tile([P, 2 * CHUNK], F32, "weighted_last", 8)
         for i, job in enumerate([(2, 2), (3, 0)]):
             sums(d_ps[:, i : i + 1, :], [job], w2_of)
+            nc.scalar.copy(weighted[:, CHUNK * i : CHUNK * (i + 1)], d_ps[:, i, :])
         for i, job in enumerate([(2, 2), (3, 0)]):
             sums(e_ps[:, i : i + 1, :], [job], w3_of)
-        weighted = slot_tile([P, 2 * CHUNK], F32, "weighted", "pair_next")
-        nc.scalar.copy(weighted[:], d_ps[:].rearrange("p c e -> p (c e)"))
         nc.gpsimd.tensor_tensor(weighted[:], weighted[:], wgo_rest[:, CHUNK:], MULT)
         y_first = slot_tile([P, CHUNK], F32, "y", "y_single")
         y_both = slot_tile([P, 2 * CHUNK], F32, "y", "y_both")

from contextlib import ExitStack

import concourse.mybir as mybir

K, H, N, T, S = 1536, 1024, 384, 4096, 1024
FLOPS = 2 * K * H * S + 4 * H * N * S

F32 = mybir.dt.float32
BF16 = mybir.dt.bfloat16
I32 = mybir.dt.int32
U32 = mybir.dt.uint32
U16 = mybir.dt.uint16
U8 = mybir.dt.uint8
FP8X4 = mybir.dt.float8_e4m3fn_x4
FP4X4 = mybir.dt.float4_e2m1fn_x4
ACT = mybir.ActivationFunctionType
MULT = mybir.AluOpType.mult
ADD = mybir.AluOpType.add

P = 128
PACK = 4
PASS = P * PACK
QUADS = 4
LIST_ROWS = 16
K_PASSES = K // PASS
R_PASSES = H // PASS
N_TILES = N // P
UNIT = 128
CHUNK = 2 * UNIT
CHUNKS = S // CHUNK
POOL_END = 640


def tile_list_junction_desk_kernel(
    tc, tab_words, tab_scales, offs, offs2, w1, gain, w2_words, w2_scales, w3, wgo, x0, out
):
    nc = tc.nc
    with ExitStack() as ctx:
        keep = ctx.enter_context(tc.tile_pool(name="keep", bufs=1))
        ring = ctx.enter_context(tc.tile_pool(name="ring", bufs=1))
        relay = ctx.enter_context(tc.tile_pool(name="relay", bufs=1))
        psum = ctx.enter_context(tc.psum_pool(name="psum", bufs=1))

        def slot_tile(shape, dtype, name, tag):
            return ring.tile(shape, dtype, name=name, tag=tag, bufs=1, align_bytes=64)

        def relay_tile(shape, dtype, name, kib):
            return relay.tile(shape, dtype, name=name, align_bytes=64, offset=int(1024 * kib))

        def bank(number, shape):
            return psum.tile(shape, F32, name=f"bank{number}")

        idx = keep.tile([P, S // LIST_ROWS], U16, name="idx")
        idx2 = keep.tile([P, S // LIST_ROWS], U16, name="idx2")
        tab = [slot_tile([P, T], I32, f"tab{a}", f"tab{a}") for a in range(K_PASSES)]
        tab_sc = keep.tile([P, T], U8, name="tab_sc", align_bytes=64)
        v_codes = [keep.tile([P, S], U32, name=f"v_codes{a}", align_bytes=64) for a in range(K_PASSES)]
        v_sc = keep.tile([P, S], U8, name="v_sc", align_bytes=64)
        gain_sb = keep.tile([P, R_PASSES, PACK], F32, name="gain_sb")
        w2_codes = keep.tile([P, R_PASSES, 2 * N], U8, name="w2_codes", align_bytes=64)
        w2_sc = keep.tile([P, R_PASSES, N], U8, name="w2_sc", align_bytes=64)

        nc.vector.memset(tab_sc[:].bitcast(I32), 0)
        nc.vector.memset(w2_sc[:].rearrange("p b n -> p (b n)").bitcast(I32), 0)
        for q in range(QUADS):
            nc.gpsimd.dma_start(
                out=tab_sc[32 * q : 32 * q + 4 * K_PASSES, :].bitcast(I32),
                in_=tab_scales[:, 4 * q : 4 * q + 4, :].bitcast(I32),
            )
        for q in range(QUADS):
            nc.gpsimd.dma_start(
                out=w2_sc[32 * q : 32 * q + 4, :, :].bitcast(I32),
                in_=w2_scales[:, 4 * q : 4 * q + 4, :].rearrange("b r n -> r b n").bitcast(I32),
            )

        w1_raw, w1_grouped, w1_codes, w1_sc = {}, {}, {}, {}

        def load_tab(a):
            nc.sync.dma_start(out=tab[a][:], in_=tab_words[a].rearrange("p t i -> p (t i)").bitcast(I32))

        def load_w1_rows(a):
            raw = slot_tile([P, PACK, H], F32, "w1_rows", f"rows{a}")
            nc.sync.dma_start(out=raw[:], in_=w1[PASS * a : PASS * (a + 1), :].rearrange("(p j) r -> p j r", j=PACK))
            for b in range(R_PASSES):
                w1_raw[(b, a)] = raw[:, :, PASS * b : PASS * (b + 1)]

        def cast_w1(b, a, on_vector):
            grouped = ring.tile([P, PASS * PACK], BF16, name="w1_grouped", bufs=2, align_bytes=64)
            dst = grouped[:].rearrange("p (t m j) -> p m j t", t=PACK, j=PACK)
            src = w1_raw[(b, a)].rearrange("p j (m t) -> p m j t", t=PACK)
            if on_vector:
                nc.vector.tensor_copy(dst.rearrange("p m j t -> p m t j"), src.rearrange("p m j t -> p m t j"))
            else:
                nc.scalar.copy(dst, src)
            w1_grouped[(b, a)] = grouped

        def quantize_w1(b, a):
            codes = keep.tile([P, PASS], U32, name=f"w1_codes{b}{a}", align_bytes=64)
            sc = keep.tile([P, PASS], U8, name=f"w1_sc{b}{a}", align_bytes=64)
            nc.vector.quantize_mx(out=codes[:].bitcast(FP8X4), scales=sc[:], in_=w1_grouped[(b, a)][:])
            w1_codes[(b, a)], w1_sc[(b, a)] = codes, sc

        banks = {}

        def first_product(b, a, u, number):
            if a == 0:
                banks[(b, u)] = bank(number, [P, PACK, UNIT])
            cols = slice(UNIT * u, UNIT * (u + 1))
            for t in range(PACK):
                m = slice(P * t, P * (t + 1))
                nc.tensor.matmul_mx(
                    out=banks[(b, u)][:, t, :],
                    lhsT=w1_codes[(b, a)][:, m].bitcast(FP8X4),
                    lhsT_scale=w1_sc[(b, a)][:, m],
                    rhs=v_codes[a][:, cols].bitcast(FP8X4),
                    rhs_scale=v_sc[4 * a :, cols],
                    start=(a == 0 and t == 0),
                    stop=(a == K_PASSES - 1 and t == PACK - 1),
                )

        def chunk_pass(c, a):
            for b in range(R_PASSES):
                for i in range(2):
                    first_product(b, a, 2 * c + i, (4 if c else 0) + 2 * b + i)

        def whole_chunk(c):
            for b in range(R_PASSES):
                for i in range(2):
                    for a in range(K_PASSES):
                        first_product(b, a, 2 * c + i, 4 + 2 * b + i)

        h_codes, h_sc = {}, {}

        def silu_woven(b, units, act):
            for i, u in enumerate(units):
                sums = banks[(b, u)][:].rearrange("p t e -> p e t")
                nc.scalar.activation(act[:, UNIT * i : UNIT * (i + 1), :], sums, ACT.Silu)
            return act

        def silu_in_runs(c, act):
            for i in range(CHUNK // UNIT):
                nc.scalar.activation(act[:, :, UNIT * i : UNIT * (i + 1)], banks[(1, 2 * c + i)][:], ACT.Silu)
            return act

        def gain_on_vector(b, act, h_bf):
            factors = gain_sb[:, b : b + 1, :].to_broadcast([P, UNIT, PACK])
            for lo in range(0, CHUNK, UNIT):
                nc.vector.tensor_tensor(h_bf[:, lo : lo + UNIT], act[:, lo : lo + UNIT], factors, MULT)

        def gain_in_runs(act, runs):
            for t in range(PACK):
                nc.scalar.activation(runs[:, t, :], act[:, t, :], ACT.Copy, scale=gain_sb[:, 1, t : t + 1])
            return runs

        def weave(h_bf, runs):
            nc.scalar.copy(
                h_bf.rearrange("p (x i) t -> p x t i", i=4), runs.rearrange("p t (x i) -> p x t i", i=4)
            )

        def quantize_h(h_tile, parts):
            width = CHUNK * len(parts)
            name = f"{parts[0][0]}{parts[0][1]}"
            codes = keep.tile([P, width], U32, name=f"h_codes{name}", align_bytes=64)
            sc = keep.tile([P, width], U8, name=f"h_sc{name}", align_bytes=64)
            nc.vector.quantize_mx(out=codes[:].bitcast(FP8X4), scales=sc[:], in_=flat(h_tile))
            for i, part in enumerate(parts):
                cols = slice(CHUNK * i, CHUNK * (i + 1))
                h_codes[part], h_sc[part] = codes[:, cols], sc[:, cols]

        def flat(h_tile):
            return h_tile[:].rearrange("p e t -> p (e t)")

        load_tab(0)
        nc.sync.dma_start(idx[:], offs)
        nc.sync.dma_start(out=gain_sb[:], in_=gain.rearrange("(b p t) -> p b t", b=R_PASSES, t=PACK))
        load_w1_rows(0)
        load_tab(1)
        load_w1_rows(1)
        load_w1_rows(2)
        load_tab(2)

        gain_row = keep.tile([P, CHUNK, PACK], F32, name="gain_row")
        nc.vector.tensor_copy(gain_row[:], gain_sb[:, 0:1, :].to_broadcast([P, CHUNK, PACK]))

        nc.vector.tensor_copy(v_sc[:], tab_sc[:].indirect(idx[:]))
        for a in range(K_PASSES):
            for b in range(R_PASSES):
                cast_w1(b, a, on_vector=(b == 1))
                quantize_w1(b, a)
            cuts = [0, S] if a < K_PASSES - 1 else [0, CHUNK, S]
            for lo, hi in zip(cuts, cuts[1:]):
                entries = idx[:, lo // LIST_ROWS : hi // LIST_ROWS]
                nc.vector.tensor_copy(v_codes[a][:, lo:hi], tab[a][:].bitcast(U32).indirect(entries))
            for c in range(2):
                chunk_pass(c, a)

        w3_raw = keep.tile([P, R_PASSES, PACK, N], F32, name="w3_raw")
        for b in range(R_PASSES):
            rows3 = w3[PASS * b : PASS * (b + 1), :]
            nc.sync.dma_start(out=w3_raw[:, b], in_=rows3.rearrange("(p j) n -> p j n", j=PACK))
        nc.sync.dma_start(out=w2_codes[:].bitcast(I32), in_=w2_words.rearrange("b p c -> p b c").bitcast(I32))
        nc.sync.dma_start(idx2[:], offs2)
        wgo_first = keep.tile([P, CHUNK], F32, name="wgo0")
        nc.sync.dma_start(out=wgo_first[:], in_=wgo[:, :CHUNK])
        wgo_rest = slot_tile([P, S - CHUNK], F32, "wgo1", "tab0")
        nc.sync.dma_start(out=wgo_rest[:], in_=wgo[:, CHUNK:])
        wgo_sb = [wgo_first[:, :]] + [wgo_rest[:, CHUNK * c : CHUNK * (c + 1)] for c in range(CHUNKS - 1)]
        x0_sb = slot_tile([P, N_TILES, S], F32, "x0_sb", f"tab{K_PASSES - 1}")
        for n in range(N_TILES):
            nc.sync.dma_start(out=x0_sb[:, n, :], in_=x0[P * n : P * (n + 1), :])

        w3_codes, w3_sc = {}, {}

        def cast_w3(dst, b, tiles_n, cast=nc.vector.tensor_copy):
            cols = slice(P * tiles_n[0], P * (tiles_n[-1] + 1))
            cast(
                dst.rearrange("p (x i) j -> p x j i", i=4),
                w3_raw[:, b, :, cols].rearrange("p j (x i) -> p x j i", i=4),
            )

        def quantize_w3(grouped3, parts):
            width = P * len(parts)
            name = f"{parts[0][0]}{parts[0][1]}"
            codes = keep.tile([P, width], U32, name=f"w3_codes{name}", align_bytes=64)
            sc = keep.tile([P, width], U8, name=f"w3_sc{name}", align_bytes=64)
            nc.vector.quantize_mx(out=codes[:].bitcast(FP8X4), scales=sc[:], in_=flat(grouped3))
            for k, part in enumerate(parts):
                cols = slice(P * k, P * (k + 1))
                w3_codes[part], w3_sc[part] = codes[:, cols], sc[:, cols]

        pages = [keep.tile([P, S], F32, name=f"page{n}") for n in range(N_TILES)]

        def sums(dst, jobs, weights):
            for b in range(R_PASSES):
                for i, (c, n) in enumerate(jobs):
                    codes, scales = weights(b, n)
                    nc.tensor.matmul_mx(
                        out=dst[:, i, :],
                        lhsT=codes,
                        lhsT_scale=scales,
                        rhs=h_codes[(b, c)].bitcast(FP8X4),
                        rhs_scale=h_sc[(b, c)],
                        start=(b == 0 and i == 0),
                        stop=(b == R_PASSES - 1 and i == len(jobs) - 1),
                    )

        def w2_of(b, n):
            return w2_codes[:, b, 2 * P * n : 2 * P * (n + 1)].bitcast(FP4X4), w2_sc[:, b, P * n : P * (n + 1)]

        def w3_of(b, n):
            return w3_codes[(b, n)].bitcast(FP8X4), w3_sc[(b, n)]

        def products(jobs, d_bank, e_bank):
            d_ps = bank(d_bank, [P, len(jobs), CHUNK])
            e_ps = bank(e_bank, [P, len(jobs), CHUNK])
            sums(d_ps, jobs, w2_of)
            sums(e_ps, jobs, w3_of)
            return d_ps, e_ps

        def weigh_on_vector(d_ps, c):
            weighted = slot_tile([P, 1, CHUNK], F32, "weighted", "single")
            nc.vector.tensor_tensor(weighted[:, 0, :], d_ps[:, 0, :], wgo_sb[c], MULT)
            return weighted

        def weigh(d_ps, c, d_sb, weighted):
            count = weighted.shape[1]
            nc.scalar.copy(d_sb, d_ps)
            factors = wgo_sb[c].rearrange("p (o e) -> p o e", o=1).to_broadcast([P, count, CHUNK])
            nc.gpsimd.tensor_tensor(weighted, d_sb, factors, MULT)

        def multiply(y, e_ps, weighted):
            nc.vector.tensor_tensor(y, e_ps, weighted, MULT)

        def place(n, lo, hi, y):
            nc.vector.tensor_copy(pages[n][:].indirect(idx2[:, lo // LIST_ROWS : hi // LIST_ROWS]), y)

        def bound(y, bounded):
            nc.scalar.activation(bounded[:], y, ACT.Tanh)
            return bounded[:]

        def finish_pair(c, e_ps, weighted, y_pair, bounded):
            for i in range(2):
                multiply(y_pair[:, i, :], e_ps[:, i, :], weighted[:, i, :])
            place(1, CHUNK * c, CHUNK * (c + 1), y_pair[:, 0, :])
            place(2, CHUNK * c, CHUNK * (c + 1), bound(y_pair[:, 1, :], bounded))

        def single_products(c, number):
            both = bank(number, [P, 2, CHUNK])
            sums(both[:, 0:1, :], [(c, 0)], w2_of)
            sums(both[:, 1:2, :], [(c, 0)], w3_of)
            return both[:, 0:1, :], both[:, 1:2, :]

        h_first = slot_tile([P, 2 * CHUNK, PACK], BF16, "h_bf", "h_first")
        act_tiles = [relay_tile([P, CHUNK, PACK], F32, "act_0", 32), relay_tile([P, CHUNK, PACK], F32, "act_10", 24)]
        for b, act in enumerate(act_tiles):
            silu_woven(b, [0, 1], act)
            gain_on_vector(b, act, h_first[:, CHUNK * b : CHUNK * (b + 1)])
        w3_first = slot_tile([P, R_PASSES * P, PACK], BF16, "w3_grouped", "w3_first")
        for b in range(R_PASSES):
            cast_w3(w3_first[:, P * b : P * (b + 1)], b, [0])
        quantize_h(h_first, [(0, 0), (1, 0)])
        quantize_w3(w3_first, [(0, 0), (1, 0)])
        act_next = silu_woven(0, [2, 3], relay_tile([P, CHUNK, PACK], F32, "act_1", 10))
        d_ps, e_ps = products([(0, 0)], 0, 1)
        y_first = slot_tile([P, CHUNK], F32, "y", "y_single")
        weighted_one = weigh_on_vector(d_ps, 0)
        w3_rest = relay_tile([P, 2 * P, PACK], BF16, "w3_second", 32)
        cast_w3(w3_rest[:], 0, [1, 2], nc.scalar.copy)
        quantize_w3(w3_rest, [(0, 1), (0, 2)])
        w3_rest = relay_tile([P, 2 * P, PACK], BF16, "w3_rest", 27)
        cast_w3(w3_rest[:], 1, [1, 2])
        quantize_w3(w3_rest, [(1, 1), (1, 2)])
        multiply(y_first[:], e_ps[:, 0, :], weighted_one[:, 0, :])
        d_ps, e_ps = products([(0, 1), (0, 2)], 2, 3)
        weighted = slot_tile([P, 2, CHUNK], F32, "weighted", "pair")
        factors = wgo_sb[0].rearrange("p (o e) -> p o e", o=1).to_broadcast([P, 2, CHUNK])
        nc.vector.tensor_tensor(weighted[:], d_ps[:], factors, MULT)
        place(0, 0, CHUNK, y_first[:])

        act_runs = silu_in_runs(1, slot_tile([P, PACK, CHUNK], F32, "act", "rows0"))
        h_both = relay_tile([P, 2 * CHUNK, PACK], BF16, "h_1", 28.5)
        nc.gpsimd.tensor_tensor(h_both[:, :CHUNK], act_next[:], gain_row[:], MULT)
        weave(h_both[:, CHUNK:], gain_in_runs(act_runs, relay_tile([P, PACK, CHUNK], BF16, "runs_1", 1))[:])
        quantize_h(h_both, [(0, 1), (1, 1)])

        h_both = relay_tile([P, 2 * CHUNK, PACK], BF16, "h_2", 25)
        whole_chunk(2)
        act = silu_woven(0, [4, 5], relay_tile([P, CHUNK, PACK], F32, "act_2", 2))
        nc.gpsimd.tensor_tensor(h_both[:, :CHUNK], act[:], gain_row[:], MULT)
        act_runs = silu_in_runs(2, slot_tile([P, PACK, CHUNK], F32, "act", "rows0"))
        runs = gain_in_runs(act_runs, relay_tile([P, PACK, CHUNK], BF16, "runs_2", 18))
        y_pair = relay_tile([P, 2, CHUNK], F32, "y_0", 0)
        finish_pair(0, e_ps, weighted, y_pair, slot_tile([P, CHUNK], F32, "bounded", "bounded_y"))
        d_one, e_one = single_products(1, 0)
        d_ps, e_ps = products([(1, 1), (1, 2)], 1, 2)
        weighted_one = weigh_on_vector(d_one, 1)
        y_first = slot_tile([P, CHUNK], F32, "y", "y_single")
        multiply(y_first[:], e_one[:, 0, :], weighted_one[:, 0, :])
        place(0, CHUNK, 2 * CHUNK, y_first[:])
        whole_chunk(3)
        act = silu_woven(0, [6, 7], slot_tile([P, CHUNK, PACK], F32, "act", "rows0"))
        weighted = slot_tile([P, 2, CHUNK], F32, "weighted", "pair_next")
        weigh(d_ps[:], 1, weighted[:], weighted[:])
        weave(h_both[:, CHUNK:], runs[:])
        quantize_h(h_both, [(0, 2), (1, 2)])

        h_both = relay_tile([P, 2 * CHUNK, PACK], BF16, "h_3", 22)
        nc.gpsimd.tensor_tensor(h_both[:, :CHUNK], act[:], gain_row[:], MULT)
        act_runs = silu_in_runs(3, relay_tile([P, PACK, CHUNK], F32, "act_13", 14))
        runs = gain_in_runs(act_runs, relay_tile([P, PACK, CHUNK], BF16, "runs_3", 7))
        y_pair = relay_tile([P, 2, CHUNK], F32, "y_1", 18)
        finish_pair(1, e_ps, weighted, y_pair, relay_tile([P, CHUNK], F32, "bounded_1", 16))

        weave(h_both[:, CHUNK : CHUNK + UNIT], runs[:, :, :UNIT])
        d_ps, e_ps = products([(2, 0), (2, 1)], 3, 0)
        weighted = relay_tile([P, 1, CHUNK], F32, "weighted_2", 14)
        weigh(d_ps[:, :1], 2, weighted[:], weighted[:])
        weighted_one = weigh_on_vector(d_ps[:, 1:], 2)
        weave(h_both[:, CHUNK + UNIT :], runs[:, :, UNIT:])
        quantize_h(h_both, [(0, 3), (1, 3)])
        y_pair = relay_tile([P, 2, CHUNK], F32, "y_2", 6)
        for n, factor in enumerate((weighted, weighted_one)):
            multiply(y_pair[:, n, :], e_ps[:, n, :], factor[:, 0, :])
        for n in range(2):
            place(n, 2 * CHUNK, 3 * CHUNK, y_pair[:, n, :])

        d_ps, e_ps = bank(1, [P, 2, CHUNK]), bank(2, [P, 2, CHUNK])
        weighted = relay_tile([P, 2 * CHUNK], F32, "weighted_last", 8)
        for i, job in enumerate([(2, 2), (3, 0)]):
            sums(d_ps[:, i : i + 1, :], [job], w2_of)
            nc.scalar.copy(weighted[:, CHUNK * i : CHUNK * (i + 1)], d_ps[:, i, :])
        for i, job in enumerate([(2, 2), (3, 0)]):
            sums(e_ps[:, i : i + 1, :], [job], w3_of)
        nc.gpsimd.tensor_tensor(weighted[:], weighted[:], wgo_rest[:, CHUNK:], MULT)
        y_first = slot_tile([P, CHUNK], F32, "y", "y_single")
        y_both = slot_tile([P, 2 * CHUNK], F32, "y", "y_both")
        multiply(y_first[:], e_ps[:, 1, :], weighted[:, CHUNK:])
        multiply(y_both[:, :CHUNK], e_ps[:, 0, :], weighted[:, :CHUNK])
        place(0, 3 * CHUNK, S, y_first[:])
        d_ps, e_ps = products([(3, 1), (3, 2)], 4, 5)
        weighted = slot_tile([P, 2, CHUNK], F32, "weighted", "pair")
        weigh(d_ps[:], 3, weighted[:], weighted[:])
        y_second = slot_tile([P, CHUNK], F32, "y", "y_second")
        multiply(y_second[:], e_ps[:, 0, :], weighted[:, 0, :])
        multiply(y_both[:, CHUNK:], e_ps[:, 1, :], weighted[:, 1, :])
        place(1, 3 * CHUNK, S, y_second[:])
        place(2, 2 * CHUNK, S, bound(y_both[:], slot_tile([P, 2 * CHUNK], F32, "bounded", "bounded_y")))

        for n, lo, hi, tag in (
            (0, 0, CHUNK, "rows1"),
            (0, CHUNK, S, "rows2"),
            (1, 0, POOL_END - CHUNK, "tab1b"),
            (1, POOL_END - CHUNK, POOL_END, "tab1"),
        ):
            bounded = slot_tile([P, hi - lo], F32, "bounded", tag)
            nc.scalar.activation(bounded[:], pages[n][:, lo:hi], ACT.Tanh)
            nc.gpsimd.tensor_tensor(x0_sb[:, n, lo:hi], x0_sb[:, n, lo:hi], bounded[:], ADD)
            nc.sync.dma_start(out=out[P * n : P * (n + 1), lo:hi], in_=x0_sb[:, n, lo:hi])
        totals = slot_tile([P, 2, S], F32, "totals", "tab1")
        bounded = slot_tile([P, S - POOL_END], F32, "bounded", "rows0")
        nc.scalar.activation(bounded[:], pages[1][:, POOL_END:], ACT.Tanh)
        nc.vector.tensor_tensor(totals[:, 0, POOL_END:], x0_sb[:, 1, POOL_END:], bounded[:], ADD)
        nc.sync.dma_start(out=out[P : 2 * P, POOL_END:], in_=totals[:, 0, POOL_END:])
        for lo in range(0, S, S // 4):
            cols = slice(lo, lo + S // 4)
            nc.vector.tensor_tensor(totals[:, 1, cols], x0_sb[:, 2, cols], pages[2][:, cols], ADD)
            nc.sync.dma_start(out=out[2 * P :, cols], in_=totals[:, 1, cols])
